import numpy as np, ml_dtypes
CORES = [48,51,52,55]
N = 4
BF = ml_dtypes.bfloat16
def gentries(a):
    return np.ascontiguousarray(a.reshape(8, 16, -1).transpose(0, 2, 1)).reshape(8, -1)
def gtable(e):
    e = np.asarray(e); return np.ascontiguousarray(e.reshape(8, -1, 16).transpose(0, 2, 1)).reshape(128, -1).astype(np.int32)
R0, I0, B0, F, CAP, RO = 1024, 3072, 4096, 1024, 272, 3
def weigh(b):
    return np.add.reduce(b * (2 * np.arange(16) + 1)[:, None], axis=-2)
def parts(rng):
    return (rng.integers(0, I0, (N, 8, 16, R0)), rng.integers(0, B0, (N, 8, 16, I0)), rng.integers(0, 256, (N, 8, 16, B0)), rng.integers(0, R0, (N, 8, F)), rng.integers(0, 256, (N, 8, F)))
def pack(rc, ic, b, cur, x):
    return {"rtab": np.ascontiguousarray(rc.reshape(N, 128, R0)).astype(np.int32), "itab": np.ascontiguousarray(ic.reshape(N, 128, I0)).astype(np.int32),
            "btab": np.ascontiguousarray(b.reshape(N, 128, B0)).astype(np.float32).astype(BF), "rn0": np.stack([gtable(a) for a in cur]), "x0": np.ascontiguousarray(x).astype(np.int32)}
def heavy(rng, w):
    b = rng.integers(0, 16, w.shape[:-1] + (16,) + w.shape[-1:]); b = np.where((weigh(b) > w)[..., None, :], 0, b); rest = w - weigh(b)
    for i in range(15, -1, -1):
        a = np.minimum(255 - b[..., i, :], rest // (2 * i + 1)); b[..., i, :] += a; rest = rest - a * (2 * i + 1)
    return b
def setup_inputs(rng):
    return pack(*parts(rng))
def setup_inputs_room(rng):
    rc, ic, b, cur, x = parts(rng)
    w = weigh(b) - b[:, :, 0]; b[:, :, 0] = b[:, :, 0] // N * N + ((np.arange(B0) - w) & (N - 1))
    ic = ic // N * N + (np.arange(16) & (N - 1))[:, None]
    for a in range(N):
        for g in range(8):
            n = int(rng.choice(np.array([0, 1, CAP - 1, CAP, CAP + 1, 2 * CAP, F]))); m = int(rng.integers(0, N))
            if a == 0: m = 1; n = (CAP, CAP + 1, F, CAP - 1, 1, 0, CAP, 2 * CAP)[g]
            e = rng.permutation(np.concatenate([np.full(n, m), (m + rng.integers(1, N, F - n)) & (N - 1)]))
            d2 = ((e - np.arange(F)) & (N - 1)) + N * rng.integers(0, 16 // N, F)
            x[a, g] = (x[a, g] & 15) + 16 * d2
    return pack(rc, ic, b, cur, x)
def setup_inputs_full(rng):
    rc, ic, b, cur, x = parts(rng); m = int(rng.integers(0, N)); P = 1 << (B0 - 1).bit_length(); f = np.arange(F); k = np.arange(N); n = CAP // N
    for g in range(8):
        col = np.argsort(rng.random((N, B0 // N)), axis=1)[:, :CAP] * N + k[:, None]
        for a in range(N):
            late = np.argsort(rng.random((N, F // 2 // N)), axis=1)[:, :n] * N + k[:, None] + F // 2
            e = (m + rng.integers(1, N, F)) & (N - 1); w = ((e - f) & (N - 1)) + N * rng.integers(0, 65280 // N, F)
            c = col[(m - k) & (N - 1), a * n:(a + 1) * n]; w[late] = c + P * rng.integers(0, (65280 - c) // P + 1)
            q = rng.permutation(16 * R0)[:F]; inn = rng.permutation(I0)[:F]; blk = rng.permutation(B0)[:F]; d2 = rng.integers(0, 16, F)
            rc[a, g, q // R0, q % R0] = inn; ic[a, g, d2, inn] = blk; b[a, g][:, blk] = heavy(rng, w)
            cur[a, g] = q % R0; x[a, g] = q // R0 + 16 * d2
    return pack(rc, ic, b, cur, x)
def setup_inputs_deep(rng):
    rc, ic, b, cur, x = parts(rng)
    e = np.array([7, 6, 5, 4, 7, 6, 4, 3])[:, None, None]
    b = (b >> e) << e; x = (x >> e[:, :, 0]) << e[:, :, 0]
    b[:, 4:, 0] += 1; x[:, 4:] += 4
    return pack(rc, ic, b, cur, x)
def setup_inputs_ends(rng):
    rc, ic, b, cur, x = parts(rng); tg = [0, 1, 7, 8, 65279, 65280]; h = N // 2
    for t in range(RO):
        c = B0 + t * F; p = 1 << (c - 1).bit_length(); tg += [c - 1, c, c + 1, p - 1, p, p + c]
    b[::2, ::2] = heavy(rng, rng.choice(np.array(tg), (h, 4, B0)))
    b[::2, 1::4] = 255 * (b[::2, 1::4] & 1)
    rc[::2, 7] = (I0 - 1) * rng.integers(0, 2, (h, 16, R0)); ic[::2, 7] = (B0 - 1) * rng.integers(0, 2, (h, 16, I0)); cur[::2, 7] = (R0 - 1) * rng.integers(0, 2, (h, F))
    b[::2, 3] = np.where(rng.random((h, 1, B0)) < 0.25, 0, b[::2, 3]); b[:, 3, :, 0] = ((256 - RO) * 171) & 255
    cur[1::2, 0:6:2] = rng.integers(0, R0, (h, 3, 1)); rc[1::2, 1::4] = rng.integers(0, I0, (h, 2, 1, R0)); ic[1::2, 3] = rng.integers(0, B0, (h, 1, I0))
    b[1::2, 2] = np.take_along_axis(b[1::2, 2, :, :3], rng.integers(0, 3, (h, 1, B0)), 2)
    x[1::2, 4:6] = rng.integers(0, 256, (h, 2, 1))
    for g, z in ((6, 0), (7, int(rng.integers(1, 8)))):
        e = rng.integers(0, 256, 16); n = rng.integers(0, 256, 16)
        rest = int(weigh(n[:, None])[0]) - int(n[0]); n[0] = int(n[0]) // 8 * 8 + ((z - rest) & 7)
        old = (n - 3 * e) & 255; key = int(weigh(n[:, None])[0]) & 255
        v = int(weigh(old[:, None])[0]) & ((1 << (B0 - 1).bit_length()) - 1)
        if v >= B0: v -= B0
        c = (v + 1) % B0
        b[:, g, :, v] = e; b[1::2, g, :, c] = old; ic[1::2, g, key >> 4] = c; x[1::2, g] = key
    return pack(rc, ic, b, cur, x)
def setup_inputs_spread(rng):
    rc, ic, b, cur, x = parts(rng); k = rng.choice(np.array([1.0, 3.0, 8.0]), (N, 8, 1, 1))
    rc = np.minimum((I0 * rng.random((N, 8, 16, R0)) ** k).astype(np.int64), I0 - 1)
    ic = np.minimum((B0 * rng.random((N, 8, 16, I0)) ** k).astype(np.int64), B0 - 1)
    cur = np.minimum((R0 * rng.random((N, 8, F)) ** k[..., 0]).astype(np.int64), R0 - 1)
    b = b >> rng.integers(0, 9, (N, 8, 1, B0)); x = x >> rng.integers(0, 9, (N, 8, F))
    return pack(rc, ic, b, cur, x)
def check_inputs(d):
    bad = []
    for k, hi in (("rtab", I0 - 1), ("itab", B0 - 1), ("rn0", R0 - 1), ("x0", 255)):
        if np.min(d[k]) < 0 or np.max(d[k]) > hi: bad.append("range of " + k)
    v = np.asarray(d["btab"]).astype(np.float32)
    if not np.all((v >= 0) & (v <= 255) & (v == np.floor(v))): bad.append("whole numbers of btab")
    return bad
def reference(rtab, itab, btab, rn0, x0):
    r = rtab.astype(np.int64).reshape(N, 8, 16, R0); s = itab.astype(np.int64).reshape(N, 8, 16, I0); b = btab.astype(np.float32).astype(np.int64).reshape(N, 8, 16, B0)
    cur = np.stack([gentries(a) for a in rn0]).astype(np.int64); x = x0.astype(np.int64)
    f = np.arange(F); row = np.arange(16)[:, None]
    for t in range(RO):
        C = B0 + t * F; P = 1 << (C - 1).bit_length()
        d1 = (x & 15)[:, :, None, :]; d2 = ((x >> 4) & 15)[:, :, None, :]
        rc = np.take_along_axis(r, cur[:, :, None, :], 3)
        ic = np.take_along_axis(s, np.take_along_axis(rc, d1, 2), 3)
        old = np.take_along_axis(b, np.take_along_axis(ic, d2, 2), 3)
        h = weigh(old)
        to = (h + f) & (N - 1); v = h & (P - 1); v = np.where(v >= C, v - C, v)
        ok = np.zeros(to.shape, bool)
        for q in range(N):
            m = (to == q).astype(np.int64)
            ok |= (m == 1) & (np.add.accumulate(m, axis=2) - m < CAP)
        far = b[to[:, :, None, :], np.arange(8)[:, None, None], row, v[:, :, None, :]]
        far = np.where(ok[:, :, None, :], far, 0)
        new = (old + 3 * far + t) & 255
        ic = np.where(row == d2, B0 + t * F + f, ic); rc = np.where(row == d1, I0 + t * F + f, rc)
        b = np.concatenate([b, new], axis=3); s = np.concatenate([s, ic], axis=3); r = np.concatenate([r, rc], axis=3)
        x = weigh(new)
        cur = R0 + t * F + np.where((x & 7) == 0, (x >> 3) & (F - 1), f)
    return {"yb": new.reshape(N, 128, F).astype(np.float32).astype(BF), "yi": ic.reshape(N, 128, F).astype(np.float32), "yn": cur.astype(np.float32)}

@@ -1,0 +1,615 @@
+from concourse.bass import DstId, RemoteDMATransfer
+from concourse.mybir import AluOpType as ALU, ActivationFunctionType as ACT
+
+F, CAP, RO, N = 1024, 272, 3, 4
+ZP = 16
+NAT = ZP
+ORG = ZP + 2048
+TW = ORG + 4096 + 2048 + 4096
+BIG = 32768.0
+i32, u16, f32, f16, b16 = "int32", "uint16", "float32", "float16", "bfloat16"
+
+
+def _s(d, *shape):
+    return ("sbuf", [128] + list(shape), d)
+
+
+SCRATCH = {
+    "ri": _s(i32, 1024), "ii": _s(i32, 3072), "rn": _s(i32, 64), "x8": _s(i32, 1024), "x16": _s(f16, 1024),
+    "IT": _s(f32, 6144), "RT": _s(f32, 3, 1024), "IC": _s(f32, 1024), "SEL": _s(f16, 2, 1024), "E16": _s(f16, 4, 1024),
+    "YI": _s(f32, 1024), "STG": _s(b16, 3, 1024), "LND": _s(b16, 4, 1024), "TAB": _s(b16, TW), "OLD": _s(b16, 1024),
+    "G4": _s(b16, 4096), "Y": _s(b16, 1024), "NEW": _s(b16, 1024), "NEW4": _s(b16, 2, 4, 128),
+    "CUR": _s(u16, 64), "IL": _s(u16, 64), "OL": _s(u16, 64), "FL": _s(u16, 256),
+    "BN": _s(f16, 6, 32), "LB": _s(f16, 24, 32), "WS": _s(f16, 4, 64), "LW": _s(f16, 16, 64),
+    "YNS": _s(f32, 64), "LYN": _s(f32, 8, 8), "LYB": _s(b16, 8, 128),
+    "XI": _s(i32, 128), "D": _s(i32, 256), "DE": _s(f16, 256), "FT": _s(f16, 256),
+    "HI": _s(i32, 64), "Q0": _s(i32, 64), "O": _s(b16, 256), "SC": _s(b16, 2, 256), "VI": _s(i32, 128), "VF": _s(b16, 128),
+    "C12": _s(b16, 128), "GD": _s(b16, 256), "WI": _s(i32, 64), "W3": _s(i32, 192), "DFC": _s(f32, 192),
+    "PI": _s(i32, 16), "PF": _s(f32, 16), "DF": _s(f32, 56), "J": _s(b16, 256), "J8": _s(b16, 256), "J15": _s(b16, 128),
+    "JG": _s(b16, 128), "J31": _s(b16, 128), "CFI": _s(f32, 1024), "CF": _s(f16, 1024), "ONH": _s(f16, 512), "ONB": _s(b16, 512),
+    "FCI": _s(i32, 96), "FC": _s(f32, 192), "FC16": _s(f16, 64), "CQI": _s(i32, 4),
+    "WB": _s(b16, 144), "GB": _s(f16, 144), "CB": _s(b16, 224), "EA": _s(b16, 4, 224), "EM": _s(f16, 224), "FH": _s(f16, 2, 224),
+    "X0B": _s(f16, 144), "QT": _s(f16, 2, 128), "QB": _s(f16, 128), "QA": _s(f16, 8, 128), "CC": _s(f16, 144), "SQ": _s(f32, 128),
+    "KB": _s(f16, 128), "KZ": _s(f16, 128), "KA": _s(f16, 4, 128), "OG": _s(b16, 128), "T2": _s(b16, 4, 128), "SM": _s(b16, 256),
+    "RB": _s(b16, 128), "RA": _s(b16, 4, 128), "C3": _s(b16, 224), "IB": _s(b16, 128), "IH": _s(f16, 128),
+    "KS": _s(b16, 3, 128), "DI": _s(f16, 4, 128), "LO": _s(b16, 5, 144), "LF": _s(b16, 144), "WL": _s(b16, 144),
+}
+for _k in "XYZW":
+    for _h in "01":
+        SCRATCH["p" + _k + _h] = ("psum", [128, 512], f32)
+SHAPES = {k: v[1] for k, v in SCRATCH.items()}
+SHAPES.update({"rtab": [128, 1024], "itab": [128, 3072], "btab": [128, 4096], "rn0": [128, 64], "x0": [8, 1024],
+               "yb": [128, 1024], "yi": [128, 1024], "yn": [8, 1024]})
+SIZE = {k: (4 if v[2] in (i32, f32) else 2) for k, v in SCRATCH.items()}
+SIZE.update({"rtab": 4, "itab": 4, "btab": 2, "rn0": 4, "x0": 4, "yb": 2, "yi": 4, "yn": 4})
+PSUM = [k for k, v in SCRATCH.items() if v[0] == "psum"]
+ICH = [(0, 1280), (1280, 2560), (2560, 3072)]
+SEMAPHORES = (["ev", "ea", "et", "eg", "sent", "out", "lrn", "lx", "lr", "lown", "ls0", "ls1", "ls2", "li0", "li1", "li2"]
+              + ["ab%d" % q for q in range(N)] + ["an%d" % t for t in range(2 * RO)] + ["aw%d" % t for t in range(2 * RO)]
+              + ["ay0", "ay1"])
+CYC, GAT, PEC, HOP, FIX, BW, ROW, RIS, RLAT = 1.04e-3, 1.56, 0.5e-3, 0.06, 0.03, 250e3, 0.04, 0.6, 1.6
+TUNE = {"bias": 7.0, "pen": 1.0, "win": 0.08}
+
+
+def rank_program(g, core, T, topo):
+    me = T.rank_of(core)
+    if me is None:
+        return
+    Q = {"v": g.vector, "a": g.scalar, "t": g.tensor, "g": g, "s": g.sync}
+    ops = []
+    half = [None]
+    ALL = slice(None)
+
+    def A(name, *idx):
+        shp = SHAPES[name]
+        idx = list(idx) + [ALL] * (len(shp) - len(idx))
+        p = range(shp[0])[idx[0]]
+        lo = hi = 0
+        st = n = 1
+        for d in range(len(shp) - 1, 0, -1):
+            r = range(shp[d])[idx[d]]
+            a, b = (r, r) if isinstance(r, int) else (r[0], r[-1])
+            n *= 1 if isinstance(r, int) else len(r)
+            lo += a * st
+            hi += b * st
+            st *= shp[d]
+        reg = (name, 0, 128, 0, 512) if name in PSUM else (name, p[0], p[-1] + 1, lo, hi + 1)
+        return (T[name][tuple(idx)], [reg], n, SIZE[name], len(p))
+
+    def C(name, a, b, step=None):
+        return A(name, ALL, slice(a, b, step))
+
+    def col(name, k):
+        return C(name, k, k + 1)
+
+    def rows(name, a, b, *idx):
+        return A(name, slice(a, b), *idx)
+
+    def ind(win, off):
+        return (win[0].indirect(off[0]), win[1] + off[1], -16 * off[2], 4)
+
+    def regs(*xs):
+        out = []
+        for x in xs:
+            if isinstance(x, tuple):
+                out += x[1]
+        return out
+
+    def val(x):
+        return x[0] if isinstance(x, tuple) else x
+
+    def add(e, fn, rd, wr, cost, sem=None, n=0, after=None, lat=0.0):
+        ops.append({"e": e, "fn": fn, "rd": rd, "wr": wr, "sem": sem, "n": n, "cost": cost, "after": after, "lat": lat, "half": half[0]})
+        return len(ops) - 1
+
+    def tv(i, o, f=None):
+        if i[2] < 0:
+            return 0.06 - i[2] * GAT * CYC
+        return max(64, i[2] * (f or (0.5 if i[3] == 2 and o[3] == 2 else 1.0))) * CYC + FIX
+
+    def ta(i):
+        return (0.09 - i[2] * GAT * CYC) if i[2] < 0 else max(64, i[2]) * CYC + 2 * FIX
+
+    def lin(o, i, scale=None, bias=None, e="*"):
+        def fn(q):
+            if q == "a":
+                if bias is None:
+                    return g.scalar.activation(o[0], i[0], ACT.Copy, scale=1.0 if scale is None else val(scale))
+                return g.scalar.activation(o[0], i[0], ACT.Identity, bias=val(bias), scale=1.0 if scale is None else val(scale))
+            if scale is None and bias is None:
+                return g.vector.tensor_copy(o[0], i[0])
+            if bias is None:
+                return g.vector.tensor_scalar(o[0], i[0], val(scale), None, ALU.mult)
+            if scale is None:
+                return g.vector.tensor_scalar(o[0], i[0], val(bias), None, ALU.add)
+            return g.vector.tensor_scalar(o[0], i[0], val(scale), val(bias), ALU.mult, ALU.add)
+        add(e, fn, regs(i, scale, bias), o[1], {"v": tv(i, o), "a": ta(i)})
+
+    def cp(o, i):
+        lin(o, i, e="v")
+
+    def ts(o, i, s1, op0, s2=None, op1=None):
+        if op1 is None:
+            add("v", lambda q: g.vector.tensor_scalar(o[0], i[0], val(s1), None, op0), regs(i, s1), o[1], {"v": tv(i, o)})
+        else:
+            add("v", lambda q: g.vector.tensor_scalar(o[0], i[0], val(s1), val(s2), op0, op1), regs(i, s1, s2), o[1], {"v": tv(i, o)})
+
+    def tt(o, a, b, op):
+        f = 1.0 if a[1][0][0] in PSUM or b[1][0][0] in PSUM else 2.0
+        add("v", lambda q: g.vector.tensor_tensor(o[0], a[0], b[0], op), a[1] + b[1], o[1], {"v": tv(a, o, f)})
+
+    def ms(o, c):
+        add("v", lambda q: g.vector.memset(o[0], c), [], o[1], {"v": tv(o, o)})
+
+    def mm(o, l, r, start, stop):
+        add("t", lambda q: g.tensor.matmul(o[0], l[0], r[0], start, stop), l[1] + r[1], o[1],
+            {"t": max(64, r[2]) * PEC * (4 if l[3] == 4 else 1)})
+
+    def iota(o, pat, base, cm, fl=False):
+        c = {"g": 0.13 + 2 * o[2] * CYC}
+        if fl:
+            add("g", lambda q: g.iota(o[0], pat, base, cm, allow_small_or_imprecise_dtypes=True), [], o[1], c)
+        else:
+            add("g", lambda q: g.iota(o[0], pat, base, cm), [], o[1], c)
+
+    chain = [None]
+
+    def dma(e, o, i, sem, first=False):
+        k = add(e, lambda q: Q[q].dma_start(o[0], i[0]), i[1], o[1], {e: 0.1}, sem, 16, chain[0] if first else None,
+                o[2] * o[3] * o[4] / BW + max(o[4], i[4]) / 16 * ROW)
+        if first:
+            chain[0] = k
+
+    sent = [0]
+
+    def exchange(parts, sem, land, n):
+        trs = []
+        d = 0.0
+        for src, dsts, en in parts:
+            ids = [DstId(rid=topo.addr(T.cores[r])[0], pnc=topo.addr(T.cores[r])[1]) for r, _ in dsts]
+            trs.append(RemoteDMATransfer(dst_ids=ids, dma_engine_mask=sum(1 << x for x in en), remote_sem=T.sem[sem[0]],
+                                         srcs=[src[0]], dsts=[x[0] for _, x in dsts]))
+            sent[0] += len(en)
+            d = max(d, len(dsts) * (src[2] * src[3] * 128 / BW * 16 + 128 * ROW) / len(en))
+        k = add("g", lambda q: g.remote_dma_fused(trs, local_sem=T.sem.sent), regs(*[x[0] for x in parts]), [], {"g": RIS}, "remote", lat=d)
+        add("x", None, [], regs(*land), {"x": 0.0}, sem[1], n, k)
+
+    peers = [(me + k) % N for k in (1, 2, 3)]
+    order = [me] + peers
+    engs = [x for x in topo.engines(core, T.cores[peers[0]]) if all(x in topo.engines(core, T.cores[r]) for r in peers)]
+    NE = len(engs)
+    share = [engs[0:NE // 4], engs[NE // 4:NE // 2], engs[NE // 2:]]
+    EQ, MUL, ADD, SUB, AND, SHR = ALU.is_equal, ALU.mult, ALU.add, ALU.subtract, ALU.bitwise_and, ALU.logical_shift_right
+
+    dma("s", A("rn"), A("rn0"), "lrn", True)
+    dma("a", rows("x8", 0, 8), A("x0"), "lx", True)
+    dma("s", A("ri"), A("rtab"), "lr", True)
+    for j, o in enumerate(peers):
+        for c in range(4):
+            dma("sa"[c % 2], rows("STG", 32 * c, 32 * c + 32, j),
+                rows("btab", 32 * o, 32 * o + 32, slice(1024 * c, 1024 * c + 1024)), "ls%d" % j, True)
+    for j, (a, b) in enumerate(ICH):
+        dma("s", C("ii", a, b), C("itab", a, b), "li%d" % j, True)
+    dma("s", rows("TAB", 32 * me, 32 * me + 32, slice(ORG, ORG + 4096)), rows("btab", 32 * me, 32 * me + 32), "lown", True)
+    for j, o in enumerate(peers):
+        q = peers[2 - j]
+        exchange([(A("STG", ALL, j), [(o, A("LND", ALL, me))], engs)], ("ab%d" % me, "ab%d" % q), [A("LND", ALL, q)], NE)
+
+    iota(col("PI", 9), [[0, 1]], 0, 1)
+    iota(A("J"), [[1, 256]], 0, 0, True)
+    iota(A("J8"), [[16, 16], [0, 2], [1, 8]], 0, 0, True)
+    iota(A("J15"), [[0, 8], [1, 16]], 0, 0, True)
+    iota(A("JG"), [[16, 8], [0, 16]], 0, 0, True)
+    iota(A("J31"), [[0, 4], [1, 32]], 0, 0, True)
+    iota(A("CQI"), [[1, 4]], 128, -1)
+    iota(C("FCI", 0, 64), [[16, 64]], 0, 1)
+    iota(C("FCI", 64, 96), [[0, 4], [1, 8]], 0, 8)
+    for h in range(2):
+        iota(rows("CFI", 0, 32, slice(512 * h, 512 * h + 512)), [[1, 512]], 512 * h, 0, True)
+    ms(rows("ONH", 0, 32), 1.0)
+    ms(rows("ONB", 0, 32), 1.0)
+    ms(C("TAB", 0, ZP), 0.0)
+    ms(rows("KZ", 0, 32), ORG - BIG)
+    ms(A("SM"), 1.0)
+    ms(C("SM", 0, 256, 64), 0.0)
+    ms(A("O"), 0.0)
+    p = col("PI", 9)
+    for k, (sh, m) in enumerate([(0, 15), (0, 0x70), (0, 31), (5, 3), (3, 1), (0, 7), (2, 15), (0, 3), (0, 64)]):
+        ts(col("PI", k), p, sh, SHR, m, AND)
+    ts(col("PI", 10), p, 16, AND)
+    cp(C("PF", 0, 11), C("PI", 0, 11))
+    pi, pg, pr, pa, pb, p8, pi4, pc4, pv64, pp, pv16 = [col("PF", k) for k in range(11)]
+    dT0, dTW, dC10, dC5, dTC, dCC, dNB, dWT, dTE, dTF, dM5, dM10, dP0, dTL, dTWL, dW4, dCF0, dCF1 = [col("DF", k) for k in range(18)]
+    M8, AM, MF, KSC, CQ = 20, 28, 32, 36, 40
+
+    def low(k):
+        return rows("DF", 0, 32, slice(k, k + 1))
+
+    lin(dT0, pp, 16.0, 16.0)
+    lin(dTW, pg, None, 15.0)
+    lin(dC10, pb, -10.0, 10.0)
+    lin(dC5, pb, -5.0)
+    ts(dTC, pg, p8, ADD, 8.0, ADD)
+    lin(dCC, pb, 1280.0, -1200.0)
+    lin(dNB, pb, -1.0, 1.0)
+    ts(C("DF", M8, M8 + 8), C("J", 0, 8), p8, EQ)
+    ts(rows("X0B", 0, 32), rows("J8", 0, 32, slice(0, 144)), low(0), EQ)
+    lin(A("QT", ALL, 0), A("J15"), dC10, dC5)
+    ts(A("QT", ALL, 1), A("JG"), pg, EQ)
+    tt(A("SQ"), A("J15"), A("J15"), MUL)
+    tt(A("QB"), A("QT", ALL, 0), A("QT", ALL, 1), MUL)
+    lin(A("KB"), A("SQ"), -5.0, 4.0)
+    ts(A("GB"), C("J", 0, 144), dTW, EQ)
+    ts(A("CC"), C("J", 0, 144), dTC, EQ, dCC, MUL)
+    lin(rows("x16", 0, 8), rows("x8", 0, 8))
+    for a8 in range(8):
+        lin(A("QA", ALL, a8), A("QB"), col("DF", M8 + a8))
+    lin(dWT, pi, 2.0, 1.0)
+    lin(dTE, pr, None, 96.0)
+    ts(dTF, pv16, p8, ADD, 96.0, ADD)
+    ts(dM5, pp, 1.0, ALU.min, -5.0, MUL)
+    ts(dP0, pp, 0.0, EQ)
+    ts(C("DF", AM, AM + 4), C("J", 0, 4), pa, EQ)
+    ts(A("CQI"), A("CQI"), 3, AND)
+    ts(A("CB"), C("J", 0, 224), dTE, EQ)
+    ts(A("RB"), A("J31"), pr, EQ)
+    ts(C("DF", MF, MF + 2), C("J", 0, 2), pb, EQ, col("DF", AM + me), MUL)
+    cp(C("DF", CQ, CQ + 4), A("CQI"))
+    lin(A("EM"), A("CB"), col("DF", AM + me))
+    ts(A("WB"), C("J", 0, 144), dTW, EQ, dWT, MUL)
+    ts(A("OG"), A("JG"), pg, EQ)
+    ts(A("T2", ALL, 0), A("J15"), pi, ALU.is_lt, -1.0, MUL)
+    ts(A("IB"), C("J", 0, 128), pp, EQ)
+    lin(A("T2", ALL, 1), A("IB"), -2048.0)
+    lin(A("IH"), A("IB"))
+    tt(A("T2", ALL, 2), A("T2", ALL, 0), A("OG"), MUL)
+    tt(A("T2", ALL, 3), A("T2", ALL, 2), A("T2", ALL, 1), ADD)
+    lin(dCF0, dP0, 1.0 / 1024)
+    lin(dCF1, dP0, -1.0, 1.0)
+    for t in range(RO):
+        lin(col("DF", KSC + t), dP0, 49152.0 - t, float(t))
+        lin(rows("KS", 0, 32, t), rows("ONB", 0, 32, slice(0, 128)), low(KSC + t))
+    ts(dM10, pp, 1.0, ALU.min, -10.0, MUL)
+    ts(col("DF", 18), pp, 1.0, EQ, -5.0, MUL)
+    ts(col("DF", 19), pp, 1.0, ALU.not_equal, 0.5, MUL)
+    for k, (m, al) in enumerate([(18, low(19)), (10, 1.0), (10, 2.0), (11, 4.0)]):
+        lin(rows("KA", 0, 32, k), rows("SQ", 0, 32), low(m), al)
+    for h in range(2):
+        ts(A("FH", ALL, h), C("J8", 0, 224), dTF, EQ, col("DF", MF + h), MUL)
+        lin(rows("CF", 0, 32, slice(512 * h, 512 * h + 512)), rows("CFI", 0, 32, slice(512 * h, 512 * h + 512)), low(16), low(17))
+    for a in range(N):
+        lin(A("EA", ALL, a), A("CB"), col("DF", AM + a))
+        lin(A("RA", ALL, a), A("RB"), col("DF", AM + a))
+    lin(A("C3"), A("CB"), 3.0)
+    ts(C("FC", 0, 64), C("FCI", 0, 64), pg, SUB)
+    ts(C("FCI", 64, 96), C("FCI", 64, 96), 511, AND)
+    lin(A("FC16"), C("FC", 0, 64))
+    for h in range(2):
+        lin(C("FC", 64 + 32 * h, 96 + 32 * h), C("FCI", 64, 96), None, 512.0 * h)
+        lin(C("FC", 128 + 32 * h, 160 + 32 * h), C("FCI", 64, 96), None, 3072.0 + 512.0 * h)
+    lin(dTL, pr, 4.0, 3.0)
+    ts(col("DF", 48), pc4, 16.0, MUL, pv64, ADD)
+    lin(dW4, pi4, 2.0, 1.0)
+    ts(A("LO", ALL, 4), C("J", 0, 144), dTL, EQ)
+    lin(dTWL, col("DF", 48), None, 15.0)
+    ts(A("WL"), C("J", 0, 144), dTWL, EQ, dW4, MUL)
+    for a in range(N):
+        lin(A("LO", ALL, a), A("LO", ALL, 4), col("DF", AM + a))
+    lin(A("LF"), A("LO", ALL, 4), 3.0)
+    for k, s in enumerate([2048.0, -1024.0, -512.0, -256.0]):
+        lin(A("DI", ALL, k), A("IB"), s)
+    for a, b in ICH:
+        for x in range(a, b, 320 if b - a > 512 else 256):
+            y = x + (320 if b - a > 512 else 256)
+            lin(C("IT", x, y), C("ii", x, y), 1.0 / 2048, -1.0)
+    for q in peers[::-1]:
+        for c in range(4):
+            lin(rows("TAB", 32 * q, 32 * q + 32, slice(ORG + 1024 * c, ORG + 1024 * c + 1024)), rows("LND", 32 * c, 32 * c + 32, q))
+
+    def plane(ps, s, lvl, const, times=1):
+        mm(A(ps), const[0], const[1], True, False)
+        for rep in range(times):
+            for i in range(16):
+                o = 128 * s + 64 * lvl + 32 * (i // 8)
+                mm(C(ps, i, 512, 16), A("QA", ALL, i % 8), C("FT", o, o + 32), False, i == 15 and rep == times - 1)
+
+    def features(s, lvl):
+        o = 128 * s + 64 * lvl
+        ts(C("D", o, o + 64), C("XI", 64 * s, 64 * s + 64), 4 * lvl, SHR, 15, AND)
+        lin(C("DE", o, o + 64), C("D", o, o + 64), pb, dNB)
+        tt(C("FT", o, o + 64), C("D", o, o + 64), C("DE", o, o + 64), MUL)
+
+    def to_list(o, big, data, start=True):
+        for i in range(16):
+            mm(o, C(big, 15 - i, 143 - i), data(i), start and i == 0, i == 15)
+
+    def pick(o, s, lvl):
+        for h in range(2):
+            c = 128 * s + 64 * lvl + 32 * h
+            mm(o, C("CC", 8 - 8 * h, 136 - 8 * h), C("FT", c, c + 32), h == 0, False)
+        to_list(o, "GB", lambda i: A("SEL", ALL, lvl, slice(512 * s + i, 512 * s + 512, 16)), False)
+
+    def gather(dst, win, lst, k0, k1, step=16, scale=None, bias=None):
+        for k in range(k0, k1, step):
+            lin(dst(16 * k, 16 * k + 16 * step), ind(win, C(lst, k, k + step)), scale, bias)
+
+    def home(t, s):
+        X, Y, Z, W = ["p%s%d" % (x, s) for x in "XYZW"]
+        half[0] = s
+        k0, c0, u = 32 * s, 512 * s, 2 * t + s
+        rc = lambda a, b: A("RT", ALL, t, slice(a, b))
+        ic = (lambda a, b: C("IT", 3072 + a, 3072 + b)) if t == 0 else (lambda a, b: C("IC", a, b))
+        iw = C("IT", 0, (3072, 4096, 6144)[t])
+        xb = lambda h: C(Z, 32 * h, 32 * h + 32)
+        cur, il = C("CUR", k0, k0 + 32), C("IL", k0, k0 + 32)
+        KBc = (rows("KB", 0, 1), rows("ONH", 0, 1))
+        KAc = lambda k: (rows("KA", 0, 2 + (k == 0), k), rows("CF", 0, 2 + (k == 0), slice(c0, c0 + 512)))
+        if t == 0:
+            for h in range(2):
+                for a8 in range(8):
+                    mm(xb(h), rows("X0B", 0, 8, slice(16 - a8, 144 - a8)), rows("x16", 0, 8, slice(c0 + a8 + 8 * h, c0 + 512, 16)), a8 == 0, a8 == 7)
+            cp(cur, C("rn", k0, k0 + 32))
+            gather(rc, A("ri"), "CUR", k0, k0 + 32, 16, 1.0 / 2048, -1.0)
+        else:
+            src = lambda o, a, b: A("WS", ALL, u - 2, slice(a, b)) if o == me else A("LW", ALL, 4 * (u - 2) + o, slice(a, b))
+            mm(C(W, 0, 32), A("IH"), C("FC16", k0, k0 + 32), True, False)
+            for o in order:
+                mm(C(W, 0, 32), C("EM", 96 - 32 * o, 224 - 32 * o), src(o, 0, 32), False, o == order[-1])
+            for h in range(2):
+                for o in order:
+                    mm(xb(h), A("FH", ALL, h, slice(96 - 32 * o, 224 - 32 * o)), src(o, 32, 64), o == me, o == order[-1])
+            cp(cur, C(W, 0, 32))
+            gather(rc, A("RT", ALL, t - 1), "CUR", k0, k0 + 32)
+        cp(C("XI", 64 * s, 64 * s + 64), C(Z, 0, 64))
+        features(s, 0)
+        features(s, 1)
+        plane(X, s, 0, KBc)
+        tt(A("SEL", ALL, 0, slice(c0, c0 + 512)), rc(c0, c0 + 512), A(X), ALU.min)
+        pick(C(W, 32, 64), s, 0)
+        ts(il, C(W, 32, 64), 6141.0, ADD, 2048.0, MUL)
+        plane(Y, s, 1, KBc)
+        gather(ic, iw, "IL", k0, k0 + 32)
+        tt(A("SEL", ALL, 1, slice(c0, c0 + 512)), ic(c0, c0 + 512), A(Y), ALU.min)
+        pick(C(W, 64, 96), s, 1)
+        bn = A("BN", ALL, u)
+        lin(bn, C(W, 64, 96), None, 6140.0)
+        exchange([(bn, [(r, A("LB", ALL, 4 * u + me)) for r in peers], engs)], ("an%d" % u,) * 2,
+                 [A("LB", ALL, 4 * u + r) for r in peers], 3 * NE)
+        if t < 2:
+            plane(Z, s, 0, KAc(t))
+            tt(rc(c0, c0 + 512), rc(c0, c0 + 512), A(Z), ALU.max)
+        plane(X, s, 1, KAc(t + 1), 1 + (t == 2))
+        if t == 0:
+            tt(ic(c0, c0 + 512), ic(c0, c0 + 512), A(X), ALU.max)
+        elif t == 1:
+            tt(C("IT", 4096 + 2 * c0, 5120 + 2 * c0, 2), ic(c0, c0 + 512), A(X), ALU.max)
+        else:
+            e = lambda k: A("E16", ALL, k, slice(c0, c0 + 512))
+            tt(e(0), ic(c0, c0 + 512), A(X), ALU.max)
+            for k, x in ((1, 1.0), (2, 2.0), (3, 4.0)):
+                ts(e(k), e(0), x, SUB, 0.0, ALU.max)
+            for k in range(4):
+                mm(A(Y), A("DI", ALL, k), e(k), k == 0, k == 3)
+            lin(C("YI", c0, c0 + 512), A(Y), None, 2048.0)
+            dma("s", C("yi", c0, c0 + 512), C("YI", c0, c0 + 512), "out")
+
+    def owner(t, s):
+        FAR, SUM, CNT, W = ["p%s%d" % (x, s) for x in ("XZZW" if t == RO - 1 else "XYZW")]
+        half[0] = s
+        k0, c0, u = 32 * s, 512 * s, 2 * t + s
+        last = t == RO - 1
+        sm = lambda name, j=0: C(name, 64 * j + k0, 64 * j + k0 + 32)
+        for a in order:
+            mm(C(W, 96, 128), C("EM", 96 - 32 * a, 224 - 32 * a), A("BN", ALL, u) if a == me else A("LB", ALL, 4 * u + a),
+               a == me, a == order[-1])
+        ts(sm("OL"), C(W, 96, 128), 1.0, ADD, 2048.0, MUL)
+        gather(lambda a, b: C("OLD", a, b), C("TAB", ORG, ORG + (4096, 6144, 10240)[t]), "OL", k0, k0 + 32)
+        to_list(C(W, 128, 160), "WB", lambda i: C("OLD", c0 + i, c0 + 512, 16))
+        cp(sm("HI"), C(W, 128, 160))
+        ts(sm("Q0"), sm("HI"), 3, AND)
+        for q in range(N):
+            ts(sm("O", q), sm("Q0"), col("DF", CQ + q), EQ)
+        sc = A("SC", ALL, s)
+        add("v", lambda q: g.vector.tensor_tensor_scan(sc[0], A("SM")[0], A("O")[0], 0.0, MUL, ADD), regs(A("SM"), A("O")), sc[1],
+            {"v": tv(sc, sc)})
+        for q in range(N):
+            mm(C(CNT, 32 * q, 32 * q + 32), A("T2", ALL, 3), sm("O", q), True, False)
+            mm(C(CNT, 32 * q, 32 * q + 32), A("OG"), A("SC", ALL, s, slice(64 * q + k0, 64 * q + k0 + 32)), False, True)
+        lo, hi = C("VI", 2 * k0, 2 * k0 + 32), C("VI", 2 * k0 + 32, 2 * k0 + 64)
+        ts(lo, sm("HI"), 255, AND)
+        ts(hi, sm("HI"), (4096 if t == 0 else 8192) - 256, AND)
+        lin(C("VF", 2 * k0, 2 * k0 + 64), C("VI", 2 * k0, 2 * k0 + 64))
+        mm(C(FAR, 0, 128), rows("KZ", 0, 1), rows("ONH", 0, 1, slice(0, 128)), True, False)
+        feats = [C("VF", 2 * k0, 2 * k0 + 32), C("VF", 2 * k0 + 32, 2 * k0 + 64)]
+        if t >= 1:
+            ts(sm("C12"), hi, 4096.0, ALU.is_ge, -6144.0, MUL)
+            feats.append(sm("C12"))
+        if t == 1:
+            ts(sm("C12", 1), hi, 5120.0, ALU.is_ge, 1024.0, MUL)
+            feats.append(sm("C12", 1))
+        ts(C("GD", 128 * s, 128 * s + 128), C(CNT, 0, 128), CAP + 1 - 2048.0, ALU.is_lt, BIG, MUL)
+        for x in feats:
+            for a in range(N):
+                mm(C(FAR, 32 * a, 32 * a + 32), A("RA", ALL, a), x, False, False)
+        for a in range(N):
+            for q in range(N):
+                mm(C(FAR, 32 * a, 32 * a + 32), A("EA", ALL, a, slice(96 - 32 * q, 224 - 32 * q)),
+                   C("GD", 128 * s + 32 * q, 128 * s + 32 * q + 32), False, a == N - 1 and q == N - 1)
+        cp(C("FL", 128 * s, 128 * s + 128), C(FAR, 0, 128))
+        gather(lambda a, b: C("G4", a, b), C("TAB", 0, ORG + 4096), "FL", 128 * s, 128 * s + 128, 32)
+        mm(A(SUM), rows("KS", 0, 2, t), rows("ONB", 0, 2), True, False)
+        g0 = 2048 * s
+        if not last:
+            new = C("NEW", c0, c0 + 512)
+            mm(A(SUM), A("IB"), C("OLD", c0, c0 + 512), False, False)
+            for a in range(N):
+                mm(A(SUM), C("C3", 96 - 32 * a, 224 - 32 * a), C("G4", g0 + 512 * a, g0 + 512 * a + 512), False, a == N - 1)
+        else:
+            for a in range(N):
+                for c in range(4):
+                    mm(C(SUM, 128 * a, 128 * a + 128), A("LO", ALL, a, slice(3 - c, 131 - c)), C("OLD", c0 + 128 * c, c0 + 128 * c + 128), False, False)
+            for a in range(N):
+                for c in range(4):
+                    o = g0 + 512 * a + 128 * c
+                    mm(C(SUM, 128 * a, 128 * a + 128), C("LF", 3 - c, 131 - c), C("G4", o, o + 128), False, a == N - 1 and c == 3)
+        lin(C("Y", c0, c0 + 512), A(SUM), None, -127.5)
+        if not last:
+            tt(new, A(SUM), C("Y", c0, c0 + 512), SUB)
+            to_list(C(W, 160, 192), "WB", lambda i: C("NEW", c0 + i, c0 + 512, 16))
+        else:
+            for a in range(N):
+                tt(A("NEW4", ALL, s, a), C(SUM, 128 * a, 128 * a + 128), C("Y", c0 + 128 * a, c0 + 128 * a + 128), SUB)
+            exchange([(A("NEW4", ALL, s, r), [(r, A("LYB", ALL, 4 * s + me))], share[j]) for j, r in enumerate(peers)], ("ay%d" % s,) * 2,
+                     [A("LYB", ALL, 4 * s + r) for r in peers], NE)
+            for r in order:
+                dma("s", rows("yb", 32 * r, 32 * r + 32, slice(c0, c0 + 512)), A("NEW4", ALL, s, me) if r == me else A("LYB", ALL, 4 * s + r), "out")
+            to_list(C(W, 160, 192), "WL", lambda i: A("NEW4", ALL, s, ALL, slice(8 * i, 8 * i + 8)))
+        cp(sm("WI"), C(W, 160, 192))
+        ts(sm("W3"), sm("WI"), 3, SHR, 1023, AND)
+        ts(sm("W3", 1), sm("WI"), 7, AND)
+        if not last:
+            ts(sm("W3", 2), sm("WI"), 255, AND)
+            lin(A("WS", ALL, u, slice(32, 64)), sm("W3", 2))
+        tt(sm("DFC"), sm("W3"), sm("FC", 1 if last else 0), SUB)
+        ts(sm("DFC", 1), sm("W3", 1), 0.0, EQ)
+        if not last:
+            tt(A("WS", ALL, u, slice(0, 32)), sm("DFC"), sm("DFC", 1), MUL)
+            exchange([(A("WS", ALL, u), [(r, A("LW", ALL, 4 * u + me)) for r in peers], engs)], ("aw%d" % u,) * 2,
+                     [A("LW", ALL, 4 * u + r) for r in peers], 3 * NE)
+            lin(C("TAB", NAT + 1024 * t + c0, NAT + 1024 * t + c0 + 512), new)
+            st = (2, 4)[t]
+            o = ORG + (4096, 6144)[t] + st * c0
+            lin(C("TAB", o, o + 512 * st, st), new)
+        else:
+            tt(sm("DFC", 2), sm("DFC"), sm("DFC", 1), MUL)
+            tt(sm("YNS"), sm("DFC", 2), sm("FC", 2), ADD)
+            yns = lambda r: C("YNS", k0 + 8 * r, k0 + 8 * r + 8)
+            exchange([(yns(r), [(r, A("LYN", ALL, 4 * s + me))], share[j]) for j, r in enumerate(peers)], ("aw%d" % u,) * 2,
+                     [A("LYN", ALL, 4 * s + r) for r in peers], NE)
+            for j, r in enumerate(order):
+                dma("sa"[j % 2] if s else "s", rows("yn", 2 * r, 2 * r + 2, slice(c0, c0 + 512)), yns(me) if r == me else A("LYN", ALL, 4 * s + r), "out")
+
+    for t in range(RO):
+        home(t, 0)
+        home(t, 1)
+        owner(t, 0)
+        late = []
+        if t < RO - 1:
+            late = ops[-2:]
+            del ops[-2:]
+        owner(t, 1)
+        ops.extend(late)
+
+    def meet(x, y):
+        return x[1] < y[2] and y[1] < x[2] and x[3] < y[4] and y[3] < x[4]
+
+    n_ops = len(ops)
+    hist = {}
+    group = {}
+    for n, o in enumerate(ops):
+        if o["n"]:
+            group.setdefault(o["sem"], []).append(n)
+    for n, o in enumerate(ops):
+        pre = set()
+        for mine, w in [(r, False) for r in o["rd"]] + [(r, True) for r in o["wr"]]:
+            ps = mine[0] in PSUM
+            keep = []
+            for item in hist.get(mine[0], []):
+                m, reg, mw = item
+                if (w or mw or ps) and m != n and meet(mine, reg) and ops[m]["sem"] != "remote":
+                    pre.update(group[ops[m]["sem"]] if ops[m]["n"] else [m])
+                if not ((w or ps) and mine[1] <= reg[1] and reg[2] <= mine[2] and mine[3] <= reg[3] and reg[4] <= mine[4]):
+                    keep.append(item)
+            keep.append((n, mine, w))
+            hist[mine[0]] = keep
+        o["pre"] = pre
+        o["dep"] = pre | ({o["after"]} if o["after"] is not None else set())
+        o["post"] = []
+    for n, o in enumerate(ops):
+        for m in o["dep"]:
+            ops[m]["post"].append(n)
+    for n in range(n_ops - 1, -1, -1):
+        o = ops[n]
+        own = min(o["cost"].values()) + (o["lat"] + RLAT if o["sem"] and o["e"] != "x" else 0.0)
+        o["rank"] = own + max([ops[m]["rank"] + HOP for m in o["post"]] + [0.0])
+        o["prio"] = o["rank"] + TUNE["bias"] * (o["half"] == 0)
+    free = {e: 0.0 for e in "vatgsx"}
+    lanes = [0.0]
+    left = [len(o["dep"]) for o in ops]
+    ready = [n for n in range(n_ops) if not left[n]]
+    for n in ready:
+        ops[n]["at"] = 0.0
+    seq = []
+    while ready:
+        cand = []
+        for n in ready:
+            o = ops[n]
+            e = min(o["cost"] if o["e"] == "*" else [o["e"]],
+                    key=lambda x: max(free[x], o["at"]) + o["cost"][x] * (1.0 + TUNE["pen"] * (x == "v")))
+            cand.append((max(free[e], o["at"]), e, n))
+        t0, e0, _ = min(cand)
+        t1, e, n = max([c for c in cand if c[1] == e0 and c[0] <= t0 + TUNE["win"]], key=lambda c: (ops[c[2]]["prio"], -c[2]))
+        o = ops[n]
+        o["e"] = e
+        free[e] = end = t1 + o["cost"][e]
+        issue = end
+        if o["sem"] and e != "x":
+            lanes[0] = max(end + (0.6 if o["sem"] == "remote" else 1.0), lanes[0]) + o["lat"]
+            end = lanes[0] + 1.0
+        ready.remove(n)
+        seq.append(n)
+        for m in o["post"]:
+            q = ops[m]
+            link = issue if (q["after"] == n and q["e"] != "x" and n not in q["pre"]) else end + (0.0 if e == "t" and q["e"] == "t" or q["e"] == "x" else HOP)
+            q["at"] = max(q.get("at", 0.0), link)
+            left[m] -= 1
+            if not left[m]:
+                ready.append(m)
+    esem = {"v": "ev", "a": "ea", "t": "et", "g": "eg"}
+    total = {k: sum(ops[m]["n"] for m in v) for k, v in group.items()}
+    pos = {n: k for k, n in enumerate(seq)}
+    seen = {e: {} for e in Q}
+    for n in seq:
+        o = ops[n]
+        o["wait"] = []
+        if o["e"] == "x":
+            continue
+        need = {}
+        for m in o["pre"]:
+            pm = ops[m]
+            if pm["e"] == "t" and o["e"] == "t":
+                continue
+            key = pm["sem"] or pm["e"]
+            if key not in need or pos[m] > pos[need[key]]:
+                need[key] = m
+        for key, m in need.items():
+            if seen[o["e"]].get(key, -1) < pos[m]:
+                seen[o["e"]][key] = n_ops if ops[m]["sem"] else pos[m]
+                o["wait"].append(m)
+                ops[m]["sig"] = True
+    count = {e: 0 for e in esem}
+    for n in seq:
+        o = ops[n]
+        e = o["e"]
+        if e == "x":
+            continue
+        for m in o["wait"]:
+            pm = ops[m]
+            if pm["sem"]:
+                Q[e].wait_ge(T.sem[pm["sem"]], total[pm["sem"]])
+            else:
+                Q[e].wait_ge(T.sem[esem[pm["e"]]], pm["cnt"])
+        ins = o["fn"](e)
+        if o["sem"] == "remote":
+            continue
+        if o["sem"]:
+            ins.then_inc(T.sem[o["sem"]], 16)
+        elif o.get("sig"):
+            count[e] += 1
+            o["cnt"] = count[e]
+            ins.then_inc(T.sem[esem[e]], 1)
+    for e in esem:
+        if count[e]:
+            g.wait_ge(T.sem[esem[e]], count[e])
+    g.wait_ge(T.sem.sent, sent[0])
+    g.wait_ge(T.sem.out, total["out"])

@@ -17,17 +17,18 @@ def _s(d, *shape):
 SCRATCH = {
     "ri": _s(i32, 1024), "ii": _s(i32, 3072), "rn": _s(i32, 64), "x8": _s(i32, 1024), "x16": _s(f16, 1024),
     "IT": _s(f32, 6144), "RT": _s(f32, 3, 1024), "IC": _s(f32, 1024), "SEL": _s(f16, 2, 1024), "E16": _s(f16, 4, 1024),
-    "YI": _s(f32, 1024), "STG": _s(b16, 3, 1024), "LND": _s(b16, 4, 1024), "TAB": _s(b16, TW), "OLD": _s(b16, 1024),
+    "YI": _s(f32, 1024), "STG": _s(b16, 3, 1024), "LND": _s(b16, 4, 1024), "TAB": _s(b16, TW + 6144), "OLD": _s(b16, 1024),
+    "R2": _s(b16, 12, 128), "RT2": _s(b16, 2, 128), "LF2": _s(b16, 2, 144),
     "G4": _s(b16, 4096), "Y": _s(b16, 1024), "NEW": _s(b16, 1024), "NEW4": _s(b16, 2, 4, 128),
     "CUR": _s(u16, 64), "IL": _s(u16, 64), "OL": _s(u16, 64), "FL": _s(u16, 256),
     "BN": _s(f16, 6, 32), "LB": _s(f16, 24, 32), "WS": _s(f16, 4, 64), "LW": _s(f16, 16, 64),
-    "YNS": _s(f32, 64), "LYN": _s(f32, 8, 8), "LYB": _s(b16, 8, 128),
+    "YNS": _s(f32, 2, 128), "WI2": _s(i32, 6, 128), "DF2": _s(f32, 6, 128), "FL2": _s(f32, 4, 128), "LYB": _s(b16, 8, 128),
     "XI": _s(i32, 128), "D": _s(i32, 256), "DE": _s(f16, 256), "FT": _s(f16, 256),
     "HI": _s(i32, 64), "Q0": _s(i32, 64), "O": _s(b16, 256), "SC": _s(b16, 2, 256), "VI": _s(i32, 128), "VF": _s(b16, 128),
     "C12": _s(b16, 128), "GD": _s(b16, 256), "WI": _s(i32, 64), "W3": _s(i32, 192), "DFC": _s(f32, 192),
     "PI": _s(i32, 16), "PF": _s(f32, 16), "DF": _s(f32, 56), "J": _s(b16, 256), "J8": _s(b16, 256), "J15": _s(b16, 128),
     "JG": _s(b16, 128), "J31": _s(b16, 128), "CFI": _s(f32, 1024), "CF": _s(f16, 1024), "ONH": _s(f16, 512), "ONB": _s(b16, 512),
-    "FCI": _s(i32, 96), "FC": _s(f32, 192), "FC16": _s(f16, 64), "CQI": _s(i32, 4),
+    "FCI": _s(i32, 192), "FC": _s(f32, 64), "FC16": _s(f16, 64), "CQI": _s(i32, 4),
     "WB": _s(b16, 144), "GB": _s(f16, 144), "CB": _s(b16, 224), "EA": _s(b16, 4, 224), "EM": _s(f16, 224), "FH": _s(f16, 2, 224),
     "X0B": _s(f16, 144), "QT": _s(f16, 2, 128), "QB": _s(f16, 128), "QA": _s(f16, 8, 128), "CC": _s(f16, 144), "SQ": _s(f32, 128),
     "KB": _s(f16, 128), "KZ": _s(f16, 128), "KA": _s(f16, 4, 128), "OG": _s(b16, 128), "T2": _s(b16, 4, 128), "SM": _s(b16, 256),
@@ -45,10 +46,10 @@ SIZE.update({"rtab": 4, "itab": 4, "btab": 2, "rn0": 4, "x0": 4, "yb": 2, "yi": 
 PSUM = [k for k, v in SCRATCH.items() if v[0] == "psum"]
 ICH = [(0, 1280), (1280, 2560), (2560, 3072)]
 SEMAPHORES = (["ev", "ea", "et", "eg", "sent", "out", "lrn", "lx", "lr", "lown", "ls0", "ls1", "ls2", "li0", "li1", "li2"]
-              + ["ab%d" % q for q in range(N)] + ["an%d" % t for t in range(2 * RO)] + ["aw%d" % t for t in range(2 * RO)]
-              + ["ay0", "ay1"])
-CYC, GAT, PEC, HOP, FIX, BW, ROW, RIS, RLAT = 1.04e-3, 1.56, 0.5e-3, 0.06, 0.03, 250e3, 0.04, 0.6, 1.6
-TUNE = {"bias": 7.0, "pen": 1.0, "win": 0.08}
+              + ["ab%d" % q for q in range(N)] + ["an%d" % t for t in range(2 * RO)] + ["aw%d" % t for t in range(4)]
+              + ["ay0", "ay1", "rp", "rn0", "rn1", "rn2", "rn3"])
+CYC, GAT, PEC, HOP, FIX, BW, ROW, RIS, RLAT = 0.95e-3, 1.45, 0.5e-3, 0.07, 0.03, 250e3, 0.04, 0.6, 1.6
+TUNE = {"bias": 5.0, "pen": 0.6, "win": 0.08, "rel": 0.0}
 
 
 def rank_program(g, core, T, topo):
@@ -99,7 +100,8 @@ def rank_program(g, core, T, topo):
         return x[0] if isinstance(x, tuple) else x
 
     def add(e, fn, rd, wr, cost, sem=None, n=0, after=None, lat=0.0):
-        ops.append({"e": e, "fn": fn, "rd": rd, "wr": wr, "sem": sem, "n": n, "cost": cost, "after": after, "lat": lat, "half": half[0]})
+        ops.append({"e": e, "fn": fn, "rd": rd, "wr": wr, "sem": sem, "n": n, "cost": cost, "after": after, "lat": lat,
+                    "half": half[0], "pen": TUNE["pen"]})
         return len(ops) - 1
 
     def tv(i, o, f=None):
@@ -203,7 +205,7 @@ def rank_program(g, core, T, topo):
     iota(A("J31"), [[0, 4], [1, 32]], 0, 0, True)
     iota(A("CQI"), [[1, 4]], 128, -1)
     iota(C("FCI", 0, 64), [[16, 64]], 0, 1)
-    iota(C("FCI", 64, 96), [[0, 4], [1, 8]], 0, 8)
+    iota(C("FCI", 64, 192), [[1, 128]], 0, 128)
     for h in range(2):
         iota(rows("CFI", 0, 32, slice(512 * h, 512 * h + 512)), [[1, 512]], 512 * h, 0, True)
     ms(rows("ONH", 0, 32), 1.0)
@@ -282,20 +284,35 @@ def rank_program(g, core, T, topo):
         lin(A("RA", ALL, a), A("RB"), col("DF", AM + a))
     lin(A("C3"), A("CB"), 3.0)
     ts(C("FC", 0, 64), C("FCI", 0, 64), pg, SUB)
-    ts(C("FCI", 64, 96), C("FCI", 64, 96), 511, AND)
+    ts(C("FCI", 64, 192), C("FCI", 64, 192), 511, AND)
     lin(A("FC16"), C("FC", 0, 64))
     for h in range(2):
-        lin(C("FC", 64 + 32 * h, 96 + 32 * h), C("FCI", 64, 96), None, 512.0 * h)
-        lin(C("FC", 128 + 32 * h, 160 + 32 * h), C("FCI", 64, 96), None, 3072.0 + 512.0 * h)
+        lin(A("FL2", ALL, h), C("FCI", 64, 192), None, 512.0 * h)
+        lin(A("FL2", ALL, 2 + h), C("FCI", 64, 192), None, 3072.0 + 512.0 * h)
     lin(dTL, pr, 4.0, 3.0)
-    ts(col("DF", 48), pc4, 16.0, MUL, pv64, ADD)
+    ts(col("DF", 48), pv64, 1.0 / 16, MUL, pc4, ADD)
     lin(dW4, pi4, 2.0, 1.0)
     ts(A("LO", ALL, 4), C("J", 0, 144), dTL, EQ)
-    lin(dTWL, col("DF", 48), None, 15.0)
+    lin(dTWL, col("DF", 48), None, 24.0)
     ts(A("WL"), C("J", 0, 144), dTWL, EQ, dW4, MUL)
     for a in range(N):
         lin(A("LO", ALL, a), A("LO", ALL, 4), col("DF", AM + a))
     lin(A("LF"), A("LO", ALL, 4), 3.0)
+    for j in range(2):
+        for b in range(2):
+            for a in (j, j + 2):
+                x = (a & 2) | b
+                blk = lambda k: A("R2", ALL, k, slice(32 * x, 32 * x + 32))
+                lin(blk(j), A("RA", ALL, a, slice(0, 32)))
+                lin(A("R2", ALL, 10 + j, slice(32 * ((a & 2) | (1 - j)), 32 * ((a & 2) | (1 - j)) + 32)), A("RA", ALL, a, slice(0, 32)), 0.0)
+                for q in range(N):
+                    lin(blk(2 + 4 * j + q), A("RA", ALL, a, slice(0, 32)), 0.0 if q & 1 != b else 1.0 if q == x else 1.375)
+        tt(A("RT2", ALL, j, slice(0, 32)), A("RA", ALL, 2 * j, slice(0, 32)), A("RA", ALL, 2 * j + 1, slice(0, 32)), ADD)
+        tt(col("DF", 50 + j), col("DF", AM + 2 * j), col("DF", AM + 2 * j + 1), ADD)
+        lin(A("LF2", ALL, j), A("LF"), col("DF", 50 + j))
+    for j in range(2):
+        for h in range(2):
+            lin(A("R2", ALL, 10 + j, slice(64 * h + 32 * j, 64 * h + 32 * j + 32)), A("RT2", ALL, h, slice(0, 32)), 3.0)
     for k, s in enumerate([2048.0, -1024.0, -512.0, -256.0]):
         lin(A("DI", ALL, k), A("IB"), s)
     for a, b in ICH:
@@ -305,6 +322,9 @@ def rank_program(g, core, T, topo):
     for q in peers[::-1]:
         for c in range(4):
             lin(rows("TAB", 32 * q, 32 * q + 32, slice(ORG + 1024 * c, ORG + 1024 * c + 1024)), rows("LND", 32 * c, 32 * c + 32, q))
+            ops[-1]["pen"] = TUNE["rel"]
+    for h in range(2):
+        dma("s", rows("TAB", 64 * h, 64 * h + 64, slice(ORG + TW - ZP, ORG + TW - ZP + 4096)), rows("TAB", 64 - 64 * h, 128 - 64 * h, slice(ORG, ORG + 4096)), "rp")
 
     def plane(ps, s, lvl, const, times=1):
         mm(A(ps), const[0], const[1], True, False)
@@ -419,7 +439,8 @@ def rank_program(g, core, T, topo):
         ts(lo, sm("HI"), 255, AND)
         ts(hi, sm("HI"), (4096 if t == 0 else 8192) - 256, AND)
         lin(C("VF", 2 * k0, 2 * k0 + 64), C("VI", 2 * k0, 2 * k0 + 64))
-        mm(C(FAR, 0, 128), rows("KZ", 0, 1), rows("ONH", 0, 1, slice(0, 128)), True, False)
+        nf = 128 if t == 0 else 64
+        mm(C(FAR, 0, nf), rows("KZ", 0, 1), rows("ONH", 0, 1, slice(0, nf)), True, False)
         feats = [C("VF", 2 * k0, 2 * k0 + 32), C("VF", 2 * k0 + 32, 2 * k0 + 64)]
         if t >= 1:
             ts(sm("C12"), hi, 4096.0, ALU.is_ge, -6144.0, MUL)
@@ -429,29 +450,30 @@ def rank_program(g, core, T, topo):
             feats.append(sm("C12", 1))
         ts(C("GD", 128 * s, 128 * s + 128), C(CNT, 0, 128), CAP + 1 - 2048.0, ALU.is_lt, BIG, MUL)
         for x in feats:
-            for a in range(N):
-                mm(C(FAR, 32 * a, 32 * a + 32), A("RA", ALL, a), x, False, False)
-        for a in range(N):
+            for a in range(nf // 32):
+                mm(C(FAR, 32 * a, 32 * a + 32), A("R2" if t else "RA", ALL, a), x, False, False)
+        for a in range(nf // 32):
             for q in range(N):
-                mm(C(FAR, 32 * a, 32 * a + 32), A("EA", ALL, a, slice(96 - 32 * q, 224 - 32 * q)),
-                   C("GD", 128 * s + 32 * q, 128 * s + 32 * q + 32), False, a == N - 1 and q == N - 1)
-        cp(C("FL", 128 * s, 128 * s + 128), C(FAR, 0, 128))
-        gather(lambda a, b: C("G4", a, b), C("TAB", 0, ORG + 4096), "FL", 128 * s, 128 * s + 128, 32)
+                mm(C(FAR, 32 * a, 32 * a + 32), A("R2", ALL, 2 + 4 * a + q) if t else A("EA", ALL, a, slice(96 - 32 * q, 224 - 32 * q)),
+                   C("GD", 128 * s + 32 * q, 128 * s + 32 * q + 32), False, a == nf // 32 - 1 and q == N - 1)
+        cp(C("FL", 128 * s, 128 * s + nf), C(FAR, 0, nf))
+        gather(lambda a, b: C("G4", a, b), C("TAB", 0, TW + 6144 if t else ORG + 4096), "FL", 128 * s, 128 * s + nf, 32)
         mm(A(SUM), rows("KS", 0, 2, t), rows("ONB", 0, 2), True, False)
         g0 = 2048 * s
         if not last:
             new = C("NEW", c0, c0 + 512)
             mm(A(SUM), A("IB"), C("OLD", c0, c0 + 512), False, False)
-            for a in range(N):
-                mm(A(SUM), C("C3", 96 - 32 * a, 224 - 32 * a), C("G4", g0 + 512 * a, g0 + 512 * a + 512), False, a == N - 1)
+            for a in range(nf // 32):
+                mm(A(SUM), A("R2", ALL, 10 + a) if t else C("C3", 96 - 32 * a, 224 - 32 * a), C("G4", g0 + 512 * a, g0 + 512 * a + 512),
+                   False, a == nf // 32 - 1)
         else:
             for a in range(N):
                 for c in range(4):
                     mm(C(SUM, 128 * a, 128 * a + 128), A("LO", ALL, a, slice(3 - c, 131 - c)), C("OLD", c0 + 128 * c, c0 + 128 * c + 128), False, False)
             for a in range(N):
                 for c in range(4):
-                    o = g0 + 512 * a + 128 * c
-                    mm(C(SUM, 128 * a, 128 * a + 128), C("LF", 3 - c, 131 - c), C("G4", o, o + 128), False, a == N - 1 and c == 3)
+                    o = g0 + 512 * (a & 1) + 128 * c
+                    mm(C(SUM, 128 * a, 128 * a + 128), A("LF2", ALL, a // 2, slice(3 - c, 131 - c)), C("G4", o, o + 128), False, a == N - 1 and c == 3)
         lin(C("Y", c0, c0 + 512), A(SUM), None, -127.5)
         if not last:
             tt(new, A(SUM), C("Y", c0, c0 + 512), SUB)
@@ -463,31 +485,37 @@ def rank_program(g, core, T, topo):
                      [A("LYB", ALL, 4 * s + r) for r in peers], NE)
             for r in order:
                 dma("s", rows("yb", 32 * r, 32 * r + 32, slice(c0, c0 + 512)), A("NEW4", ALL, s, me) if r == me else A("LYB", ALL, 4 * s + r), "out")
-            to_list(C(W, 160, 192), "WL", lambda i: A("NEW4", ALL, s, ALL, slice(8 * i, 8 * i + 8)))
+            wp = rows(W, 0, 32, slice(256, 384))
+            for r in order:
+                mm(wp, C("WL", 24 - 8 * r, 56 - 8 * r), A("NEW4", ALL, s, me) if r == me else A("LYB", ALL, 4 * s + r), r == me, r == order[-1])
+            wi = lambda j: rows("WI2", 0, 32, 3 * s + j)
+            df = lambda j: rows("DF2", 0, 32, 3 * s + j)
+            cp(wi(0), wp)
+            ts(wi(1), wi(0), 3, SHR, 1023, AND)
+            ts(wi(2), wi(0), 7, AND)
+            tt(df(0), wi(1), rows("FL2", 0, 32, s), SUB)
+            ts(df(1), wi(2), 0.0, EQ)
+            tt(df(2), df(0), df(1), MUL)
+            tt(rows("YNS", 0, 32, s), df(2), rows("FL2", 0, 32, 2 + s), ADD)
+            dma("a" if s else "s", C("yn", c0, c0 + 512), rows("YNS", 0, 32, s), "out")
+            return
         cp(sm("WI"), C(W, 160, 192))
         ts(sm("W3"), sm("WI"), 3, SHR, 1023, AND)
         ts(sm("W3", 1), sm("WI"), 7, AND)
-        if not last:
-            ts(sm("W3", 2), sm("WI"), 255, AND)
-            lin(A("WS", ALL, u, slice(32, 64)), sm("W3", 2))
-        tt(sm("DFC"), sm("W3"), sm("FC", 1 if last else 0), SUB)
+        ts(sm("W3", 2), sm("WI"), 255, AND)
+        lin(A("WS", ALL, u, slice(32, 64)), sm("W3", 2))
+        tt(sm("DFC"), sm("W3"), sm("FC"), SUB)
         ts(sm("DFC", 1), sm("W3", 1), 0.0, EQ)
-        if not last:
-            tt(A("WS", ALL, u, slice(0, 32)), sm("DFC"), sm("DFC", 1), MUL)
-            exchange([(A("WS", ALL, u), [(r, A("LW", ALL, 4 * u + me)) for r in peers], engs)], ("aw%d" % u,) * 2,
-                     [A("LW", ALL, 4 * u + r) for r in peers], 3 * NE)
-            lin(C("TAB", NAT + 1024 * t + c0, NAT + 1024 * t + c0 + 512), new)
-            st = (2, 4)[t]
-            o = ORG + (4096, 6144)[t] + st * c0
-            lin(C("TAB", o, o + 512 * st, st), new)
-        else:
-            tt(sm("DFC", 2), sm("DFC"), sm("DFC", 1), MUL)
-            tt(sm("YNS"), sm("DFC", 2), sm("FC", 2), ADD)
-            yns = lambda r: C("YNS", k0 + 8 * r, k0 + 8 * r + 8)
-            exchange([(yns(r), [(r, A("LYN", ALL, 4 * s + me))], share[j]) for j, r in enumerate(peers)], ("aw%d" % u,) * 2,
-                     [A("LYN", ALL, 4 * s + r) for r in peers], NE)
-            for j, r in enumerate(order):
-                dma("sa"[j % 2] if s else "s", rows("yn", 2 * r, 2 * r + 2, slice(c0, c0 + 512)), yns(me) if r == me else A("LYN", ALL, 4 * s + r), "out")
+        tt(A("WS", ALL, u, slice(0, 32)), sm("DFC"), sm("DFC", 1), MUL)
+        exchange([(A("WS", ALL, u), [(r, A("LW", ALL, 4 * u + me)) for r in peers], engs)], ("aw%d" % u,) * 2,
+                 [A("LW", ALL, 4 * u + r) for r in peers], 3 * NE)
+        lin(C("TAB", NAT + 1024 * t + c0, NAT + 1024 * t + c0 + 512), new)
+        for h in range(2):
+            o = TW + 1024 * t + c0
+            dma("s", rows("TAB", 64 * h, 64 * h + 64, slice(o, o + 512)), rows("NEW", 64 - 64 * h, 128 - 64 * h, slice(c0, c0 + 512)), "rn%d" % u)
+        st = (2, 4)[t]
+        o = ORG + (4096, 6144)[t] + st * c0
+        lin(C("TAB", o, o + 512 * st, st), new)
 
     for t in range(RO):
         home(t, 0)
@@ -495,8 +523,8 @@ def rank_program(g, core, T, topo):
         owner(t, 0)
         late = []
         if t < RO - 1:
-            late = ops[-2:]
-            del ops[-2:]
+            late = ops[-4:]
+            del ops[-4:]
         owner(t, 1)
         ops.extend(late)
 
@@ -545,7 +573,7 @@ def rank_program(g, core, T, topo):
         for n in ready:
             o = ops[n]
             e = min(o["cost"] if o["e"] == "*" else [o["e"]],
-                    key=lambda x: max(free[x], o["at"]) + o["cost"][x] * (1.0 + TUNE["pen"] * (x == "v")))
+                    key=lambda x: max(free[x], o["at"]) + o["cost"][x] * (1.0 + o["pen"] * (x == "v")))
             cand.append((max(free[e], o["at"]), e, n))
         t0, e0, _ = min(cand)
         t1, e, n = max([c for c in cand if c[1] == e0 and c[0] <= t0 + TUNE["win"]], key=lambda c: (ops[c[2]]["prio"], -c[2]))

@@ -6,6 +6,7 @@ ZP = 16
 NAT = ZP
 ORG = ZP + 2048
 TW = ORG + 4096 + 2048 + 4096
+OR2 = ORG + TW - ZP
 BIG = 32768.0
 i32, u16, f32, f16, b16 = "int32", "uint16", "float32", "float16", "bfloat16"
 
@@ -18,7 +19,7 @@ SCRATCH = {
     "ri": _s(i32, 1024), "ii": _s(i32, 3072), "rn": _s(i32, 64), "x8": _s(i32, 1024), "x16": _s(f16, 1024),
     "IT": _s(f32, 6144), "RT": _s(f32, 3, 1024), "IC": _s(f32, 1024), "SEL": _s(f16, 2, 1024), "E16": _s(f16, 4, 1024),
     "YI": _s(f32, 1024), "STG": _s(b16, 3, 1024), "LND": _s(b16, 4, 1024), "TAB": _s(b16, TW + 6144), "OLD": _s(b16, 1024),
-    "R2": _s(b16, 12, 128), "RT2": _s(b16, 2, 128), "LF2": _s(b16, 2, 144),
+    "R2": _s(b16, 12, 128), "JP": _s(b16, 128), "LF2": _s(b16, 2, 144),
     "G4": _s(b16, 4096), "Y": _s(b16, 1024), "NEW": _s(b16, 1024), "NEW4": _s(b16, 2, 4, 128),
     "CUR": _s(u16, 64), "IL": _s(u16, 64), "OL": _s(u16, 64), "FL": _s(u16, 256),
     "BN": _s(f16, 6, 32), "LB": _s(f16, 24, 32), "WS": _s(f16, 4, 64), "LW": _s(f16, 16, 64),
@@ -29,10 +30,10 @@ SCRATCH = {
     "PI": _s(i32, 16), "PF": _s(f32, 16), "DF": _s(f32, 56), "J": _s(b16, 256), "J8": _s(b16, 256), "J15": _s(b16, 128),
     "JG": _s(b16, 128), "J31": _s(b16, 128), "CFI": _s(f32, 1024), "CF": _s(f16, 1024), "ONH": _s(f16, 512), "ONB": _s(b16, 512),
     "FCI": _s(i32, 192), "FC": _s(f32, 64), "FC16": _s(f16, 64), "CQI": _s(i32, 4),
-    "WB": _s(b16, 144), "GB": _s(f16, 144), "CB": _s(b16, 224), "EA": _s(b16, 4, 224), "EM": _s(f16, 224), "FH": _s(f16, 2, 224),
+    "WB": _s(b16, 144), "GB": _s(f16, 144), "CB": _s(b16, 224), "EM": _s(f16, 224), "FH": _s(f16, 2, 224),
     "X0B": _s(f16, 144), "QT": _s(f16, 2, 128), "QB": _s(f16, 128), "QA": _s(f16, 8, 128), "CC": _s(f16, 144), "SQ": _s(f32, 128),
     "KB": _s(f16, 128), "KZ": _s(f16, 128), "KA": _s(f16, 4, 128), "OG": _s(b16, 128), "T2": _s(b16, 4, 128), "SM": _s(b16, 256),
-    "RB": _s(b16, 128), "RA": _s(b16, 4, 128), "C3": _s(b16, 224), "IB": _s(b16, 128), "IH": _s(f16, 128),
+    "RB": _s(b16, 128), "RA": _s(b16, 4, 128), "IB": _s(b16, 128), "IH": _s(f16, 128),
     "KS": _s(b16, 3, 128), "DI": _s(f16, 4, 128), "LO": _s(b16, 5, 144), "LF": _s(b16, 144), "WL": _s(b16, 144),
 }
 for _k in "XYZW":
@@ -48,8 +49,8 @@ ICH = [(0, 1280), (1280, 2560), (2560, 3072)]
 SEMAPHORES = (["ev", "ea", "et", "eg", "sent", "out", "lrn", "lx", "lr", "lown", "ls0", "ls1", "ls2", "li0", "li1", "li2"]
               + ["ab%d" % q for q in range(N)] + ["an%d" % t for t in range(2 * RO)] + ["aw%d" % t for t in range(4)]
               + ["ay0", "ay1", "rp", "rn0", "rn1", "rn2", "rn3"])
-CYC, GAT, PEC, HOP, FIX, BW, ROW, RIS, RLAT = 0.95e-3, 1.45, 0.5e-3, 0.07, 0.03, 250e3, 0.04, 0.6, 1.6
-TUNE = {"bias": 5.0, "pen": 0.6, "win": 0.08, "rel": 0.0}
+CYC, GAT, PEC, HOP, FIX, BW, ROW, RIS, RLAT = 0.87e-3, 1.53, 0.49e-3, 0.075, 0.035, 290e3, 0.035, 0.6, 1.6
+TUNE = {"bias": 4.0, "pen": 0.5, "win": 0.06, "ext": 0.4}
 
 
 def rank_program(g, core, T, topo):
@@ -193,6 +194,7 @@ def rank_program(g, core, T, topo):
     for j, (a, b) in enumerate(ICH):
         dma("s", C("ii", a, b), C("itab", a, b), "li%d" % j, True)
     dma("s", rows("TAB", 32 * me, 32 * me + 32, slice(ORG, ORG + 4096)), rows("btab", 32 * me, 32 * me + 32), "lown", True)
+    dma("s", rows("TAB", 32 * (me ^ 2), 32 * (me ^ 2) + 32, slice(OR2, OR2 + 4096)), rows("btab", 32 * me, 32 * me + 32), "rp", True)
     for j, o in enumerate(peers):
         q = peers[2 - j]
         exchange([(A("STG", ALL, j), [(o, A("LND", ALL, me))], engs)], ("ab%d" % me, "ab%d" % q), [A("LND", ALL, q)], NE)
@@ -203,6 +205,7 @@ def rank_program(g, core, T, topo):
     iota(A("J15"), [[0, 8], [1, 16]], 0, 0, True)
     iota(A("JG"), [[16, 8], [0, 16]], 0, 0, True)
     iota(A("J31"), [[0, 4], [1, 32]], 0, 0, True)
+    iota(A("JP"), [[0, 2], [1, 2], [0, 32]], 0, 0, True)
     iota(A("CQI"), [[1, 4]], 128, -1)
     iota(C("FCI", 0, 64), [[16, 64]], 0, 1)
     iota(C("FCI", 64, 192), [[1, 128]], 0, 128)
@@ -279,10 +282,6 @@ def rank_program(g, core, T, topo):
     for h in range(2):
         ts(A("FH", ALL, h), C("J8", 0, 224), dTF, EQ, col("DF", MF + h), MUL)
         lin(rows("CF", 0, 32, slice(512 * h, 512 * h + 512)), rows("CFI", 0, 32, slice(512 * h, 512 * h + 512)), low(16), low(17))
-    for a in range(N):
-        lin(A("EA", ALL, a), A("CB"), col("DF", AM + a))
-        lin(A("RA", ALL, a), A("RB"), col("DF", AM + a))
-    lin(A("C3"), A("CB"), 3.0)
     ts(C("FC", 0, 64), C("FCI", 0, 64), pg, SUB)
     ts(C("FCI", 64, 192), C("FCI", 64, 192), 511, AND)
     lin(A("FC16"), C("FC", 0, 64))
@@ -298,21 +297,21 @@ def rank_program(g, core, T, topo):
     for a in range(N):
         lin(A("LO", ALL, a), A("LO", ALL, 4), col("DF", AM + a))
     lin(A("LF"), A("LO", ALL, 4), 3.0)
+    lin(col("DF", 51), pv64, 1.0 / 64)
+    lin(col("DF", 50), pv64, -1.0 / 64, 1.0)
+    ts(A("RA", ALL, 0), C("J", 0, 128), 64.0, ALU.is_ge, col("DF", 51), EQ)
+    tt(A("RA", ALL, 1), A("RA", ALL, 0), A("RB"), MUL)
+    tt(A("RA", ALL, 3), A("RA", ALL, 1), A("JP"), MUL)
+    tt(A("RA", ALL, 2), A("RA", ALL, 1), A("RA", ALL, 3), SUB)
     for j in range(2):
-        for b in range(2):
-            for a in (j, j + 2):
-                x = (a & 2) | b
-                blk = lambda k: A("R2", ALL, k, slice(32 * x, 32 * x + 32))
-                lin(blk(j), A("RA", ALL, a, slice(0, 32)))
-                lin(A("R2", ALL, 10 + j, slice(32 * ((a & 2) | (1 - j)), 32 * ((a & 2) | (1 - j)) + 32)), A("RA", ALL, a, slice(0, 32)), 0.0)
-                for q in range(N):
-                    lin(blk(2 + 4 * j + q), A("RA", ALL, a, slice(0, 32)), 0.0 if q & 1 != b else 1.0 if q == x else 1.375)
-        tt(A("RT2", ALL, j, slice(0, 32)), A("RA", ALL, 2 * j, slice(0, 32)), A("RA", ALL, 2 * j + 1, slice(0, 32)), ADD)
-        tt(col("DF", 50 + j), col("DF", AM + 2 * j), col("DF", AM + 2 * j + 1), ADD)
+        tt(col("DF", 44 + j), col("DF", AM + j), col("DF", AM + j + 2), ADD)
+        lin(col("DF", 52 + 2 * j), col("DF", AM + j + 2), 0.375, col("DF", 44 + j))
+        lin(col("DF", 53 + 2 * j), col("DF", AM + j), 0.375, col("DF", 44 + j))
+        lin(A("R2", ALL, j), A("RA", ALL, 1), col("DF", 44 + j))
+        for q in range(N):
+            lin(A("R2", ALL, 2 + 4 * j + q), A("RA", ALL, 2 + q % 2), col("DF", 52 + 2 * j + q // 2))
+        lin(A("R2", ALL, 10 + j), A("RA", ALL, 2 + j), 3.0)
         lin(A("LF2", ALL, j), A("LF"), col("DF", 50 + j))
-    for j in range(2):
-        for h in range(2):
-            lin(A("R2", ALL, 10 + j, slice(64 * h + 32 * j, 64 * h + 32 * j + 32)), A("RT2", ALL, h, slice(0, 32)), 3.0)
     for k, s in enumerate([2048.0, -1024.0, -512.0, -256.0]):
         lin(A("DI", ALL, k), A("IB"), s)
     for a, b in ICH:
@@ -322,9 +321,11 @@ def rank_program(g, core, T, topo):
     for q in peers[::-1]:
         for c in range(4):
             lin(rows("TAB", 32 * q, 32 * q + 32, slice(ORG + 1024 * c, ORG + 1024 * c + 1024)), rows("LND", 32 * c, 32 * c + 32, q))
-            ops[-1]["pen"] = TUNE["rel"]
-    for h in range(2):
-        dma("s", rows("TAB", 64 * h, 64 * h + 64, slice(ORG + TW - ZP, ORG + TW - ZP + 4096)), rows("TAB", 64 - 64 * h, 128 - 64 * h, slice(ORG, ORG + 4096)), "rp")
+            ops[-1]["pen"] = 0.0
+    for q in peers[::-1]:
+        for c in range(4):
+            o = OR2 + 1024 * c
+            dma("s", rows("TAB", 32 * (q ^ 2), 32 * (q ^ 2) + 32, slice(o, o + 1024)), rows("LND", 32 * c, 32 * c + 32, q), "rp")
 
     def plane(ps, s, lvl, const, times=1):
         mm(A(ps), const[0], const[1], True, False)
@@ -439,8 +440,7 @@ def rank_program(g, core, T, topo):
         ts(lo, sm("HI"), 255, AND)
         ts(hi, sm("HI"), (4096 if t == 0 else 8192) - 256, AND)
         lin(C("VF", 2 * k0, 2 * k0 + 64), C("VI", 2 * k0, 2 * k0 + 64))
-        nf = 128 if t == 0 else 64
-        mm(C(FAR, 0, nf), rows("KZ", 0, 1), rows("ONH", 0, 1, slice(0, nf)), True, False)
+        mm(C(FAR, 0, 64), rows("KZ", 0, 1), rows("ONH", 0, 1, slice(0, 64)), True, False)
         feats = [C("VF", 2 * k0, 2 * k0 + 32), C("VF", 2 * k0 + 32, 2 * k0 + 64)]
         if t >= 1:
             ts(sm("C12"), hi, 4096.0, ALU.is_ge, -6144.0, MUL)
@@ -450,23 +450,28 @@ def rank_program(g, core, T, topo):
             feats.append(sm("C12", 1))
         ts(C("GD", 128 * s, 128 * s + 128), C(CNT, 0, 128), CAP + 1 - 2048.0, ALU.is_lt, BIG, MUL)
         for x in feats:
-            for a in range(nf // 32):
-                mm(C(FAR, 32 * a, 32 * a + 32), A("R2" if t else "RA", ALL, a), x, False, False)
-        for a in range(nf // 32):
+            for a in range(2):
+                mm(C(FAR, 32 * a, 32 * a + 32), A("R2", ALL, a), x, False, False)
+        for a in range(2):
             for q in range(N):
-                mm(C(FAR, 32 * a, 32 * a + 32), A("R2", ALL, 2 + 4 * a + q) if t else A("EA", ALL, a, slice(96 - 32 * q, 224 - 32 * q)),
-                   C("GD", 128 * s + 32 * q, 128 * s + 32 * q + 32), False, a == nf // 32 - 1 and q == N - 1)
-        cp(C("FL", 128 * s, 128 * s + nf), C(FAR, 0, nf))
-        gather(lambda a, b: C("G4", a, b), C("TAB", 0, TW + 6144 if t else ORG + 4096), "FL", 128 * s, 128 * s + nf, 32)
-        mm(A(SUM), rows("KS", 0, 2, t), rows("ONB", 0, 2), True, False)
+                mm(C(FAR, 32 * a, 32 * a + 32), A("R2", ALL, 2 + 4 * a + q),
+                   C("GD", 128 * s + 32 * q, 128 * s + 32 * q + 32), False, a == 1 and q == N - 1)
+        cp(C("FL", 128 * s, 128 * s + 64), C(FAR, 0, 64))
+        gather(lambda a, b: C("G4", a, b), C("TAB", 0, TW + 6144), "FL", 128 * s, 128 * s + 64)
         g0 = 2048 * s
         if not last:
             new = C("NEW", c0, c0 + 512)
-            mm(A(SUM), A("IB"), C("OLD", c0, c0 + 512), False, False)
-            for a in range(nf // 32):
-                mm(A(SUM), A("R2", ALL, 10 + a) if t else C("C3", 96 - 32 * a, 224 - 32 * a), C("G4", g0 + 512 * a, g0 + 512 * a + 512),
-                   False, a == nf // 32 - 1)
+            for b, bank in enumerate((SUM, CNT)):
+                o, c = C(bank, 0, 256), c0 + 256 * b
+                mm(o, rows("KS", 0, 2, t), rows("ONB", 0, 2, slice(0, 256)), True, False)
+                mm(o, A("IB"), C("OLD", c, c + 256), False, False)
+                for a in range(2):
+                    mm(o, A("R2", ALL, 10 + a), C("G4", g0 + 512 * a + 256 * b, g0 + 512 * a + 256 * b + 256), False, a == 1)
+                lin(C("Y", c, c + 256), o, None, -127.5)
+                tt(C("NEW", c, c + 256), o, C("Y", c, c + 256), SUB)
+            to_list(C(W, 160, 192), "WB", lambda i: C("NEW", c0 + i, c0 + 512, 16))
         else:
+            mm(A(SUM), rows("KS", 0, 2, t), rows("ONB", 0, 2), True, False)
             for a in range(N):
                 for c in range(4):
                     mm(C(SUM, 128 * a, 128 * a + 128), A("LO", ALL, a, slice(3 - c, 131 - c)), C("OLD", c0 + 128 * c, c0 + 128 * c + 128), False, False)
@@ -474,11 +479,7 @@ def rank_program(g, core, T, topo):
                 for c in range(4):
                     o = g0 + 512 * (a & 1) + 128 * c
                     mm(C(SUM, 128 * a, 128 * a + 128), A("LF2", ALL, a // 2, slice(3 - c, 131 - c)), C("G4", o, o + 128), False, a == N - 1 and c == 3)
-        lin(C("Y", c0, c0 + 512), A(SUM), None, -127.5)
-        if not last:
-            tt(new, A(SUM), C("Y", c0, c0 + 512), SUB)
-            to_list(C(W, 160, 192), "WB", lambda i: C("NEW", c0 + i, c0 + 512, 16))
-        else:
+            lin(C("Y", c0, c0 + 512), A(SUM), None, -127.5)
             for a in range(N):
                 tt(A("NEW4", ALL, s, a), C(SUM, 128 * a, 128 * a + 128), C("Y", c0 + 128 * a, c0 + 128 * a + 128), SUB)
             exchange([(A("NEW4", ALL, s, r), [(r, A("LYB", ALL, 4 * s + me))], share[j]) for j, r in enumerate(peers)], ("ay%d" % s,) * 2,
@@ -583,7 +584,7 @@ def rank_program(g, core, T, topo):
         issue = end
         if o["sem"] and e != "x":
             lanes[0] = max(end + (0.6 if o["sem"] == "remote" else 1.0), lanes[0]) + o["lat"]
-            end = lanes[0] + 1.0
+            end = lanes[0] + 1.0 + (TUNE["ext"] if o["sem"] == "remote" else 0.0)
         ready.remove(n)
         seq.append(n)
         for m in o["post"]:

@@ -2,12 +2,15 @@ from concourse.bass import DstId, RemoteDMATransfer
 from concourse.mybir import AluOpType as ALU, ActivationFunctionType as ACT
 
 F, CAP, RO, N = 1024, 272, 3, 4
-ZP = 16
-NAT = ZP
-ORG = ZP + 2048
-TW = ORG + 4096 + 2048 + 4096
-OR2 = ORG + TW - ZP
+HELD = (2, 4, 4)
+NS = 2
+SEG = 6176
+POS = {3: 0, 1: 1, 2: 2, 0: 3}
+ORG = {j: SEG * k + 2080 for j, k in POS.items()}
+ORA = ORG[0]
+TW = 4 * SEG
 BIG = 32768.0
+HB = 1280.0
 i32, u16, f32, f16, b16 = "int32", "uint16", "float32", "float16", "bfloat16"
 
 
@@ -16,25 +19,27 @@ def _s(d, *shape):
 
 
 SCRATCH = {
-    "ri": _s(i32, 1024), "ii": _s(i32, 3072), "rn": _s(i32, 64), "x8": _s(i32, 1024), "x16": _s(f16, 1024),
-    "IT": _s(f32, 6144), "RT": _s(f32, 3, 1024), "IC": _s(f32, 1024), "SEL": _s(f16, 2, 1024), "E16": _s(f16, 4, 1024),
-    "YI": _s(f32, 1024), "STG": _s(b16, 3, 1024), "LND": _s(b16, 4, 1024), "TAB": _s(b16, TW + 6144), "OLD": _s(b16, 1024),
-    "R2": _s(b16, 12, 128), "JP": _s(b16, 128), "LF2": _s(b16, 2, 144),
-    "G4": _s(b16, 4096), "Y": _s(b16, 1024), "NEW": _s(b16, 1024), "NEW4": _s(b16, 2, 4, 128),
+    "rx": _s(i32, 128), "RX": _s(f16, 128), "XT": _s(f16, 128), "SR": _s(f16, 4, 288), "LR": _s(f16, 4, 288),
+    "SI": _s(i32, 4096), "SH": _s(f16, 3072), "LH": _s(f16, 4096), "SB": _s(b16, 3, 1024), "PK": _s(u16, 3, 512),
+    "LP": _s(u16, 4, 512),
+    "IT": _s(f32, 6144), "RT": _s(f32, 3, 1024), "IC": _s(f32, 1024), "SEL": _s(f16, 2, 1024),
+    "E0": _s(f16, 1024), "LE": _s(f16, 1024), "YI": _s(f32, 1024),
+    "TAB": _s(b16, TW + 6144), "OLD": _s(b16, 1024), "IS": _s(f16, 4, 128), "PX": _s(f16, 4, 128), "PS": _s(f16, 2, 128),
+    "G4": _s(f16, 4096), "Y": _s(b16, 1024), "NEW": _s(b16, 1024), "PY": _s(u16, 512), "LY": _s(u16, 512),
+    "HY": _s(f16, 512), "XY": _s(f32, 512), "NH": _s(b16, 1024),
     "CUR": _s(u16, 64), "IL": _s(u16, 64), "OL": _s(u16, 64), "FL": _s(u16, 256),
-    "BN": _s(f16, 6, 32), "LB": _s(f16, 24, 32), "WS": _s(f16, 4, 64), "LW": _s(f16, 16, 64),
-    "YNS": _s(f32, 2, 128), "WI2": _s(i32, 6, 128), "DF2": _s(f32, 6, 128), "FL2": _s(f32, 4, 128), "LYB": _s(b16, 8, 128),
-    "XI": _s(i32, 128), "D": _s(i32, 256), "DE": _s(f16, 256), "FT": _s(f16, 256),
-    "HI": _s(i32, 64), "Q0": _s(i32, 64), "O": _s(b16, 256), "SC": _s(b16, 2, 256), "VI": _s(i32, 128), "VF": _s(b16, 128),
-    "C12": _s(b16, 128), "GD": _s(b16, 256), "WI": _s(i32, 64), "W3": _s(i32, 192), "DFC": _s(f32, 192),
-    "PI": _s(i32, 16), "PF": _s(f32, 16), "DF": _s(f32, 56), "J": _s(b16, 256), "J8": _s(b16, 256), "J15": _s(b16, 128),
-    "JG": _s(b16, 128), "J31": _s(b16, 128), "CFI": _s(f32, 1024), "CF": _s(f16, 1024), "ONH": _s(f16, 512), "ONB": _s(b16, 512),
-    "FCI": _s(i32, 192), "FC": _s(f32, 64), "FC16": _s(f16, 64), "CQI": _s(i32, 4),
-    "WB": _s(b16, 144), "GB": _s(f16, 144), "CB": _s(b16, 224), "EM": _s(f16, 224), "FH": _s(f16, 2, 224),
-    "X0B": _s(f16, 144), "QT": _s(f16, 2, 128), "QB": _s(f16, 128), "QA": _s(f16, 8, 128), "CC": _s(f16, 144), "SQ": _s(f32, 128),
-    "KB": _s(f16, 128), "KZ": _s(f16, 128), "KA": _s(f16, 4, 128), "OG": _s(b16, 128), "T2": _s(b16, 4, 128), "SM": _s(b16, 256),
-    "RB": _s(b16, 128), "RA": _s(b16, 4, 128), "IB": _s(b16, 128), "IH": _s(f16, 128),
-    "KS": _s(b16, 3, 128), "DI": _s(f16, 4, 128), "LO": _s(b16, 5, 144), "LF": _s(b16, 144), "WL": _s(b16, 144),
+    "YNS": _s(f32, 64), "WI2": _s(i32, 3, 64), "DF2": _s(f32, 3, 64), "FL2": _s(f32, 2, 64),
+    "WI": _s(i32, 128), "W3": _s(i32, 2, 128), "DM": _s(f16, 3, 128), "FD": _s(f32, 128), "D": _s(i32, 2, 128), "FT": _s(f16, 2, 128),
+    "HI": _s(i32, 64), "Q0": _s(i32, 64), "O": _s(b16, 264), "SC": _s(b16, 264), "VI": _s(i32, 128), "VF": _s(b16, 128),
+    "C12": _s(b16, 128), "GD": _s(f16, 264),
+    "PI": _s(i32, 16), "PF": _s(f32, 16), "DF": _s(f32, 64), "J": _s(b16, 160), "J8": _s(b16, 144), "J15": _s(b16, 128),
+    "JG": _s(b16, 128), "JX": _s(b16, 4, 128), "CF": _s(f16, 1024), "ONH": _s(f16, 512),
+    "ONB": _s(b16, 512), "FCI": _s(i32, 256), "FC16": _s(f16, 64), "CQI": _s(i32, 16),
+    "WB": _s(b16, 144), "WD": _s(b16, 144), "GB": _s(f16, 144), "XP": _s(f16, 2, 144), "UU": _s(f16, 128),
+    "QT": _s(f16, 2, 128), "QB": _s(f16, 128), "QA": _s(f16, 8, 128), "CC": _s(f16, 144), "SQ": _s(f32, 2, 128),
+    "KB": _s(f16, 128), "KZ": _s(f16, 3, 128), "KA": _s(f16, 4, 128), "OG": _s(b16, 128), "T2": _s(b16, 4, 128), "SM": _s(b16, 256),
+    "IB": _s(b16, 2, 128), "IH": _s(f16, 3, 128),
+    "KS": _s(b16, 3, 128), "DI": _s(f16, 4, 128), "LO": _s(b16, 5, 144), "WL": _s(b16, 2, 160),
 }
 for _k in "XYZW":
     for _h in "01":
@@ -45,12 +50,11 @@ SHAPES.update({"rtab": [128, 1024], "itab": [128, 3072], "btab": [128, 4096], "r
 SIZE = {k: (4 if v[2] in (i32, f32) else 2) for k, v in SCRATCH.items()}
 SIZE.update({"rtab": 4, "itab": 4, "btab": 2, "rn0": 4, "x0": 4, "yb": 2, "yi": 4, "yn": 4})
 PSUM = [k for k, v in SCRATCH.items() if v[0] == "psum"]
-ICH = [(0, 1280), (1280, 2560), (2560, 3072)]
-SEMAPHORES = (["ev", "ea", "et", "eg", "sent", "out", "lrn", "lx", "lr", "lown", "ls0", "ls1", "ls2", "li0", "li1", "li2"]
-              + ["ab%d" % q for q in range(N)] + ["an%d" % t for t in range(2 * RO)] + ["aw%d" % t for t in range(4)]
-              + ["ay0", "ay1", "rp", "rn0", "rn1", "rn2", "rn3"])
-CYC, GAT, PEC, HOP, FIX, BW, ROW, RIS, RLAT = 0.87e-3, 1.53, 0.49e-3, 0.075, 0.035, 290e3, 0.035, 0.6, 1.6
-TUNE = {"bias": 4.0, "pen": 0.5, "win": 0.06, "ext": 0.4}
+SEMAPHORES = (["ev", "ea", "et", "eg", "sent", "out", "lrx", "ta", "tb1", "tb2", "tb3", "rn0", "rn1"]
+              + [x + "%d" % q for x in ("lb", "li", "lr", "le", "ap", "ah", "ar", "ae", "ay") for q in range(N)])
+CYC, GAT, PEC, HOP, FIX, BW, ROW, RIS, RLAT = 0.83e-3, 1.56, 0.42e-3, 0.15, 0.03, 350e3, 0.03, 0.5, 1.6
+TUNE = {"pen": 0.0, "win": 0.06, "ext": 0.1, "h1": 0, "h2": 2, "h3": 4, "h4": 6, "rs": 0.8, "first": 2.8,
+        "yi": 0.0, "pen2": 0.2, "passes": 4, "own": 1, "bias": 0.0, "nat": 1}
 
 
 def rank_program(g, core, T, topo):
@@ -59,7 +63,7 @@ def rank_program(g, core, T, topo):
         return
     Q = {"v": g.vector, "a": g.scalar, "t": g.tensor, "g": g, "s": g.sync}
     ops = []
-    half = [None]
+    stream = [None]
     ALL = slice(None)
 
     def A(name, *idx):
@@ -81,6 +85,9 @@ def rank_program(g, core, T, topo):
     def C(name, a, b, step=None):
         return A(name, ALL, slice(a, b, step))
 
+    def R(name, k, a=None, b=None, step=None):
+        return A(name, ALL, k, slice(a, b, step))
+
     def col(name, k):
         return C(name, k, k + 1)
 
@@ -100,18 +107,18 @@ def rank_program(g, core, T, topo):
     def val(x):
         return x[0] if isinstance(x, tuple) else x
 
-    def add(e, fn, rd, wr, cost, sem=None, n=0, after=None, lat=0.0):
-        ops.append({"e": e, "fn": fn, "rd": rd, "wr": wr, "sem": sem, "n": n, "cost": cost, "after": after, "lat": lat,
-                    "half": half[0], "pen": TUNE["pen"]})
+    def add(e, fn, rd, wr, cost, sem=None, n=0, after=None, lat=0.0, hold=()):
+        ops.append({"e": e, "fn": fn, "rd": rd, "wr": wr, "sem": sem, "n": n, "cost": cost, "after": after, "lat": lat, "hold": list(hold),
+                    "lead": TUNE["bias"] * (stream[0] == 0)})
         return len(ops) - 1
 
     def tv(i, o, f=None):
         if i[2] < 0:
-            return 0.06 - i[2] * GAT * CYC
+            return 0.05 - i[2] * GAT * CYC
         return max(64, i[2] * (f or (0.5 if i[3] == 2 and o[3] == 2 else 1.0))) * CYC + FIX
 
     def ta(i):
-        return (0.09 - i[2] * GAT * CYC) if i[2] < 0 else max(64, i[2]) * CYC + 2 * FIX
+        return (0.065 - i[2] * GAT * CYC) if i[2] < 0 else max(64, i[2]) * CYC + 2 * FIX
 
     def lin(o, i, scale=None, bias=None, e="*"):
         def fn(q):
@@ -126,10 +133,28 @@ def rank_program(g, core, T, topo):
             if scale is None:
                 return g.vector.tensor_scalar(o[0], i[0], val(bias), None, ALU.add)
             return g.vector.tensor_scalar(o[0], i[0], val(scale), val(bias), ALU.mult, ALU.add)
-        add(e, fn, regs(i, scale, bias), o[1], {"v": tv(i, o), "a": ta(i)})
+        return add(e, fn, regs(i, scale, bias), o[1], {"v": tv(i, o), "a": ta(i)})
 
     def cp(o, i):
-        lin(o, i, e="v")
+        return lin(o, i, e="v")
+
+    def act(o, i, func, scale, bias):
+        return add("a", lambda q: g.scalar.activation(o[0], i[0], func, bias=val(bias), scale=val(scale)), regs(i, scale, bias), o[1],
+                   {"a": ta(i)})
+
+    def relu(o, i, x):
+        def fn(q):
+            if q == "a":
+                return g.scalar.activation(o[0], i[0], ACT.Relu, bias=-x, scale=1.0)
+            return g.vector.tensor_scalar(o[0], i[0], x, 0.0, ALU.subtract, ALU.max)
+        return add("*", fn, i[1], o[1], {"v": tv(i, o), "a": ta(i)})
+
+    def is_zero(o, i):
+        def fn(q):
+            if q == "a":
+                return g.scalar.activation(o[0], i[0], ACT.Relu, bias=1.0, scale=-1.0)
+            return g.vector.tensor_scalar(o[0], i[0], 0.0, None, ALU.is_equal)
+        return add("*", fn, i[1], o[1], {"v": tv(i, o), "a": ta(i)})
 
     def ts(o, i, s1, op0, s2=None, op1=None):
         if op1 is None:
@@ -146,7 +171,7 @@ def rank_program(g, core, T, topo):
 
     def mm(o, l, r, start, stop):
         add("t", lambda q: g.tensor.matmul(o[0], l[0], r[0], start, stop), l[1] + r[1], o[1],
-            {"t": max(64, r[2]) * PEC * (4 if l[3] == 4 else 1)})
+            {"t": max(min(64, l[2]), r[2]) * PEC * (4 if l[3] == 4 else 1)})
 
     def iota(o, pat, base, cm, fl=False):
         c = {"g": 0.13 + 2 * o[2] * CYC}
@@ -157,377 +182,459 @@ def rank_program(g, core, T, topo):
 
     chain = [None]
 
-    def dma(e, o, i, sem, first=False):
-        k = add(e, lambda q: Q[q].dma_start(o[0], i[0]), i[1], o[1], {e: 0.1}, sem, 16, chain[0] if first else None,
-                o[2] * o[3] * o[4] / BW + max(o[4], i[4]) / 16 * ROW)
+    def dma(e, o, i, sem, first=False, hold=()):
+        run = min(o[2] if o[1][0][0] in SCRATCH else 1 << 20, i[2] if i[1][0][0] in SCRATCH else 1 << 20)
+        size = o[2] * o[3] * o[4]
+        k = add(e, lambda q: Q[q].dma_start(o[0], i[0]), i[1], o[1], {e: 0.06}, sem, 16, chain[0] if first else None,
+                size / BW + max(16, o[2] * o[4] / run) / 16 * ROW, hold)
         if first:
             chain[0] = k
-
-    sent = [0]
-
-    def exchange(parts, sem, land, n):
-        trs = []
-        d = 0.0
-        for src, dsts, en in parts:
-            ids = [DstId(rid=topo.addr(T.cores[r])[0], pnc=topo.addr(T.cores[r])[1]) for r, _ in dsts]
-            trs.append(RemoteDMATransfer(dst_ids=ids, dma_engine_mask=sum(1 << x for x in en), remote_sem=T.sem[sem[0]],
-                                         srcs=[src[0]], dsts=[x[0] for _, x in dsts]))
-            sent[0] += len(en)
-            d = max(d, len(dsts) * (src[2] * src[3] * 128 / BW * 16 + 128 * ROW) / len(en))
-        k = add("g", lambda q: g.remote_dma_fused(trs, local_sem=T.sem.sent), regs(*[x[0] for x in parts]), [], {"g": RIS}, "remote", lat=d)
-        add("x", None, [], regs(*land), {"x": 0.0}, sem[1], n, k)
+        return k
 
     peers = [(me + k) % N for k in (1, 2, 3)]
-    order = [me] + peers
     engs = [x for x in topo.engines(core, T.cores[peers[0]]) if all(x in topo.engines(core, T.cores[r]) for r in peers)]
     NE = len(engs)
-    share = [engs[0:NE // 4], engs[NE // 4:NE // 2], engs[NE // 2:]]
+    sent = [0]
+
+    def send(j, src, land, sem):
+        r, q = peers[j], peers[N - 2 - j]
+        rid, pnc = topo.addr(T.cores[r])[:2]
+        tr = RemoteDMATransfer(dst_ids=[DstId(rid=rid, pnc=pnc)], dma_engine_mask=sum(1 << x for x in engs),
+                               remote_sem=T.sem[sem + str(me)], srcs=[src[0]], dsts=[land(me)[0]])
+        sent[0] += NE
+        k = add("g", lambda _: g.remote_dma_fused([tr], local_sem=T.sem.sent), src[1], [], {"g": RIS}, "remote",
+                lat=src[2] * src[3] * 128 / BW + 128 * ROW / NE)
+        add("x", None, [], land(q)[1], {"x": 0.0}, sem + str(q), NE, k)
+
     EQ, MUL, ADD, SUB, AND, SHR = ALU.is_equal, ALU.mult, ALU.add, ALU.subtract, ALU.bitwise_and, ALU.logical_shift_right
 
-    dma("s", A("rn"), A("rn0"), "lrn", True)
-    dma("a", rows("x8", 0, 8), A("x0"), "lx", True)
-    dma("s", A("ri"), A("rtab"), "lr", True)
+    def load_inner(o, hold=()):
+        dma("s", C("SI", 1024 + 768 * o, 1792 + 768 * o), rows("itab", 32 * o, 32 * o + 32), "li%d" % o, True, hold)
+
+    dma("s", C("rx", 0, 64), A("rn0"), "lrx", True)
+    dma("s", C("rx", 64, 128), A("x0"), "lrx", True)
+    for o in peers + [me]:
+        dma("s", C("SI", 256 * o, 256 * o + 256), rows("rtab", 32 * o, 32 * o + 32), "lr%d" % o, True)
     for j, o in enumerate(peers):
-        for c in range(4):
-            dma("sa"[c % 2], rows("STG", 32 * c, 32 * c + 32, j),
-                rows("btab", 32 * o, 32 * o + 32, slice(1024 * c, 1024 * c + 1024)), "ls%d" % j, True)
-    for j, (a, b) in enumerate(ICH):
-        dma("s", C("ii", a, b), C("itab", a, b), "li%d" % j, True)
-    dma("s", rows("TAB", 32 * me, 32 * me + 32, slice(ORG, ORG + 4096)), rows("btab", 32 * me, 32 * me + 32), "lown", True)
-    dma("s", rows("TAB", 32 * (me ^ 2), 32 * (me ^ 2) + 32, slice(OR2, OR2 + 4096)), rows("btab", 32 * me, 32 * me + 32), "rp", True)
-    for j, o in enumerate(peers):
-        q = peers[2 - j]
-        exchange([(A("STG", ALL, j), [(o, A("LND", ALL, me))], engs)], ("ab%d" % me, "ab%d" % q), [A("LND", ALL, q)], NE)
+        dma("s", R("SB", j), rows("btab", 32 * o, 32 * o + 32), "lb%d" % j, True)
 
     iota(col("PI", 9), [[0, 1]], 0, 1)
-    iota(A("J"), [[1, 256]], 0, 0, True)
-    iota(A("J8"), [[16, 16], [0, 2], [1, 8]], 0, 0, True)
+    iota(A("J"), [[1, 160]], 0, 0, True)
+    iota(A("J8"), [[16, 9], [0, 2], [1, 8]], 0, 0, True)
     iota(A("J15"), [[0, 8], [1, 16]], 0, 0, True)
     iota(A("JG"), [[16, 8], [0, 16]], 0, 0, True)
-    iota(A("J31"), [[0, 4], [1, 32]], 0, 0, True)
-    iota(A("JP"), [[0, 2], [1, 2], [0, 32]], 0, 0, True)
-    iota(A("CQI"), [[1, 4]], 128, -1)
-    iota(C("FCI", 0, 64), [[16, 64]], 0, 1)
-    iota(C("FCI", 64, 192), [[1, 128]], 0, 128)
+    iota(R("JX", 0), [[1, 4], [4, 32]], 0, -1, True)
+    for j in range(1, N):
+        iota(R("JX", j), [[64 - 64 * (j & 2), 2], [32 - 64 * (j & 1), 2], [1, 32]], 32 * j, -1, True)
+    for a in range(N):
+        iota(C("CQI", 4 * a, 4 * a + 4), [[2 - 2 * (a & 2), 2], [1 - 2 * (a & 1), 2]], 128 + a, -1)
+    iota(C("FCI", 0, 64), [[16, 64]], 0, 0)
+    iota(C("FCI", 64, 128), [[1, 64]], 0, 64)
+    iota(C("FCI", 128, 256), [[8, 128]], 0, 0)
     for h in range(2):
-        iota(rows("CFI", 0, 32, slice(512 * h, 512 * h + 512)), [[1, 512]], 512 * h, 0, True)
+        iota(rows("YI", 0, 32, slice(512 * h, 512 * h + 512)), [[1, 512]], 512 * h, 0, True)
     ms(rows("ONH", 0, 32), 1.0)
     ms(rows("ONB", 0, 32), 1.0)
-    ms(C("TAB", 0, ZP), 0.0)
-    ms(rows("KZ", 0, 32), ORG - BIG)
+    START = [ORA - 32 if t == 0 and r == 1 else TW - SEG * r for t, r in enumerate(HELD)]
+    for t in range(RO):
+        if START[t] not in START[:t]:
+            ms(C("TAB", START[t], START[t] + 32), 0.0)
+        ms(rows("KZ", 0, 32, t), 2080.0 - START[t] - BIG)
     ms(A("SM"), 1.0)
-    ms(C("SM", 0, 256, 64), 0.0)
-    ms(A("O"), 0.0)
+    ms(C("SM", 0, 256, 64 // NS + NS - 1), 0.0)
+    ms(C("O", 0, 132), 0.0)
     p = col("PI", 9)
     for k, (sh, m) in enumerate([(0, 15), (0, 0x70), (0, 31), (5, 3), (3, 1), (0, 7), (2, 15), (0, 3), (0, 64)]):
         ts(col("PI", k), p, sh, SHR, m, AND)
     ts(col("PI", 10), p, 16, AND)
     cp(C("PF", 0, 11), C("PI", 0, 11))
     pi, pg, pr, pa, pb, p8, pi4, pc4, pv64, pp, pv16 = [col("PF", k) for k in range(11)]
-    dT0, dTW, dC10, dC5, dTC, dCC, dNB, dWT, dTE, dTF, dM5, dM10, dP0, dTL, dTWL, dW4, dCF0, dCF1 = [col("DF", k) for k in range(18)]
-    M8, AM, MF, KSC, CQ = 20, 28, 32, 36, 40
+    dTW, dC10, dC5, dTC, dCC, dNB, dWT, dTD, dP0, dTL, dTWL, dW4, dCF0, dCF1, dTX, dTY = [col("DF", k) for k in range(16)]
+    M8, AM, MF, KSC, CQ, KD = 20, 28, 32, 36, 40, 56
 
     def low(k):
         return rows("DF", 0, 32, slice(k, k + 1))
 
-    lin(dT0, pp, 16.0, 16.0)
-    lin(dTW, pg, None, 15.0)
-    lin(dC10, pb, -10.0, 10.0)
-    lin(dC5, pb, -5.0)
-    ts(dTC, pg, p8, ADD, 8.0, ADD)
-    lin(dCC, pb, 1280.0, -1200.0)
+    IB, I256, IH, IM = R("IB", 0), R("IB", 1), R("PX", 0), R("IH", 2)
+    ts(IB, C("J", 0, 128), pp, EQ)
+    ts(I256, C("J", 0, 128), pp, EQ, 256.0, MUL)
+    ts(IM, C("J", 0, 128), pp, EQ, -256.0, MUL)
+    ts(C("DF", AM, AM + 4), C("J", 0, 4), pa, EQ)
+    lin(dTL, pr, 4.0, 3.0)
+    ts(R("LO", 4), C("J", 0, 144), dTL, EQ)
+    for a in range(N):
+        lin(R("LO", a), R("LO", 4), col("DF", AM + a))
+    ts(A("UU"), R("JX", 0), 0.0, EQ)
+    lin(IH, IB)
     lin(dNB, pb, -1.0, 1.0)
+    lin(R("IH", 0), IB, dNB)
+    lin(R("IH", 1), IB, pb)
+    lin(dTW, pg, None, 15.0)
+    lin(dTD, pg, None, 7.0)
+    lin(dC10, pb, 10.0, -5.0)
+    lin(dC5, pb, 5.0, -5.0)
+    ts(dTC, pg, p8, ADD, 8.0, ADD)
+    lin(dCC, pb, -1280.0, 680.0)
     ts(C("DF", M8, M8 + 8), C("J", 0, 8), p8, EQ)
-    ts(rows("X0B", 0, 32), rows("J8", 0, 32, slice(0, 144)), low(0), EQ)
-    lin(A("QT", ALL, 0), A("J15"), dC10, dC5)
-    ts(A("QT", ALL, 1), A("JG"), pg, EQ)
-    tt(A("SQ"), A("J15"), A("J15"), MUL)
-    tt(A("QB"), A("QT", ALL, 0), A("QT", ALL, 1), MUL)
-    lin(A("KB"), A("SQ"), -5.0, 4.0)
+    lin(R("QT", 0), A("J15"), dC10, dC5)
+    ts(R("QT", 1), A("JG"), pg, EQ)
+    lin(R("SQ", 0), A("J15"), None, 1.0)
+    tt(R("SQ", 1), R("SQ", 0), A("J15"), MUL)
+    tt(A("QB"), R("QT", 0), R("QT", 1), MUL)
+    lin(A("KB"), R("SQ", 1), -5.0, 4.0)
     ts(A("GB"), C("J", 0, 144), dTW, EQ)
     ts(A("CC"), C("J", 0, 144), dTC, EQ, dCC, MUL)
-    lin(rows("x16", 0, 8), rows("x8", 0, 8))
     for a8 in range(8):
-        lin(A("QA", ALL, a8), A("QB"), col("DF", M8 + a8))
+        lin(R("QA", a8), A("QB"), col("DF", M8 + a8))
     lin(dWT, pi, 2.0, 1.0)
-    lin(dTE, pr, None, 96.0)
-    ts(dTF, pv16, p8, ADD, 96.0, ADD)
-    ts(dM5, pp, 1.0, ALU.min, -5.0, MUL)
     ts(dP0, pp, 0.0, EQ)
-    ts(C("DF", AM, AM + 4), C("J", 0, 4), pa, EQ)
     ts(A("CQI"), A("CQI"), 3, AND)
-    ts(A("CB"), C("J", 0, 224), dTE, EQ)
-    ts(A("RB"), A("J31"), pr, EQ)
-    ts(C("DF", MF, MF + 2), C("J", 0, 2), pb, EQ, col("DF", AM + me), MUL)
-    cp(C("DF", CQ, CQ + 4), A("CQI"))
-    lin(A("EM"), A("CB"), col("DF", AM + me))
+    for a in range(N):
+        lin(rows("DF", 32 * a, 32 * a + 32, slice(CQ, CQ + 4)), rows("CQI", 32 * a, 32 * a + 32, slice(4 * a, 4 * a + 4)))
     ts(A("WB"), C("J", 0, 144), dTW, EQ, dWT, MUL)
+    ts(A("WD"), A("J8"), dTD, EQ, dWT, MUL)
+    ts(dTX, pg, p8, ADD)
+    lin(dTY, pv16, 1.0 / 16)
+    ts(C("DF", MF, MF + 2), C("J", 0, 2), pb, EQ, dTY, MUL)
+    for h in range(2):
+        ts(R("XP", h), A("J8"), dTX, EQ, col("DF", MF + h), MUL)
     ts(A("OG"), A("JG"), pg, EQ)
-    ts(A("T2", ALL, 0), A("J15"), pi, ALU.is_lt, -1.0, MUL)
-    ts(A("IB"), C("J", 0, 128), pp, EQ)
-    lin(A("T2", ALL, 1), A("IB"), -2048.0)
-    lin(A("IH"), A("IB"))
-    tt(A("T2", ALL, 2), A("T2", ALL, 0), A("OG"), MUL)
-    tt(A("T2", ALL, 3), A("T2", ALL, 2), A("T2", ALL, 1), ADD)
+    ts(R("T2", 0), A("J15"), pi, ALU.is_lt, -1.0, MUL)
+    lin(R("T2", 1), IB, -2048.0)
+    tt(R("T2", 2), R("T2", 0), A("OG"), MUL)
+    tt(R("T2", 3), R("T2", 2), R("T2", 1), ADD)
     lin(dCF0, dP0, 1.0 / 1024)
     lin(dCF1, dP0, -1.0, 1.0)
     for t in range(RO):
         lin(col("DF", KSC + t), dP0, 49152.0 - t, float(t))
         lin(rows("KS", 0, 32, t), rows("ONB", 0, 32, slice(0, 128)), low(KSC + t))
-    ts(dM10, pp, 1.0, ALU.min, -10.0, MUL)
-    ts(col("DF", 18), pp, 1.0, EQ, -5.0, MUL)
-    ts(col("DF", 19), pp, 1.0, ALU.not_equal, 0.5, MUL)
-    for k, (m, al) in enumerate([(18, low(19)), (10, 1.0), (10, 2.0), (11, 4.0)]):
-        lin(rows("KA", 0, 32, k), rows("SQ", 0, 32), low(m), al)
+    ts(col("DF", KD), pp, 1.0, EQ, -5.0, MUL)
+    ts(col("DF", KD + 1), pp, 1.0, EQ, -10.0, MUL)
+    for k, al in enumerate((0.5, 1.0, 2.0, 4.0)):
+        ts(col("DF", KD + 2 + k), pp, 1.0, ALU.not_equal, al, MUL)
+        lin(rows("KA", 0, 32, k), rows("SQ", 0, 32, 1), low(KD + k // 3), low(KD + 2 + k))
     for h in range(2):
-        ts(A("FH", ALL, h), C("J8", 0, 224), dTF, EQ, col("DF", MF + h), MUL)
-        lin(rows("CF", 0, 32, slice(512 * h, 512 * h + 512)), rows("CFI", 0, 32, slice(512 * h, 512 * h + 512)), low(16), low(17))
-    ts(C("FC", 0, 64), C("FCI", 0, 64), pg, SUB)
-    ts(C("FCI", 64, 192), C("FCI", 64, 192), 511, AND)
-    lin(A("FC16"), C("FC", 0, 64))
-    for h in range(2):
-        lin(A("FL2", ALL, h), C("FCI", 64, 192), None, 512.0 * h)
-        lin(A("FL2", ALL, 2 + h), C("FCI", 64, 192), None, 3072.0 + 512.0 * h)
-    lin(dTL, pr, 4.0, 3.0)
+        lin(rows("CF", 0, 32, slice(512 * h, 512 * h + 512)), rows("YI", 0, 32, slice(512 * h, 512 * h + 512)), low(12), low(13))
+    lin(A("FC16"), C("FCI", 0, 64), None, pi)
+    lin(A("FD"), C("FCI", 128, 256), None, p8)
+    ts(C("FCI", 64, 128), C("FCI", 64, 128), 1023, AND)
+    lin(R("FL2", 0), C("FCI", 64, 128))
+    lin(R("FL2", 1), C("FCI", 64, 128), None, 3072.0)
     ts(col("DF", 48), pv64, 1.0 / 16, MUL, pc4, ADD)
     lin(dW4, pi4, 2.0, 1.0)
-    ts(A("LO", ALL, 4), C("J", 0, 144), dTL, EQ)
-    lin(dTWL, col("DF", 48), None, 24.0)
-    ts(A("WL"), C("J", 0, 144), dTWL, EQ, dW4, MUL)
-    for a in range(N):
-        lin(A("LO", ALL, a), A("LO", ALL, 4), col("DF", AM + a))
-    lin(A("LF"), A("LO", ALL, 4), 3.0)
-    lin(col("DF", 51), pv64, 1.0 / 64)
-    lin(col("DF", 50), pv64, -1.0 / 64, 1.0)
-    ts(A("RA", ALL, 0), C("J", 0, 128), 64.0, ALU.is_ge, col("DF", 51), EQ)
-    tt(A("RA", ALL, 1), A("RA", ALL, 0), A("RB"), MUL)
-    tt(A("RA", ALL, 3), A("RA", ALL, 1), A("JP"), MUL)
-    tt(A("RA", ALL, 2), A("RA", ALL, 1), A("RA", ALL, 3), SUB)
-    for j in range(2):
-        tt(col("DF", 44 + j), col("DF", AM + j), col("DF", AM + j + 2), ADD)
-        lin(col("DF", 52 + 2 * j), col("DF", AM + j + 2), 0.375, col("DF", 44 + j))
-        lin(col("DF", 53 + 2 * j), col("DF", AM + j), 0.375, col("DF", 44 + j))
-        lin(A("R2", ALL, j), A("RA", ALL, 1), col("DF", 44 + j))
-        for q in range(N):
-            lin(A("R2", ALL, 2 + 4 * j + q), A("RA", ALL, 2 + q % 2), col("DF", 52 + 2 * j + q // 2))
-        lin(A("R2", ALL, 10 + j), A("RA", ALL, 2 + j), 3.0)
-        lin(A("LF2", ALL, j), A("LF"), col("DF", 50 + j))
+    lin(dTWL, col("DF", 48), 4.0, 3.0)
+    ts(R("WL", 0, 0, 36), C("J", 0, 36), dTWL, EQ, dW4, MUL)
+    OWN = {1: 0, 2: 2, 4: 3}
+    unit = lambda j: (BIG + SEG * POS[j]) / 32
+    for j in range(N):
+        if any(j and not j & OWN[r] for r in HELD):
+            ts(R("PX", j), R("JX", j), 0.0, EQ)
+        if any(r > 1 and j & OWN[r] == j for r in HELD):
+            lin(R("IS", j), IB, unit(j))
+        if 2 in HELD and j & 1:
+            ts(R("PS", j // 2), R("JX", 1), 0.0, EQ, unit(j & 2), MUL)
     for k, s in enumerate([2048.0, -1024.0, -512.0, -256.0]):
-        lin(A("DI", ALL, k), A("IB"), s)
-    for a, b in ICH:
-        for x in range(a, b, 320 if b - a > 512 else 256):
-            y = x + (320 if b - a > 512 else 256)
-            lin(C("IT", x, y), C("ii", x, y), 1.0 / 2048, -1.0)
-    for q in peers[::-1]:
-        for c in range(4):
-            lin(rows("TAB", 32 * q, 32 * q + 32, slice(ORG + 1024 * c, ORG + 1024 * c + 1024)), rows("LND", 32 * c, 32 * c + 32, q))
-            ops[-1]["pen"] = 0.0
-    for q in peers[::-1]:
-        for c in range(4):
-            o = OR2 + 1024 * c
-            dma("s", rows("TAB", 32 * (q ^ 2), 32 * (q ^ 2) + 32, slice(o, o + 1024)), rows("LND", 32 * c, 32 * c + 32, q), "rp")
+        lin(R("DI", k), IB, s)
 
-    def plane(ps, s, lvl, const, times=1):
-        mm(A(ps), const[0], const[1], True, False)
+    lin(A("RX"), A("rx"))
+    for o in range(N):
+        for w in range(2):
+            for c in range(4):
+                mm(C("pW0", 32 * o + 16 * w, 32 * o + 16 * w + 16), R("LO", o, 3 - c, 131 - c),
+                   C("RX", 64 * w + 16 * c, 64 * w + 16 * c + 16), c == 0, c == 3)
+    for j, o in enumerate(peers + [me]):
+        lin(R("SR", o, 0, 256), C("SI", 256 * o, 256 * o + 256), 1.0 / 2048, -1.0)
+        lin(R("SR", o, 256, 288), C("pW0", 32 * o, 32 * o + 32))
+        if o != me:
+            send(j, R("SR", o), lambda r: R("LR", r), "ar")
+    load_inner(peers[0])
+    lx = lambda a, x, y: R("SR" if a == me else "LR", a, x, y)
+    uu = lambda c: C("UU", 32 * c, 32 * c + 32)
+    for a in [me] + peers[::-1]:
+        for c in range(4):
+            mm(rows("pW1", 32 * a, 32 * a + 32, slice(16 * c, 16 * c + 16)), uu(c), lx(a, 256, 272), True, True)
+            mm(rows("pZ%d" % (c // 2), 32 * a, 32 * a + 32, slice(256 * (c % 2), 256 * (c % 2) + 256)), uu(c), lx(a, 0, 256), True, True)
+        mm(rows("pW1", 32 * a, 32 * a + 32, slice(128, 256)), lx(a, 256, 288), IH, True, True)
+    for k in range(2):
+        lin(R("RT", 2, 512 * k, 512 * k + 512), A("pZ%d" % k))
+    cp(A("CUR"), C("pW1", 0, 64))
+    lin(A("XT"), C("pW1", 128, 256))
+    for h in range(2):
+        for v in range(2):
+            mm(C("pW1", 256 + h, 384, 2), R("XP", h, 16 - 16 * v, 144 - 16 * v), C("XT", 64 * v, 64 * v + 64), v == 0, v == 1)
+    cp(A("WI"), C("pW1", 256, 384))
+    packed = []
+    for j, o in enumerate(peers):
+        bank = ("pX0", "pY0", "pX1")[j]
+        mm(A(bank), IB, R("SB", j, 0, 512), True, False)
+        mm(A(bank), I256, R("SB", j, 512, 1024), False, True)
+        packed.append(cp(R("PK", j), A(bank)))
+        send(j, R("PK", j), lambda r: R("LP", r), "ap")
+    load_inner(peers[1], packed[TUNE["h1"]:][:1])
+    load_inner(peers[2], packed[TUNE["h2"]:][:1])
+    conv = []
+    for j, o in enumerate(peers + [me]):
+        if o == me:
+            load_inner(me, (packed + conv)[TUNE["h3"]:][:1])
+            dma("s", rows("TAB", 32 * me, 32 * me + 32, slice(ORA, ORA + 4096)), rows("btab", 32 * me, 32 * me + 32), "ta", True)
+        for x in range(768 * o, 768 * o + 768, 384):
+            conv.append(lin(C("SH", x, x + 384), C("SI", 1024 + x, 1408 + x), 1.0 / 2048, -1.0))
+        if o != me:
+            send(j, C("SH", 768 * o, 768 * o + 768), lambda r: C("LH", 768 * r, 768 * r + 768), "ah")
+
+    def split(lo, hi, x, hx, xx, ps):
+        lin(hx, x, 1.0 / 256, HB - 0.498, e="v")
+        lin(xx, x, None, 256.0 * HB)
+        mm(ps, IM, hx, True, True)
+        tt(lo, xx, ps, ADD)
+        lin(hi, hx, None, -HB)
+
+    def unstack():
+        for j, q in enumerate(peers[::-1]):
+            split(R("SB", j, 0, 512), R("SB", j, 512, 1024), R("LP", q), C("G4", 512 * j, 512 * j + 512),
+                  R("RT", 1, 512 * j, 512 * j + 512) if j < 2 else C("IC", 0, 512), A(("pZ0", "pZ1", "pY1")[j]))
+        inner = ["pY0", "pY1", "pX0", "pX1", "pZ0", "pZ1"]
+        for a in peers[::-1][:2] + [me] + peers[:1]:
+            for c in range(4):
+                x = 768 * c
+                while x < 768 * c + 768:
+                    y = min(768 * c + 768, x // 512 * 512 + 512)
+                    o = 768 * (a - c)
+                    mm(rows(inner[x // 512], 32 * a, 32 * a + 32, slice(x % 512, (y - 1) % 512 + 1)), uu(c),
+                       C("SH" if a == me else "LH", x + o, y + o), True, True)
+                    x = y
+        for k in range(6):
+            lin(C("IT", 512 * k, 512 * k + 512), A(inner[k]))
+        for j, q in enumerate(peers[::-1]):
+            dma("s", rows("TAB", 32 * q, 32 * q + 32, slice(ORA, ORA + 4096)), R("SB", j), "ta", True, conv[TUNE["h4"]:][:1])
+
+    def widen(src, j, a, b, sem):
+        n = 128 if j == 0 else 64 if j == 2 else 32
+        for x in range(0, 128, n):
+            y = x ^ (32 * j)
+            dma("s", rows("TAB", x, x + n, slice(a, b)), src(y, y + n), sem)
+
+    def held(t):
+        return {1: (0,), 2: (0, 2), 4: (0, 2, 1, 3)}[HELD[t]]
+
+    KW = 64 // NS
+    CW = KW + NS - 1
+
+    def plane(ps, s, lvl, k=None, times=1):
+        if k is None:
+            mm(A(ps), rows("KB", 0, 1), rows("ONH", 0, 1), True, False)
+        else:
+            mm(A(ps), rows("KA", 0, 3, k), rows("CF", 0, 3, slice(512 * s, 512 * s + 512)), True, False)
         for rep in range(times):
-            for i in range(16):
-                o = 128 * s + 64 * lvl + 32 * (i // 8)
-                mm(C(ps, i, 512, 16), A("QA", ALL, i % 8), C("FT", o, o + 32), False, i == 15 and rep == times - 1)
-
-    def features(s, lvl):
-        o = 128 * s + 64 * lvl
-        ts(C("D", o, o + 64), C("XI", 64 * s, 64 * s + 64), 4 * lvl, SHR, 15, AND)
-        lin(C("DE", o, o + 64), C("D", o, o + 64), pb, dNB)
-        tt(C("FT", o, o + 64), C("D", o, o + 64), C("DE", o, o + 64), MUL)
+            for i in range(8):
+                mm(C(ps, i, 512, 8), R("QA", i), R("FT", lvl, 64 * s, 64 * s + 64), False, i == 7 and rep == times - 1)
 
     def to_list(o, big, data, start=True):
         for i in range(16):
             mm(o, C(big, 15 - i, 143 - i), data(i), start and i == 0, i == 15)
 
-    def pick(o, s, lvl):
+    def gather(dst, win, lst, z):
+        for k in range(KW * z, KW * z + KW, 16):
+            lin(dst(16 * k, 16 * k + 256), ind(win, C(lst, k, k + 16)))
+
+    def level(t, lvl, z):
+        if lvl == 0:
+            got, win = lambda a, b: R("RT", t, a, b), R("RT", (t - 1) % RO)
+            app = got
+        else:
+            got, win = lambda a, b: C("IC", a, b) if t else C("IT", 3072 + a, 3072 + b), C("IT", 0, (3072, 4096, 6144)[t])
+            app = (got, lambda a, b: C("IT", 4096 + 2 * a, 4096 + 2 * b, 2), lambda a, b: C("E0", a, b))[t]
+        bank = lambda s: "p%s%d" % ("XY"[lvl], s)
+        k0, k1, hs = KW * z, KW * z + KW, range(2 * z // NS, (2 * z + 2) // NS)
+        stream[0] = z
+        o = C("pW%d" % z, 64 + 64 * lvl, 64 + 64 * lvl + KW)
+        gather(got, win, ("CUR", "IL")[lvl], z)
+        for s in hs:
+            plane(bank(s), s, lvl)
+            tt(R("SEL", lvl, 512 * s, 512 * s + 512), got(512 * s, 512 * s + 512), A(bank(s)), ALU.min)
         for h in range(2):
-            c = 128 * s + 64 * lvl + 32 * h
-            mm(o, C("CC", 8 - 8 * h, 136 - 8 * h), C("FT", c, c + 32), h == 0, False)
-        to_list(o, "GB", lambda i: A("SEL", ALL, lvl, slice(512 * s + i, 512 * s + 512, 16)), False)
+            mm(o, C("CC", 8 - 8 * h, 136 - 8 * h), R("FT", lvl, 2 * k0 + h, 2 * k1, 2), h == 0, False)
+        to_list(o, "GB", lambda i: R("SEL", lvl, 16 * k0 + i, 16 * k1, 16), False)
+        ts(C(("IL", "OL")[lvl], k0, k1), o, 6741.0, ADD, 2048.0, MUL)
+        for s in hs if lvl or t < RO - 1 else ():
+            plane(bank(s), s, lvl, t + lvl, 1 + (t == RO - 1))
+            tt(app(512 * s, 512 * s + 512), got(512 * s, 512 * s + 512), A(bank(s)), ALU.max)
 
-    def gather(dst, win, lst, k0, k1, step=16, scale=None, bias=None):
-        for k in range(k0, k1, step):
-            lin(dst(16 * k, 16 * k + 16 * step), ind(win, C(lst, k, k + step)), scale, bias)
+    def root_number(z, num, m, d, prod, w, f):
+        ts(z, w, 7, AND)
+        ts(num, w, 3, SHR, 1023, AND)
+        is_zero(m, z)
+        tt(d, num, f, SUB)
+        tt(prod, d, m, MUL)
 
-    def home(t, s):
-        X, Y, Z, W = ["p%s%d" % (x, s) for x in "XYZW"]
-        half[0] = s
-        k0, c0, u = 32 * s, 512 * s, 2 * t + s
-        rc = lambda a, b: A("RT", ALL, t, slice(a, b))
-        ic = (lambda a, b: C("IT", 3072 + a, 3072 + b)) if t == 0 else (lambda a, b: C("IC", a, b))
-        iw = C("IT", 0, (3072, 4096, 6144)[t])
-        xb = lambda h: C(Z, 32 * h, 32 * h + 32)
-        cur, il = C("CUR", k0, k0 + 32), C("IL", k0, k0 + 32)
-        KBc = (rows("KB", 0, 1), rows("ONH", 0, 1))
-        KAc = lambda k: (rows("KA", 0, 2 + (k == 0), k), rows("CF", 0, 2 + (k == 0), slice(c0, c0 + 512)))
-        if t == 0:
+    def keys(t, z):
+        W, k0, k1 = "pW%d" % z, KW * z, KW * z + KW
+        stream[0] = z
+        d = lambda name, j: R(name, j, 2 * k0, 2 * k1)
+        wi = C("WI", 2 * k0, 2 * k1)
+        if t:
+            cp(wi, C(W, 256, 256 + 2 * KW))
+            root_number(d("W3", 0), d("W3", 1), d("DM", 0), d("DM", 1), d("DM", 2), wi, C("FD", 2 * k0, 2 * k1))
+            mm(C(W, 0, KW), IH, C("FC16", k0, k1), True, False)
             for h in range(2):
-                for a8 in range(8):
-                    mm(xb(h), rows("X0B", 0, 8, slice(16 - a8, 144 - a8)), rows("x16", 0, 8, slice(c0 + a8 + 8 * h, c0 + 512, 16)), a8 == 0, a8 == 7)
-            cp(cur, C("rn", k0, k0 + 32))
-            gather(rc, A("ri"), "CUR", k0, k0 + 32, 16, 1.0 / 2048, -1.0)
-        else:
-            src = lambda o, a, b: A("WS", ALL, u - 2, slice(a, b)) if o == me else A("LW", ALL, 4 * (u - 2) + o, slice(a, b))
-            mm(C(W, 0, 32), A("IH"), C("FC16", k0, k0 + 32), True, False)
-            for o in order:
-                mm(C(W, 0, 32), C("EM", 96 - 32 * o, 224 - 32 * o), src(o, 0, 32), False, o == order[-1])
-            for h in range(2):
-                for o in order:
-                    mm(xb(h), A("FH", ALL, h, slice(96 - 32 * o, 224 - 32 * o)), src(o, 32, 64), o == me, o == order[-1])
-            cp(cur, C(W, 0, 32))
-            gather(rc, A("RT", ALL, t - 1), "CUR", k0, k0 + 32)
-        cp(C("XI", 64 * s, 64 * s + 64), C(Z, 0, 64))
-        features(s, 0)
-        features(s, 1)
-        plane(X, s, 0, KBc)
-        tt(A("SEL", ALL, 0, slice(c0, c0 + 512)), rc(c0, c0 + 512), A(X), ALU.min)
-        pick(C(W, 32, 64), s, 0)
-        ts(il, C(W, 32, 64), 6141.0, ADD, 2048.0, MUL)
-        plane(Y, s, 1, KBc)
-        gather(ic, iw, "IL", k0, k0 + 32)
-        tt(A("SEL", ALL, 1, slice(c0, c0 + 512)), ic(c0, c0 + 512), A(Y), ALU.min)
-        pick(C(W, 64, 96), s, 1)
-        bn = A("BN", ALL, u)
-        lin(bn, C(W, 64, 96), None, 6140.0)
-        exchange([(bn, [(r, A("LB", ALL, 4 * u + me)) for r in peers], engs)], ("an%d" % u,) * 2,
-                 [A("LB", ALL, 4 * u + r) for r in peers], 3 * NE)
-        if t < 2:
-            plane(Z, s, 0, KAc(t))
-            tt(rc(c0, c0 + 512), rc(c0, c0 + 512), A(Z), ALU.max)
-        plane(X, s, 1, KAc(t + 1), 1 + (t == 2))
-        if t == 0:
-            tt(ic(c0, c0 + 512), ic(c0, c0 + 512), A(X), ALU.max)
-        elif t == 1:
-            tt(C("IT", 4096 + 2 * c0, 5120 + 2 * c0, 2), ic(c0, c0 + 512), A(X), ALU.max)
-        else:
-            e = lambda k: A("E16", ALL, k, slice(c0, c0 + 512))
-            tt(e(0), ic(c0, c0 + 512), A(X), ALU.max)
+                mm(C(W, 0, KW), R("IH", h), R("DM", 2, 2 * k0 + h, 2 * k1, 2), False, h == 1)
+            cp(C("CUR", k0, k1), C(W, 0, KW))
+        for lvl in range(2):
+            ts(d("D", lvl), wi, 4 * lvl, SHR, 15, AND)
+            act(d("FT", lvl), d("D", lvl), ACT.Square, 1.0, pb)
+
+    def send_inner():
+        le = lambda r: C("LE", 256 * r, 256 * r + 256)
+        for j, r in enumerate(peers + [me]):
+            dma("s", le(me) if r == me else C("LH", 256 * r, 256 * r + 256), rows("E0", 32 * r, 32 * r + 32), "le%d" % r)
+            if r != me:
+                send(j, C("LH", 256 * r, 256 * r + 256), le, "ae")
+        for s in range(2):
+            e = lambda k: C("LH" if k else "LE", 1024 * k + 512 * s, 1024 * k + 512 * s + 512)
             for k, x in ((1, 1.0), (2, 2.0), (3, 4.0)):
-                ts(e(k), e(0), x, SUB, 0.0, ALU.max)
+                relu(e(k), e(0), x)
             for k in range(4):
-                mm(A(Y), A("DI", ALL, k), e(k), k == 0, k == 3)
-            lin(C("YI", c0, c0 + 512), A(Y), None, 2048.0)
-            dma("s", C("yi", c0, c0 + 512), C("YI", c0, c0 + 512), "out")
+                mm(A("pY%d" % s), R("DI", k), e(k), k == 0, k == 3)
+            lin(C("YI", 512 * s, 512 * s + 512), A("pY%d" % s), None, 2048.0)
+        for r in range(N):
+            dma("s", rows("yi", 32 * r, 32 * r + 32), C("YI", 256 * r, 256 * r + 256), "out")
 
-    def owner(t, s):
-        FAR, SUM, CNT, W = ["p%s%d" % (x, s) for x in ("XZZW" if t == RO - 1 else "XYZW")]
-        half[0] = s
-        k0, c0, u = 32 * s, 512 * s, 2 * t + s
-        last = t == RO - 1
-        sm = lambda name, j=0: C(name, 64 * j + k0, 64 * j + k0 + 32)
-        for a in order:
-            mm(C(W, 96, 128), C("EM", 96 - 32 * a, 224 - 32 * a), A("BN", ALL, u) if a == me else A("LB", ALL, 4 * u + a),
-               a == me, a == order[-1])
-        ts(sm("OL"), C(W, 96, 128), 1.0, ADD, 2048.0, MUL)
-        gather(lambda a, b: C("OLD", a, b), C("TAB", ORG, ORG + (4096, 6144, 10240)[t]), "OL", k0, k0 + 32)
-        to_list(C(W, 128, 160), "WB", lambda i: C("OLD", c0 + i, c0 + 512, 16))
-        cp(sm("HI"), C(W, 128, 160))
+    def blocks(t, z):
+        own = OWN[HELD[t]]
+        nb = N // HELD[t]
+        W, FAR = "pW%d" % z, "pW1" if NS == 1 else "pX%d" % z
+        k0, k1, c0, c1 = KW * z, KW * z + KW, 16 * KW * z, 16 * KW * (z + 1)
+        stream[0] = z
+        sm = lambda name, j=0: C(name, 64 * j + k0, 64 * j + k1)
+        cl = lambda name, j: C(name, 4 * CW * z + CW * j + NS - 1, 4 * CW * z + CW * j + CW)
+        cz = lambda name: C(name, 4 * CW * z, 4 * CW * z + 4 * CW)
+        gather(lambda a, b: C("OLD", a, b), C("TAB", ORA, ORA + (4096, 6144, 10240)[t]), "OL", z)
+        to_list(C(W, 192, 192 + KW), "WB", lambda i: C("OLD", c0 + i, c1, 16))
+        cp(sm("HI"), C(W, 192, 192 + KW))
         ts(sm("Q0"), sm("HI"), 3, AND)
-        for q in range(N):
-            ts(sm("O", q), sm("Q0"), col("DF", CQ + q), EQ)
-        sc = A("SC", ALL, s)
-        add("v", lambda q: g.vector.tensor_tensor_scan(sc[0], A("SM")[0], A("O")[0], 0.0, MUL, ADD), regs(A("SM"), A("O")), sc[1],
-            {"v": tv(sc, sc)})
-        for q in range(N):
-            mm(C(CNT, 32 * q, 32 * q + 32), A("T2", ALL, 3), sm("O", q), True, False)
-            mm(C(CNT, 32 * q, 32 * q + 32), A("OG"), A("SC", ALL, s, slice(64 * q + k0, 64 * q + k0 + 32)), False, True)
-        lo, hi = C("VI", 2 * k0, 2 * k0 + 32), C("VI", 2 * k0 + 32, 2 * k0 + 64)
-        ts(lo, sm("HI"), 255, AND)
+        if z:
+            lin(C("O", 4 * CW, 8 * CW, CW), C("SC", KW, 4 * CW, CW))
+        for j in range(N):
+            ts(cl("O", j), sm("Q0"), col("DF", CQ + j), EQ)
+        mask = C("SM", 0, 4 * CW)
+        add("v", lambda q: g.vector.tensor_tensor_scan(cz("SC")[0], mask[0], cz("O")[0], 0.0, MUL, ADD), regs(mask, cz("O")), cz("SC")[1],
+            {"v": tv(cz("SC"), cz("SC"))})
+        cnt = C(W, 256, 256 + 4 * CW)
+        mm(cnt, R("T2", 3), cz("O"), True, False)
+        mm(cnt, A("OG"), cz("SC"), False, True)
+        hi = C("VI", 2 * k0 + KW, 2 * k1)
+        ts(C("VI", 2 * k0, 2 * k0 + KW), sm("HI"), 255, AND)
         ts(hi, sm("HI"), (4096 if t == 0 else 8192) - 256, AND)
-        lin(C("VF", 2 * k0, 2 * k0 + 64), C("VI", 2 * k0, 2 * k0 + 64))
-        mm(C(FAR, 0, 64), rows("KZ", 0, 1), rows("ONH", 0, 1, slice(0, 64)), True, False)
-        feats = [C("VF", 2 * k0, 2 * k0 + 32), C("VF", 2 * k0 + 32, 2 * k0 + 64)]
-        if t >= 1:
-            ts(sm("C12"), hi, 4096.0, ALU.is_ge, -6144.0, MUL)
-            feats.append(sm("C12"))
-        if t == 1:
-            ts(sm("C12", 1), hi, 5120.0, ALU.is_ge, 1024.0, MUL)
-            feats.append(sm("C12", 1))
-        ts(C("GD", 128 * s, 128 * s + 128), C(CNT, 0, 128), CAP + 1 - 2048.0, ALU.is_lt, BIG, MUL)
+        lin(C("VF", 2 * k0, 2 * k1), C("VI", 2 * k0, 2 * k1))
+        mm(C(FAR, 0, KW * nb), rows("KZ", 0, 1, t), rows("ONH", 0, 1, slice(0, KW * nb)), True, False)
+        feats = [C("VF", 2 * k0, 2 * k0 + KW), C("VF", 2 * k0 + KW, 2 * k1)]
+        for k, (x, y) in enumerate([(4096.0, -6144.0), (5120.0, 1024.0)][:(0, 2, 1)[t]]):
+            feats.append(sm("C12", k))
+            ts(feats[-1], hi, x, ALU.is_ge, y, MUL)
+        ts(cz("GD"), cnt, CAP + 1 - 2048.0, ALU.is_lt, 32.0 if own else 32.0 * unit(0), MUL)
         for x in feats:
-            for a in range(2):
-                mm(C(FAR, 32 * a, 32 * a + 32), A("R2", ALL, a), x, False, False)
-        for a in range(2):
-            for q in range(N):
-                mm(C(FAR, 32 * a, 32 * a + 32), A("R2", ALL, 2 + 4 * a + q),
-                   C("GD", 128 * s + 32 * q, 128 * s + 32 * q + 32), False, a == 1 and q == N - 1)
-        cp(C("FL", 128 * s, 128 * s + 64), C(FAR, 0, 64))
-        gather(lambda a, b: C("G4", a, b), C("TAB", 0, TW + 6144), "FL", 128 * s, 128 * s + 64)
-        g0 = 2048 * s
-        if not last:
-            new = C("NEW", c0, c0 + 512)
-            for b, bank in enumerate((SUM, CNT)):
-                o, c = C(bank, 0, 256), c0 + 256 * b
-                mm(o, rows("KS", 0, 2, t), rows("ONB", 0, 2, slice(0, 256)), True, False)
-                mm(o, A("IB"), C("OLD", c, c + 256), False, False)
-                for a in range(2):
-                    mm(o, A("R2", ALL, 10 + a), C("G4", g0 + 512 * a + 256 * b, g0 + 512 * a + 256 * b + 256), False, a == 1)
-                lin(C("Y", c, c + 256), o, None, -127.5)
-                tt(C("NEW", c, c + 256), o, C("Y", c, c + 256), SUB)
-            to_list(C(W, 160, 192), "WB", lambda i: C("NEW", c0 + i, c0 + 512, 16))
-        else:
-            mm(A(SUM), rows("KS", 0, 2, t), rows("ONB", 0, 2), True, False)
-            for a in range(N):
-                for c in range(4):
-                    mm(C(SUM, 128 * a, 128 * a + 128), A("LO", ALL, a, slice(3 - c, 131 - c)), C("OLD", c0 + 128 * c, c0 + 128 * c + 128), False, False)
-            for a in range(N):
-                for c in range(4):
-                    o = g0 + 512 * (a & 1) + 128 * c
-                    mm(C(SUM, 128 * a, 128 * a + 128), A("LF2", ALL, a // 2, slice(3 - c, 131 - c)), C("G4", o, o + 128), False, a == N - 1 and c == 3)
-            lin(C("Y", c0, c0 + 512), A(SUM), None, -127.5)
-            for a in range(N):
-                tt(A("NEW4", ALL, s, a), C(SUM, 128 * a, 128 * a + 128), C("Y", c0 + 128 * a, c0 + 128 * a + 128), SUB)
-            exchange([(A("NEW4", ALL, s, r), [(r, A("LYB", ALL, 4 * s + me))], share[j]) for j, r in enumerate(peers)], ("ay%d" % s,) * 2,
-                     [A("LYB", ALL, 4 * s + r) for r in peers], NE)
-            for r in order:
-                dma("s", rows("yb", 32 * r, 32 * r + 32, slice(c0, c0 + 512)), A("NEW4", ALL, s, me) if r == me else A("LYB", ALL, 4 * s + r), "out")
-            wp = rows(W, 0, 32, slice(256, 384))
-            for r in order:
-                mm(wp, C("WL", 24 - 8 * r, 56 - 8 * r), A("NEW4", ALL, s, me) if r == me else A("LYB", ALL, 4 * s + r), r == me, r == order[-1])
-            wi = lambda j: rows("WI2", 0, 32, 3 * s + j)
-            df = lambda j: rows("DF2", 0, 32, 3 * s + j)
-            cp(wi(0), wp)
-            ts(wi(1), wi(0), 3, SHR, 1023, AND)
-            ts(wi(2), wi(0), 7, AND)
-            tt(df(0), wi(1), rows("FL2", 0, 32, s), SUB)
-            ts(df(1), wi(2), 0.0, EQ)
-            tt(df(2), df(0), df(1), MUL)
-            tt(rows("YNS", 0, 32, s), df(2), rows("FL2", 0, 32, 2 + s), ADD)
-            dma("a" if s else "s", C("yn", c0, c0 + 512), rows("YNS", 0, 32, s), "out")
+            for b in range(nb):
+                mm(C(FAR, KW * b, KW * b + KW), R("PX", b), x, False, False)
+        for j in range(N):
+            b = j & ~own
+            mm(C(FAR, KW * b, KW * b + KW), R("PX", j) if not own else R("PS", j // 2) if b else R("IS", j), cl("GD", j), False, j == N - 1)
+        f0 = 4 * k0
+        for x in range(0, KW * nb, 128):
+            cp(C("FL", f0 + x, f0 + min(x + 128, KW * nb)), C(FAR, x, min(x + 128, KW * nb)))
+
+        def far(b, c):
+            k = f0 + KW * b + 16 * c - k0
+            lin(C("G4", 1024 * b + 256 * c, 1024 * b + 256 * c + 256), ind(C("TAB", START[t], TW), C("FL", k, k + 16)), 3.0)
+
+        for c in range(c0 // 256, c1 // 256):
+            if t == RO - 1:
+                for b in range(nb):
+                    far(b, c)
+                continue
+            bank = ("pZ0", "pZ1", "pX0", "pX1")[c] if NS == 1 else "p%s%d" % ("ZY"[c % 2], z)
+            o, x = C(bank, 0, 256), 256 * c
+            mm(o, rows("KS", 0, 2, t), rows("ONB", 0, 2, slice(0, 256)), True, False)
+            mm(o, IB, C("OLD", x, x + 256), False, False)
+            for b in range(nb):
+                far(b, c)
+                mm(o, R("PX", b), C("G4", 1024 * b + x, 1024 * b + x + 256), False, b == nb - 1)
+            lin(C("Y", x, x + 256), o, None, -127.5)
+            tt(C("NEW", x, x + 256), o, C("Y", x, x + 256), SUB)
+        if t == RO - 1:
             return
-        cp(sm("WI"), C(W, 160, 192))
-        ts(sm("W3"), sm("WI"), 3, SHR, 1023, AND)
-        ts(sm("W3", 1), sm("WI"), 7, AND)
-        ts(sm("W3", 2), sm("WI"), 255, AND)
-        lin(A("WS", ALL, u, slice(32, 64)), sm("W3", 2))
-        tt(sm("DFC"), sm("W3"), sm("FC"), SUB)
-        ts(sm("DFC", 1), sm("W3", 1), 0.0, EQ)
-        tt(A("WS", ALL, u, slice(0, 32)), sm("DFC"), sm("DFC", 1), MUL)
-        exchange([(A("WS", ALL, u), [(r, A("LW", ALL, 4 * u + me)) for r in peers], engs)], ("aw%d" % u,) * 2,
-                 [A("LW", ALL, 4 * u + r) for r in peers], 3 * NE)
-        lin(C("TAB", NAT + 1024 * t + c0, NAT + 1024 * t + c0 + 512), new)
-        for h in range(2):
-            o = TW + 1024 * t + c0
-            dma("s", rows("TAB", 64 * h, 64 * h + 64, slice(o, o + 512)), rows("NEW", 64 - 64 * h, 128 - 64 * h, slice(c0, c0 + 512)), "rn%d" % u)
+        for i in range(8):
+            mm(C(W, 256, 256 + 2 * KW), C("WD", 7 - i, 135 - i), C("NEW", c0 + i, c1, 8), i == 0, i == 7)
         st = (2, 4)[t]
-        o = ORG + (4096, 6144)[t] + st * c0
-        lin(C("TAB", o, o + 512 * st, st), new)
+        for x in range(c0, c1, 512):
+            o = ORA + (4096, 6144)[t] + st * x
+            lin(C("TAB", o, o + 512 * st, st), C("NEW", x, x + 512))
+
+    def spread(t):
+        stream[0] = None
+        o = 1024 * t - 2048
+        n = 1024 // TUNE["nat"]
+        for x in range(0, 1024, n):
+            for j in held(RO - 1):
+                if j == 0 and TUNE["own"]:
+                    for y in range(x, x + n, 512):
+                        lin(C("TAB", ORA + o + y, ORA + o + y + 512), C("NEW", y, y + 512))
+                else:
+                    widen(lambda a, b: rows("NEW", a, b, slice(x, x + n)), j, ORG[j] + o + x, ORG[j] + o + x + n, "rn%d" % t)
+
+    def finish(t):
+        stream[0] = None
+        W, nb, banks = "pW0", N // HELD[t], ("pZ0", "pZ1", "pX0", "pX1")
+        homes = peers + [me]
+        for a, bank in zip(homes, banks):
+            mm(C(bank, 0, 256), rows("KS", 0, 2, t), rows("ONB", 0, 2, slice(0, 256)), True, False)
+            for c in range(4):
+                mm(C(bank, 0, 256), R("LO", a, 3 - c, 131 - c), C("OLD", 256 * c, 256 * c + 256), False, False)
+        ly = lambda r: C("LY", 128 * r, 128 * r + 128)
+        for j, (a, bank) in enumerate(zip(homes, banks)):
+            o, x = C(bank, 0, 256), 256 * a
+            for c in range(4):
+                for b in range(nb):
+                    mm(o, R("LO", a ^ b, 3 - c, 131 - c), C("G4", 1024 * b + 256 * c, 1024 * b + 256 * c + 256), False, c == 3 and b == nb - 1)
+            lin(C("Y", x, x + 256), o, None, -127.5)
+            if a == me:
+                tt(C("NH", x, x + 256), o, C("Y", x, x + 256), SUB)
+                continue
+            tt(C("NEW", x, x + 256), o, C("Y", x, x + 256), SUB)
+            mm(C(bank, 256, 384), IB, C("NEW", x, x + 256, 2), True, False)
+            mm(C(bank, 256, 384), I256, C("NEW", x + 1, x + 256, 2), False, True)
+            cp(C("PY", 128 * a, 128 * a + 128), C(bank, 256, 384))
+            send(j, C("PY", 128 * a, 128 * a + 128), ly, "ay")
+        for r, bank in zip([me] + peers[::-1], (None,) + banks):
+            x = 256 * r
+            if r != me:
+                split(C("NH", x, x + 256, 2), C("NH", x + 1, x + 256, 2), ly(r), C("HY", 128 * r, 128 * r + 128),
+                      C("XY", 128 * r, 128 * r + 128), C(bank, 0, 128))
+            dma("s", rows("yb", 32 * r, 32 * r + 32), C("NH", x, x + 256), "out")
+            for q in range(4):
+                mm(rows(W, 32 * r, 32 * r + 32, slice(0, 64)), R("WL", 0, 3 - q, 35 - q), C("NH", x + 64 * q, x + 64 * q + 64), q == 0, q == 3)
+        cp(R("WI2", 0), C(W, 0, 64))
+        root_number(R("WI2", 1), R("WI2", 2), R("DF2", 0), R("DF2", 1), R("DF2", 2), R("WI2", 0), R("FL2", 0))
+        tt(A("YNS"), R("DF2", 2), R("FL2", 1), ADD)
+        dma("a", A("yn"), A("YNS"), "out")
 
     for t in range(RO):
-        home(t, 0)
-        home(t, 1)
-        owner(t, 0)
-        late = []
-        if t < RO - 1:
-            late = ops[-4:]
-            del ops[-4:]
-        owner(t, 1)
-        ops.extend(late)
+        for z in range(NS):
+            keys(t, z)
+            level(t, 0, z)
+        stream[0] = None
+        if t == 0:
+            unstack()
+        for j in held(t):
+            if j and (t == 0 or j not in held(t - 1)):
+                widen(lambda x, y: rows("TAB", x, y, slice(ORA, ORA + 4096)), j, ORG[j], ORG[j] + 4096, "tb%d" % j)
+        for z in range(NS):
+            level(t, 1, z)
+        stream[0] = None
+        if t == RO - 1:
+            send_inner()
+        for z in range(NS):
+            blocks(t, z)
+        (spread if t < RO - 1 else finish)(t)
 
     def meet(x, y):
         return x[1] < y[2] and y[1] < x[2] and x[3] < y[4] and y[3] < x[4]
@@ -539,7 +646,7 @@ def rank_program(g, core, T, topo):
         if o["n"]:
             group.setdefault(o["sem"], []).append(n)
     for n, o in enumerate(ops):
-        pre = set()
+        pre = set(o["hold"])
         for mine, w in [(r, False) for r in o["rd"]] + [(r, True) for r in o["wr"]]:
             ps = mine[0] in PSUM
             keep = []
@@ -554,46 +661,104 @@ def rank_program(g, core, T, topo):
         o["pre"] = pre
         o["dep"] = pre | ({o["after"]} if o["after"] is not None else set())
         o["post"] = []
+        o["due"] = TUNE["yi"] if o["wr"] and o["wr"][0][0] == "yi" else 0.0
     for n, o in enumerate(ops):
         for m in o["dep"]:
             ops[m]["post"].append(n)
     for n in range(n_ops - 1, -1, -1):
         o = ops[n]
         own = min(o["cost"].values()) + (o["lat"] + RLAT if o["sem"] and o["e"] != "x" else 0.0)
-        o["rank"] = own + max([ops[m]["rank"] + HOP for m in o["post"]] + [0.0])
-        o["prio"] = o["rank"] + TUNE["bias"] * (o["half"] == 0)
-    free = {e: 0.0 for e in "vatgsx"}
-    lanes = [0.0]
-    left = [len(o["dep"]) for o in ops]
-    ready = [n for n in range(n_ops) if not left[n]]
-    for n in ready:
-        ops[n]["at"] = 0.0
-    seq = []
-    while ready:
-        cand = []
-        for n in ready:
+        o["rank"] = own + max([ops[m]["rank"] + HOP * (o["e"] != "t" or ops[m]["e"] != "t") for m in o["post"]] + [o["due"]])
+    can = [list(o["cost"]) if o["e"] == "*" else [o["e"]] for o in ops]
+    tight = [{m: (ops[m]["after"] == n and ops[m]["e"] != "x" and n not in ops[m]["pre"]) or o["e"] == ops[m]["e"] == "t"
+              for m in o["post"]} for n, o in enumerate(ops)]
+    hop = [0.0 if o["e"] == "x" else HOP for o in ops]
+
+    def play(eng, queues):
+        eng = list(eng)
+        free = {e: 0.0 for e in "vatgsx"}
+        lanes = [0.0, TUNE["first"]]
+        left = [len(o["dep"]) for o in ops]
+        at, tail, seq = [0.0] * n_ops, [0.0] * n_ops, []
+        ready = {n for n in range(n_ops) if not left[n]}
+        head = {e: 0 for e in "vatgsx"}
+        while ready:
+            if queues:
+                cand = [(max(free[e], at[q[head[e]]]), e, q[head[e]]) for e, q in queues.items() if head[e] < len(q) and q[head[e]] in ready]
+                t1, e, n = min(cand)
+                head[e] += 1
+            else:
+                cand = []
+                for n in ready:
+                    e = min(can[n], key=lambda x: max(free[x], at[n]) + ops[n]["cost"][x] * (1.0 + TUNE["pen"] * (x == "v")))
+                    cand.append((max(free[e], at[n]), e, n))
+                t0, e0, _ = min(cand)
+                t1, e, n = max([c for c in cand if c[1] == e0 and c[0] <= t0 + TUNE["win"]], key=lambda c: (ops[c[2]]["rank"] + ops[c[2]]["lead"], -c[2]))
             o = ops[n]
-            e = min(o["cost"] if o["e"] == "*" else [o["e"]],
-                    key=lambda x: max(free[x], o["at"]) + o["cost"][x] * (1.0 + o["pen"] * (x == "v")))
-            cand.append((max(free[e], o["at"]), e, n))
-        t0, e0, _ = min(cand)
-        t1, e, n = max([c for c in cand if c[1] == e0 and c[0] <= t0 + TUNE["win"]], key=lambda c: (ops[c[2]]["prio"], -c[2]))
-        o = ops[n]
-        o["e"] = e
-        free[e] = end = t1 + o["cost"][e]
-        issue = end
-        if o["sem"] and e != "x":
-            lanes[0] = max(end + (0.6 if o["sem"] == "remote" else 1.0), lanes[0]) + o["lat"]
-            end = lanes[0] + 1.0 + (TUNE["ext"] if o["sem"] == "remote" else 0.0)
-        ready.remove(n)
-        seq.append(n)
-        for m in o["post"]:
-            q = ops[m]
-            link = issue if (q["after"] == n and q["e"] != "x" and n not in q["pre"]) else end + (0.0 if e == "t" and q["e"] == "t" or q["e"] == "x" else HOP)
-            q["at"] = max(q.get("at", 0.0), link)
-            left[m] -= 1
-            if not left[m]:
-                ready.append(m)
+            eng[n] = e
+            at[n] = t1
+            issue = end = t1 + o["cost"][e]
+            free[e] = issue if e != "x" else 0.0
+            if o["sem"] and e != "x":
+                far = o["sem"] == "remote"
+                lanes[0] = max(end + (TUNE["rs"] + lanes[1] if far else 1.0), lanes[0]) + o["lat"]
+                lanes[1] *= not far
+                end = lanes[0] + 0.5 + (TUNE["ext"] if far else 0.0)
+            elif e == "t":
+                end += 0.06
+            tail[n] = end - issue
+            ready.remove(n)
+            seq.append(n)
+            for m in o["post"]:
+                at[m] = max(at[m], issue if tight[n][m] else end + hop[m])
+                left[m] -= 1
+                if not left[m]:
+                    ready.add(m)
+        return max(at[n] + ops[n]["cost"][eng[n]] + tail[n] for n in seq), seq, eng, at, tail
+
+    def pack(order, tail, back):
+        busy = {e: ([], []) for e in "vatgs"}
+        at, eng = [0.0] * n_ops, [None] * n_ops
+        for n in order:
+            o = ops[n]
+            if back:
+                t = max([at[m] + ops[m]["cost"][eng[m]] + (0.0 if tight[n][m] else tail[n] + hop[m]) for m in o["post"]] + [tail[n] + o["due"]])
+            else:
+                t = max([at[m] + ops[m]["cost"][eng[m]] + (0.0 if tight[m][n] else tail[m] + hop[n]) for m in o["dep"]] + [0.0])
+            best = None
+            for e in can[n]:
+                c, t1, k = o["cost"][e], t, 0
+                if e != "x":
+                    lo, hi = busy[e]
+                    a, b = 0, len(hi)
+                    while a < b:
+                        mid = (a + b) // 2
+                        a, b = (mid + 1, b) if hi[mid] <= t1 else (a, mid)
+                    k = a
+                    while k < len(lo) and lo[k] < t1 + c:
+                        t1 = hi[k]
+                        k += 1
+                key = t1 + c * (1.0 + TUNE["pen2"] * (e == "v"))
+                if best is None or key < best[0]:
+                    best = (key, t1, e, k)
+            _, at[n], eng[n], k = best
+            if eng[n] != "x":
+                busy[eng[n]][0].insert(k, at[n])
+                busy[eng[n]][1].insert(k, at[n] + o["cost"][eng[n]])
+        return at, eng
+
+    best = now = play([None] * n_ops, None)
+    for _ in range(TUNE["passes"]):
+        _, seq, eng, at, tail = now
+        pos = {n: k for k, n in enumerate(seq)}
+        at, eng = pack(sorted(seq, key=lambda n: (-at[n], -pos[n])), tail, True)
+        at, eng = pack(sorted(seq, key=lambda n: (-at[n] - ops[n]["cost"][eng[n]], pos[n])), tail, False)
+        seq = sorted(seq, key=lambda n: (at[n], pos[n]))
+        now = play(eng, {e: [n for n in seq if eng[n] == e] for e in "vatgsx"})
+        best = min(best, now, key=lambda x: x[0])
+    seq = best[1]
+    for n, o in enumerate(ops):
+        o["e"] = best[2][n]
     esem = {"v": "ev", "a": "ea", "t": "et", "g": "eg"}
     total = {k: sum(ops[m]["n"] for m in v) for k, v in group.items()}
     pos = {n: k for k, n in enumerate(seq)}

@@ -35,7 +35,7 @@ SCRATCH = {
     "PI": _s(i32, 16), "PF": _s(f32, 16), "DF": _s(f32, 64), "J": _s(b16, 160), "J8": _s(b16, 144), "J15": _s(b16, 128),
     "JG": _s(b16, 128), "JX": _s(b16, 4, 128), "CF": _s(f16, 1024), "ONH": _s(f16, 512),
     "ONB": _s(b16, 512), "FCI": _s(i32, 256), "FC16": _s(f16, 64), "CQI": _s(i32, 16),
-    "WB": _s(b16, 144), "WD": _s(b16, 144), "GB": _s(f16, 144), "XP": _s(f16, 2, 144), "UU": _s(f16, 128),
+    "WB": _s(b16, 144), "WD": _s(b16, 4, 144), "K256": _s(b16, 128), "GB": _s(f16, 144), "XP": _s(f16, 2, 144), "UU": _s(f16, 128),
     "QT": _s(f16, 2, 128), "QB": _s(f16, 128), "QA": _s(f16, 8, 128), "CC": _s(f16, 144), "SQ": _s(f32, 2, 128),
     "KB": _s(f16, 128), "KZ": _s(f16, 3, 128), "KA": _s(f16, 4, 128), "OG": _s(b16, 128), "T2": _s(b16, 4, 128), "SM": _s(b16, 256),
     "IB": _s(b16, 2, 128), "IH": _s(f16, 3, 128),
@@ -52,9 +52,10 @@ SIZE.update({"rtab": 4, "itab": 4, "btab": 2, "rn0": 4, "x0": 4, "yb": 2, "yi": 
 PSUM = [k for k, v in SCRATCH.items() if v[0] == "psum"]
 SEMAPHORES = (["ev", "ea", "et", "eg", "sent", "out", "lrx", "ta", "tb1", "tb2", "tb3", "rn0", "rn1"]
               + [x + "%d" % q for x in ("lb", "li", "lr", "le", "ap", "ah", "ar", "ae", "ay") for q in range(N)])
-CYC, GAT, PEC, HOP, FIX, BW, ROW, RIS, RLAT = 0.83e-3, 1.56, 0.42e-3, 0.15, 0.03, 350e3, 0.03, 0.5, 1.6
-TUNE = {"pen": 0.0, "win": 0.06, "ext": 0.1, "h1": 0, "h2": 2, "h3": 4, "h4": 6, "rs": 0.8, "first": 2.8,
-        "yi": 0.0, "pen2": 0.2, "passes": 4, "own": 1, "bias": 0.0, "nat": 1}
+CYC, GAT, PEC, HOP, FIX, BW, ROW, RIS, RLAT = 0.83e-3, 1.56, 0.42e-3, 0.19, 0.005, 400e3, 0.02, 0.4, 1.4
+LOADS, ARRIVE, SET, UNP = "i0 i1 b0 b1 b2i0 i2i1 i3b1 b3i2", "i0 i1 i2 i3", "i3", ("pW0", "pW1", "pW0")
+TUNE = {"pen": 0.3, "win": 0.06, "ext": 0.0, "late": 1, "ai": 1, "wy": 1, "rs": 0.8, "first": 1.8,
+        "yi": 2.0, "pen2": 0.6, "passes": 3, "own": 1, "bias": 2.0, "pe": 0.0, "nat": 1}
 
 
 def rank_program(g, core, T, topo):
@@ -63,7 +64,7 @@ def rank_program(g, core, T, topo):
         return
     Q = {"v": g.vector, "a": g.scalar, "t": g.tensor, "g": g, "s": g.sync}
     ops = []
-    stream = [None]
+    stream, late = [None], []
     ALL = slice(None)
 
     def A(name, *idx):
@@ -138,6 +139,9 @@ def rank_program(g, core, T, topo):
     def cp(o, i):
         return lin(o, i, e="v")
 
+    def whole(o, i, scale=None, bias=None):
+        return lin(o, i, scale, bias, "*" if TUNE["ai"] else "v")
+
     def act(o, i, func, scale, bias):
         return add("a", lambda q: g.scalar.activation(o[0], i[0], func, bias=val(bias), scale=val(scale)), regs(i, scale, bias), o[1],
                    {"a": ta(i)})
@@ -208,15 +212,10 @@ def rank_program(g, core, T, topo):
 
     EQ, MUL, ADD, SUB, AND, SHR = ALU.is_equal, ALU.mult, ALU.add, ALU.subtract, ALU.bitwise_and, ALU.logical_shift_right
 
-    def load_inner(o, hold=()):
-        dma("s", C("SI", 1024 + 768 * o, 1792 + 768 * o), rows("itab", 32 * o, 32 * o + 32), "li%d" % o, True, hold)
-
     dma("s", C("rx", 0, 64), A("rn0"), "lrx", True)
     dma("s", C("rx", 64, 128), A("x0"), "lrx", True)
     for o in peers + [me]:
         dma("s", C("SI", 256 * o, 256 * o + 256), rows("rtab", 32 * o, 32 * o + 32), "lr%d" % o, True)
-    for j, o in enumerate(peers):
-        dma("s", R("SB", j), rows("btab", 32 * o, 32 * o + 32), "lb%d" % j, True)
 
     iota(col("PI", 9), [[0, 1]], 0, 1)
     iota(A("J"), [[1, 160]], 0, 0, True)
@@ -292,7 +291,14 @@ def rank_program(g, core, T, topo):
     for a in range(N):
         lin(rows("DF", 32 * a, 32 * a + 32, slice(CQ, CQ + 4)), rows("CQI", 32 * a, 32 * a + 32, slice(4 * a, 4 * a + 4)))
     ts(A("WB"), C("J", 0, 144), dTW, EQ, dWT, MUL)
-    ts(A("WD"), A("J8"), dTD, EQ, dWT, MUL)
+    ts(R("WD", 0), A("J8"), dTD, EQ, dWT, MUL)
+    ms(rows("K256", 0, 32), 256.0)
+    for b in range(1, N // min(HELD[:-1])):
+        ts(col("PI", 11), p, 32 * b, AND)
+        cp(col("DF", 44), col("PI", 11))
+        lin(col("DF", 45), col("DF", 44), -2.0, dTD)
+        lin(col("DF", 46), col("DF", 45), None, 32.0 * b)
+        ts(R("WD", b), A("J8"), col("DF", 46), EQ, dWT, MUL)
     ts(dTX, pg, p8, ADD)
     lin(dTY, pv16, 1.0 / 16)
     ts(C("DF", MF, MF + 2), C("J", 0, 2), pb, EQ, dTY, MUL)
@@ -347,7 +353,6 @@ def rank_program(g, core, T, topo):
         lin(R("SR", o, 256, 288), C("pW0", 32 * o, 32 * o + 32))
         if o != me:
             send(j, R("SR", o), lambda r: R("LR", r), "ar")
-    load_inner(peers[0])
     lx = lambda a, x, y: R("SR" if a == me else "LR", a, x, y)
     uu = lambda c: C("UU", 32 * c, 32 * c + 32)
     for a in [me] + peers[::-1]:
@@ -363,27 +368,28 @@ def rank_program(g, core, T, topo):
         for v in range(2):
             mm(C("pW1", 256 + h, 384, 2), R("XP", h, 16 - 16 * v, 144 - 16 * v), C("XT", 64 * v, 64 * v + 64), v == 0, v == 1)
     cp(A("WI"), C("pW1", 256, 384))
-    packed = []
-    for j, o in enumerate(peers):
-        bank = ("pX0", "pY0", "pX1")[j]
-        mm(A(bank), IB, R("SB", j, 0, 512), True, False)
-        mm(A(bank), I256, R("SB", j, 512, 1024), False, True)
-        packed.append(cp(R("PK", j), A(bank)))
-        send(j, R("PK", j), lambda r: R("LP", r), "ap")
-    load_inner(peers[1], packed[TUNE["h1"]:][:1])
-    load_inner(peers[2], packed[TUNE["h2"]:][:1])
-    conv = []
-    for j, o in enumerate(peers + [me]):
-        if o == me:
-            load_inner(me, (packed + conv)[TUNE["h3"]:][:1])
-            dma("s", rows("TAB", 32 * me, 32 * me + 32, slice(ORA, ORA + 4096)), rows("btab", 32 * me, 32 * me + 32), "ta", True)
-        for x in range(768 * o, 768 * o + 768, 384):
-            conv.append(lin(C("SH", x, x + 384), C("SI", 1024 + x, 1408 + x), 1.0 / 2048, -1.0))
-        if o != me:
-            send(j, C("SH", 768 * o, 768 * o + 768), lambda r: C("LH", 768 * r, 768 * r + 768), "ah")
+    done = {}
+    for step in LOADS.split():
+        j, hold = int(step[1]), [done[step[2:]]] if step[2:] else []
+        o = (peers + [me])[j]
+        if step[0] == "i":
+            dma("s", C("SI", 1024 + 768 * o, 1792 + 768 * o), rows("itab", 32 * o, 32 * o + 32), "li%d" % o, True, hold)
+            for x in range(768 * o, 768 * o + 768, 384):
+                done[step[:2]] = lin(C("SH", x, x + 384), C("SI", 1024 + x, 1408 + x), 1.0 / 2048, -1.0)
+            if o != me:
+                send(j, C("SH", 768 * o, 768 * o + 768), lambda r: C("LH", 768 * r, 768 * r + 768), "ah")
+        elif o == me:
+            dma("s", rows("TAB", 32 * me, 32 * me + 32, slice(ORA, ORA + 4096)), rows("btab", 32 * me, 32 * me + 32), "ta", True, hold)
+        else:
+            bank = ("pX0", "pW0", "pX1")[j]
+            dma("s", R("SB", j), rows("btab", 32 * o, 32 * o + 32), "lb%d" % j, True, hold)
+            mm(A(bank), IB, R("SB", j, 0, 512), True, False)
+            mm(A(bank), I256, R("SB", j, 512, 1024), False, True)
+            done[step[:2]] = whole(R("PK", j), A(bank))
+            send(j, R("PK", j), lambda r: R("LP", r), "ap")
 
     def split(lo, hi, x, hx, xx, ps):
-        lin(hx, x, 1.0 / 256, HB - 0.498, e="v")
+        lin(hx, x, 1.0 / 256, HB - 0.498)
         lin(xx, x, None, 256.0 * HB)
         mm(ps, IM, hx, True, True)
         tt(lo, xx, ps, ADD)
@@ -392,9 +398,9 @@ def rank_program(g, core, T, topo):
     def unstack():
         for j, q in enumerate(peers[::-1]):
             split(R("SB", j, 0, 512), R("SB", j, 512, 1024), R("LP", q), C("G4", 512 * j, 512 * j + 512),
-                  R("RT", 1, 512 * j, 512 * j + 512) if j < 2 else C("IC", 0, 512), A(("pZ0", "pZ1", "pY1")[j]))
-        inner = ["pY0", "pY1", "pX0", "pX1", "pZ0", "pZ1"]
-        for a in peers[::-1][:2] + [me] + peers[:1]:
+                  R("RT", 1, 512 * j, 512 * j + 512) if j < 2 else C("IC", 0, 512), A(UNP[j]))
+        inner = ["pY0", "pY1", "pZ0", "pZ1", "pX0", "pX1"]
+        for a in [me if x[1] == "3" else peers[2 - int(x[1])] for x in ARRIVE.split()]:
             for c in range(4):
                 x = 768 * c
                 while x < 768 * c + 768:
@@ -406,7 +412,7 @@ def rank_program(g, core, T, topo):
         for k in range(6):
             lin(C("IT", 512 * k, 512 * k + 512), A(inner[k]))
         for j, q in enumerate(peers[::-1]):
-            dma("s", rows("TAB", 32 * q, 32 * q + 32, slice(ORA, ORA + 4096)), R("SB", j), "ta", True, conv[TUNE["h4"]:][:1])
+            dma("s", rows("TAB", 32 * q, 32 * q + 32, slice(ORA, ORA + 4096)), R("SB", j), "ta", True, [done[SET]])
 
     def widen(src, j, a, b, sem):
         n = 128 if j == 0 else 64 if j == 2 else 32
@@ -455,10 +461,14 @@ def rank_program(g, core, T, topo):
         for h in range(2):
             mm(o, C("CC", 8 - 8 * h, 136 - 8 * h), R("FT", lvl, 2 * k0 + h, 2 * k1, 2), h == 0, False)
         to_list(o, "GB", lambda i: R("SEL", lvl, 16 * k0 + i, 16 * k1, 16), False)
-        ts(C(("IL", "OL")[lvl], k0, k1), o, 6741.0, ADD, 2048.0, MUL)
+        whole(C(("IL", "OL")[lvl], k0, k1), o, 2048.0, 6741.0 * 2048)
+        n0 = len(ops)
         for s in hs if lvl or t < RO - 1 else ():
             plane(bank(s), s, lvl, t + lvl, 1 + (t == RO - 1))
             tt(app(512 * s, 512 * s + 512), got(512 * s, 512 * s + 512), A(bank(s)), ALU.max)
+        if t == lvl == 0 and TUNE["late"]:
+            late.extend(ops[n0:])
+            del ops[n0:]
 
     def root_number(z, num, m, d, prod, w, f):
         ts(z, w, 7, AND)
@@ -473,12 +483,12 @@ def rank_program(g, core, T, topo):
         d = lambda name, j: R(name, j, 2 * k0, 2 * k1)
         wi = C("WI", 2 * k0, 2 * k1)
         if t:
-            cp(wi, C(W, 256, 256 + 2 * KW))
+            whole(wi, C(W, 256, 256 + 2 * KW))
             root_number(d("W3", 0), d("W3", 1), d("DM", 0), d("DM", 1), d("DM", 2), wi, C("FD", 2 * k0, 2 * k1))
             mm(C(W, 0, KW), IH, C("FC16", k0, k1), True, False)
             for h in range(2):
                 mm(C(W, 0, KW), R("IH", h), R("DM", 2, 2 * k0 + h, 2 * k1, 2), False, h == 1)
-            cp(C("CUR", k0, k1), C(W, 0, KW))
+            whole(C("CUR", k0, k1), C(W, 0, KW))
         for lvl in range(2):
             ts(d("D", lvl), wi, 4 * lvl, SHR, 15, AND)
             act(d("FT", lvl), d("D", lvl), ACT.Square, 1.0, pb)
@@ -510,7 +520,7 @@ def rank_program(g, core, T, topo):
         cz = lambda name: C(name, 4 * CW * z, 4 * CW * z + 4 * CW)
         gather(lambda a, b: C("OLD", a, b), C("TAB", ORA, ORA + (4096, 6144, 10240)[t]), "OL", z)
         to_list(C(W, 192, 192 + KW), "WB", lambda i: C("OLD", c0 + i, c1, 16))
-        cp(sm("HI"), C(W, 192, 192 + KW))
+        whole(sm("HI"), C(W, 192, 192 + KW))
         ts(sm("Q0"), sm("HI"), 3, AND)
         if z:
             lin(C("O", 4 * CW, 8 * CW, CW), C("SC", KW, 4 * CW, CW))
@@ -558,12 +568,17 @@ def rank_program(g, core, T, topo):
             for b in range(nb):
                 far(b, c)
                 mm(o, R("PX", b), C("G4", 1024 * b + x, 1024 * b + x + 256), False, b == nb - 1)
-            lin(C("Y", x, x + 256), o, None, -127.5)
-            tt(C("NEW", x, x + 256), o, C("Y", x, x + 256), SUB)
+            lin(C("Y", x, x + 256), o, -1.0, 127.5)
+            tt(C("NEW", x, x + 256), o, C("Y", x, x + 256), ADD)
         if t == RO - 1:
             return
-        for i in range(8):
-            mm(C(W, 256, 256 + 2 * KW), C("WD", 7 - i, 135 - i), C("NEW", c0 + i, c1, 8), i == 0, i == 7)
+        o = C(W, 256, 256 + 2 * KW)
+        terms = [(0, "OLD", 0)] + [(b, "G4", 1024 * b) for b in range(nb)] + [(0, "Y", 0)] if TUNE["wy"] else [(0, "NEW", 0)]
+        if TUNE["wy"]:
+            mm(o, rows("KS", 0, 2, t), rows("K256", 0, 2, slice(0, 2 * KW)), True, False)
+        for b, name, x in terms:
+            for i in range(8):
+                mm(o, R("WD", b, 7 - i, 135 - i), C(name, x + c0 + i, x + c1, 8), i == 0 and name == "NEW", i == 7 and name in ("Y", "NEW"))
         st = (2, 4)[t]
         for x in range(c0, c1, 512):
             o = ORA + (4096, 6144)[t] + st * x
@@ -602,7 +617,7 @@ def rank_program(g, core, T, topo):
             tt(C("NEW", x, x + 256), o, C("Y", x, x + 256), SUB)
             mm(C(bank, 256, 384), IB, C("NEW", x, x + 256, 2), True, False)
             mm(C(bank, 256, 384), I256, C("NEW", x + 1, x + 256, 2), False, True)
-            cp(C("PY", 128 * a, 128 * a + 128), C(bank, 256, 384))
+            whole(C("PY", 128 * a, 128 * a + 128), C(bank, 256, 384))
             send(j, C("PY", 128 * a, 128 * a + 128), ly, "ay")
         for r, bank in zip([me] + peers[::-1], (None,) + banks):
             x = 256 * r
@@ -624,6 +639,7 @@ def rank_program(g, core, T, topo):
         stream[0] = None
         if t == 0:
             unstack()
+            ops.extend(late)
         for j in held(t):
             if j and (t == 0 or j not in held(t - 1)):
                 widen(lambda x, y: rows("TAB", x, y, slice(ORA, ORA + 4096)), j, ORG[j], ORG[j] + 4096, "tb%d" % j)
@@ -701,11 +717,11 @@ def rank_program(g, core, T, topo):
             free[e] = issue if e != "x" else 0.0
             if o["sem"] and e != "x":
                 far = o["sem"] == "remote"
-                lanes[0] = max(end + (TUNE["rs"] + lanes[1] if far else 1.0), lanes[0]) + o["lat"]
+                lanes[0] = max(end + (TUNE["rs"] + lanes[1] if far else TUNE["rs"]), lanes[0]) + o["lat"]
                 lanes[1] *= not far
                 end = lanes[0] + 0.5 + (TUNE["ext"] if far else 0.0)
             elif e == "t":
-                end += 0.06
+                end += TUNE["pe"]
             tail[n] = end - issue
             ready.remove(n)
             seq.append(n)

@@ -22,24 +22,25 @@ SCRATCH = {
     "rx": _s(i32, 128), "RX": _s(f16, 128), "XT": _s(f16, 128), "SR": _s(f16, 4, 288), "LR": _s(f16, 4, 288),
     "SI": _s(i32, 4096), "SH": _s(f16, 3072), "LH": _s(f16, 4096), "SB": _s(b16, 3, 1024), "PK": _s(u16, 3, 512),
     "LP": _s(u16, 4, 512),
-    "IT": _s(f32, 6144), "RT": _s(f32, 3, 1024), "IC": _s(f32, 1024), "SEL": _s(f16, 2, 1024),
-    "E0": _s(f16, 1024), "LE": _s(f16, 1024), "YI": _s(f32, 1024),
-    "TAB": _s(b16, TW + 6144), "OLD": _s(b16, 1024), "IS": _s(f16, 4, 128), "PX": _s(f16, 4, 128), "PS": _s(f16, 2, 128),
+    "IT": _s(f32, 6144), "RT": _s(f32, 3, 1024), "IC": _s(f32, 512), "GOT": _s(f16, 2, 1024), "APP": _s(f16, 2, 1024),
+    "AL": _s(f16, 4, 128), "F8": _s(f16, 64), "LE": _s(f16, 1024), "YI": _s(f32, 1024),
+    "TAB": _s(b16, TW + 6144), "OLD": _s(b16, 1024), "IS": _s(f16, 4, 128), "PW": _s(f16, 256), "PS": _s(f16, 4, 128),
     "G4": _s(f16, 4096), "Y": _s(b16, 1024), "NEW": _s(b16, 1024), "PY": _s(u16, 512), "LY": _s(u16, 512),
     "HY": _s(f16, 512), "XY": _s(f32, 512), "NH": _s(b16, 1024),
     "CUR": _s(u16, 64), "IL": _s(u16, 64), "OL": _s(u16, 64), "FL": _s(u16, 256),
     "YNS": _s(f32, 64), "WI2": _s(i32, 3, 64), "DF2": _s(f32, 3, 64), "FL2": _s(f32, 2, 64),
     "WI": _s(i32, 128), "W3": _s(i32, 2, 128), "DM": _s(f16, 3, 128), "FD": _s(f32, 128), "D": _s(i32, 2, 128), "FT": _s(f16, 2, 128),
-    "HI": _s(i32, 64), "Q0": _s(i32, 64), "O": _s(b16, 264), "SC": _s(b16, 264), "VI": _s(i32, 128), "VF": _s(b16, 128),
+    "HI": _s(i32, 64), "RR": _s(f32, 5, 64), "SC": _s(b16, 272), "VI": _s(i32, 128), "VF": _s(b16, 128),
     "C12": _s(b16, 128), "GD": _s(f16, 264),
     "PI": _s(i32, 16), "PF": _s(f32, 16), "DF": _s(f32, 64), "J": _s(b16, 160), "J8": _s(b16, 144), "J15": _s(b16, 128),
-    "JG": _s(b16, 128), "JX": _s(b16, 4, 128), "CF": _s(f16, 1024), "ONH": _s(f16, 512),
-    "ONB": _s(b16, 512), "FCI": _s(i32, 256), "FC16": _s(f16, 64), "CQI": _s(i32, 16),
-    "WB": _s(b16, 144), "WD": _s(b16, 4, 144), "K256": _s(b16, 128), "GB": _s(f16, 144), "XP": _s(f16, 2, 144), "UU": _s(f16, 128),
-    "QT": _s(f16, 2, 128), "QB": _s(f16, 128), "QA": _s(f16, 8, 128), "CC": _s(f16, 144), "SQ": _s(f32, 2, 128),
-    "KB": _s(f16, 128), "KZ": _s(f16, 3, 128), "KA": _s(f16, 4, 128), "OG": _s(b16, 128), "T2": _s(b16, 4, 128), "SM": _s(b16, 256),
+    "JG": _s(b16, 128), "JU": _s(b16, 128), "CF": _s(f16, 1024), "ONH": _s(f16, 512),
+    "ONB": _s(b16, 512), "FCI": _s(i32, 264), "FC16": _s(f16, 64),
+    "WB": _s(b16, 144), "WD": _s(b16, 4, 144), "K256": _s(b16, 128), "GB": _s(f16, 2, 144), "XP": _s(f16, 2, 144), "UU": _s(f16, 128),
+    "QT": _s(f16, 2, 128), "QB": _s(f16, 128), "QA": _s(f16, 8, 128), "SQ": _s(f32, 2, 128),
+    "KZ": _s(f16, 3, 128), "KA": _s(f16, 4, 128), "OG": _s(f16, 128), "T2": _s(f16, 5, 128),
     "IB": _s(b16, 2, 128), "IH": _s(f16, 3, 128),
-    "KS": _s(b16, 3, 128), "DI": _s(f16, 4, 128), "LO": _s(b16, 5, 144), "WL": _s(b16, 2, 160),
+    "KS": _s(b16, 3, 128), "DI": _s(f16, 4, 128), "LO": _s(b16, 5, 144), "WL": _s(b16, 2, 36),
+    "WF": _s(f32, 36), "KX": _s(b16, 128), "KY": _s(b16, 32),
 }
 for _k in "XYZW":
     for _h in "01":
@@ -50,12 +51,14 @@ SHAPES.update({"rtab": [128, 1024], "itab": [128, 3072], "btab": [128, 4096], "r
 SIZE = {k: (4 if v[2] in (i32, f32) else 2) for k, v in SCRATCH.items()}
 SIZE.update({"rtab": 4, "itab": 4, "btab": 2, "rn0": 4, "x0": 4, "yb": 2, "yi": 4, "yn": 4})
 PSUM = [k for k, v in SCRATCH.items() if v[0] == "psum"]
-SEMAPHORES = (["ev", "ea", "et", "eg", "sent", "out", "lrx", "ta", "tb1", "tb2", "tb3", "rn0", "rn1"]
+SEMAPHORES = (["ev", "ea", "et", "eg", "sent", "out", "lrx", "tr", "ta", "tb1", "tb2", "tb3", "rn0", "rn1"]
               + [x + "%d" % q for x in ("lb", "li", "lr", "le", "ap", "ah", "ar", "ae", "ay") for q in range(N)])
 CYC, GAT, PEC, HOP, FIX, BW, ROW, RIS, RLAT = 0.83e-3, 1.56, 0.42e-3, 0.19, 0.005, 400e3, 0.02, 0.4, 1.4
-LOADS, ARRIVE, SET, UNP = "i0 i1 b0 b1 b2i0 i2i1 i3b1 b3i2", "i0 i1 i2 i3", "i3", ("pW0", "pW1", "pW0")
-TUNE = {"pen": 0.3, "win": 0.06, "ext": 0.0, "late": 1, "ai": 1, "wy": 1, "rs": 0.8, "first": 1.8,
-        "yi": 2.0, "pen2": 0.6, "passes": 3, "own": 1, "bias": 2.0, "pe": 0.0, "nat": 1}
+LOADS, ARRIVE, SET, BANKS = "i0 i1 b0 b1 b2i1 i2b0 i3b1 b3i2", "i0 i1 i3 i2", "i3", "X0 X1 W0 W1 W0 W1 Y0 Y1 Z0 Z1 X0 X1"
+STRIDE = (0.5, 1.0, 2.0, 4.0)
+SLOWS = (0.9, 1.0, 1.15, 1.3)
+TUNE = {"pen": 0.3, "win": 0.06, "ext": 0.0, "cut": 16, "dec": 0, "soon": 4.0, "mix": 0.4, "slow": 1.8, "joint": 1, "rc": 1, "sig": 0, "shake": 0.0, "twice": 1, "ai": 1, "wy": 1, "rs": 0.8, "first": 1.8,
+        "yi": 1.0, "pen2": 0.6, "passes": 2, "own": 1, "bias0": 0.0, "bias1": 0.0, "bias2": 0.0, "pe": 0.0, "nat": 1}
 
 
 def rank_program(g, core, T, topo):
@@ -64,7 +67,7 @@ def rank_program(g, core, T, topo):
         return
     Q = {"v": g.vector, "a": g.scalar, "t": g.tensor, "g": g, "s": g.sync}
     ops = []
-    stream, late = [None], []
+    stream = [None, 0]
     ALL = slice(None)
 
     def A(name, *idx):
@@ -110,7 +113,7 @@ def rank_program(g, core, T, topo):
 
     def add(e, fn, rd, wr, cost, sem=None, n=0, after=None, lat=0.0, hold=()):
         ops.append({"e": e, "fn": fn, "rd": rd, "wr": wr, "sem": sem, "n": n, "cost": cost, "after": after, "lat": lat, "hold": list(hold),
-                    "lead": TUNE["bias"] * (stream[0] == 0)})
+                    "lead": TUNE["bias%d" % stream[1]] * (stream[0] == 0)})
         return len(ops) - 1
 
     def tv(i, o, f=None):
@@ -159,6 +162,14 @@ def rank_program(g, core, T, topo):
                 return g.scalar.activation(o[0], i[0], ACT.Relu, bias=1.0, scale=-1.0)
             return g.vector.tensor_scalar(o[0], i[0], 0.0, None, ALU.is_equal)
         return add("*", fn, i[1], o[1], {"v": tv(i, o), "a": ta(i)})
+
+    def edge(o, i, x, up):
+        def fn(q):
+            if q == "a":
+                k = 64.0 if up else -64.0
+                return g.scalar.activation(o[0], i[0], ACT.Sigmoid, bias=-k * (x - 0.5), scale=k)
+            return g.vector.tensor_scalar(o[0], i[0], x, None, ALU.is_ge if up else ALU.is_lt)
+        return add("*" if TUNE["sig"] else "v", fn, i[1], o[1], {"v": tv(i, o), "a": ta(i)})
 
     def ts(o, i, s1, op0, s2=None, op1=None):
         if op1 is None:
@@ -215,23 +226,21 @@ def rank_program(g, core, T, topo):
     dma("s", C("rx", 0, 64), A("rn0"), "lrx", True)
     dma("s", C("rx", 64, 128), A("x0"), "lrx", True)
     for o in peers + [me]:
-        dma("s", C("SI", 256 * o, 256 * o + 256), rows("rtab", 32 * o, 32 * o + 32), "lr%d" % o, True)
+        if not TUNE["rc"]:
+            dma("s", C("SI", 256 * o, 256 * o + 256), rows("rtab", 32 * o, 32 * o + 32), "lr%d" % o, True)
+        for c in range(4 * (TUNE["rc"] > 0)):
+            dma("sa"[c % 2], rows("SI", 32 * c, 32 * c + 32, slice(256 * o, 256 * o + 256)),
+                rows("rtab", 32 * o, 32 * o + 32, slice(256 * c, 256 * c + 256)), "lr%d" % o, True)
 
     iota(col("PI", 9), [[0, 1]], 0, 1)
     iota(A("J"), [[1, 160]], 0, 0, True)
     iota(A("J8"), [[16, 9], [0, 2], [1, 8]], 0, 0, True)
     iota(A("J15"), [[0, 8], [1, 16]], 0, 0, True)
     iota(A("JG"), [[16, 8], [0, 16]], 0, 0, True)
-    iota(R("JX", 0), [[1, 4], [4, 32]], 0, -1, True)
-    for j in range(1, N):
-        iota(R("JX", j), [[64 - 64 * (j & 2), 2], [32 - 64 * (j & 1), 2], [1, 32]], 32 * j, -1, True)
-    for a in range(N):
-        iota(C("CQI", 4 * a, 4 * a + 4), [[2 - 2 * (a & 2), 2], [1 - 2 * (a & 1), 2]], 128 + a, -1)
+    iota(A("JU"), [[1, 4], [4, 32]], 0, -1, True)
     iota(C("FCI", 0, 64), [[16, 64]], 0, 0)
     iota(C("FCI", 64, 128), [[1, 64]], 0, 64)
     iota(C("FCI", 128, 256), [[8, 128]], 0, 0)
-    for h in range(2):
-        iota(rows("YI", 0, 32, slice(512 * h, 512 * h + 512)), [[1, 512]], 512 * h, 0, True)
     ms(rows("ONH", 0, 32), 1.0)
     ms(rows("ONB", 0, 32), 1.0)
     START = [ORA - 32 if t == 0 and r == 1 else TW - SEG * r for t, r in enumerate(HELD)]
@@ -239,9 +248,7 @@ def rank_program(g, core, T, topo):
         if START[t] not in START[:t]:
             ms(C("TAB", START[t], START[t] + 32), 0.0)
         ms(rows("KZ", 0, 32, t), 2080.0 - START[t] - BIG)
-    ms(A("SM"), 1.0)
-    ms(C("SM", 0, 256, 64 // NS + NS - 1), 0.0)
-    ms(C("O", 0, 132), 0.0)
+    ms(A("SC"), 0.0)
     p = col("PI", 9)
     for k, (sh, m) in enumerate([(0, 15), (0, 0x70), (0, 31), (5, 3), (3, 1), (0, 7), (2, 15), (0, 3), (0, 64)]):
         ts(col("PI", k), p, sh, SHR, m, AND)
@@ -254,7 +261,8 @@ def rank_program(g, core, T, topo):
     def low(k):
         return rows("DF", 0, 32, slice(k, k + 1))
 
-    IB, I256, IH, IM = R("IB", 0), R("IB", 1), R("PX", 0), R("IH", 2)
+    IB, I256, IH, IM = R("IB", 0), R("IB", 1), C("PW", 0, 128), R("IH", 2)
+    turn = lambda b: C("PW", -32 * b % 128, -32 * b % 128 + 128)
     ts(IB, C("J", 0, 128), pp, EQ)
     ts(I256, C("J", 0, 128), pp, EQ, 256.0, MUL)
     ts(IM, C("J", 0, 128), pp, EQ, -256.0, MUL)
@@ -263,8 +271,9 @@ def rank_program(g, core, T, topo):
     ts(R("LO", 4), C("J", 0, 144), dTL, EQ)
     for a in range(N):
         lin(R("LO", a), R("LO", 4), col("DF", AM + a))
-    ts(A("UU"), R("JX", 0), 0.0, EQ)
+    ts(A("UU"), A("JU"), 0.0, EQ)
     lin(IH, IB)
+    lin(C("PW", 128, 256), IB)
     lin(dNB, pb, -1.0, 1.0)
     lin(R("IH", 0), IB, dNB)
     lin(R("IH", 1), IB, pb)
@@ -272,55 +281,54 @@ def rank_program(g, core, T, topo):
     lin(dTD, pg, None, 7.0)
     lin(dC10, pb, 10.0, -5.0)
     lin(dC5, pb, 5.0, -5.0)
-    ts(dTC, pg, p8, ADD, 8.0, ADD)
-    lin(dCC, pb, -1280.0, 680.0)
     ts(C("DF", M8, M8 + 8), C("J", 0, 8), p8, EQ)
     lin(R("QT", 0), A("J15"), dC10, dC5)
     ts(R("QT", 1), A("JG"), pg, EQ)
     lin(R("SQ", 0), A("J15"), None, 1.0)
     tt(R("SQ", 1), R("SQ", 0), A("J15"), MUL)
     tt(A("QB"), R("QT", 0), R("QT", 1), MUL)
-    lin(A("KB"), R("SQ", 1), -5.0, 4.0)
-    ts(A("GB"), C("J", 0, 144), dTW, EQ)
-    ts(A("CC"), C("J", 0, 144), dTC, EQ, dCC, MUL)
+    ts(R("GB", 0), C("J", 0, 144), dTW, EQ)
+    ts(R("GB", 1), C("J", 0, 144), dTW, EQ, -1.0, MUL)
     for a8 in range(8):
         lin(R("QA", a8), A("QB"), col("DF", M8 + a8))
     lin(dWT, pi, 2.0, 1.0)
     ts(dP0, pp, 0.0, EQ)
-    ts(A("CQI"), A("CQI"), 3, AND)
-    for a in range(N):
-        lin(rows("DF", 32 * a, 32 * a + 32, slice(CQ, CQ + 4)), rows("CQI", 32 * a, 32 * a + 32, slice(4 * a, 4 * a + 4)))
+    ts(col("PI", 12), pa, pp, SUB, 128.0, ADD)
+    ts(col("PI", 13), col("PI", 12), 3, AND)
+    cp(col("DF", 47), col("PI", 13))
+    ts(C("DF", CQ, CQ + 5), C("J", 0, 5), col("DF", 47), ADD, 1.5, ADD)
     ts(A("WB"), C("J", 0, 144), dTW, EQ, dWT, MUL)
     ts(R("WD", 0), A("J8"), dTD, EQ, dWT, MUL)
     ms(rows("K256", 0, 32), 256.0)
     for b in range(1, N // min(HELD[:-1])):
-        ts(col("PI", 11), p, 32 * b, AND)
-        cp(col("DF", 44), col("PI", 11))
-        lin(col("DF", 45), col("DF", 44), -2.0, dTD)
-        lin(col("DF", 46), col("DF", 45), None, 32.0 * b)
+        ts(col("PI", 11), pp, 128.0 - 32 * b, ADD)
+        ts(col("PI", 14), col("PI", 11), 0x70, AND)
+        lin(col("DF", 46), col("PI", 14), None, 7.0)
         ts(R("WD", b), A("J8"), col("DF", 46), EQ, dWT, MUL)
     ts(dTX, pg, p8, ADD)
     lin(dTY, pv16, 1.0 / 16)
     ts(C("DF", MF, MF + 2), C("J", 0, 2), pb, EQ, dTY, MUL)
     for h in range(2):
         ts(R("XP", h), A("J8"), dTX, EQ, col("DF", MF + h), MUL)
-    ts(A("OG"), A("JG"), pg, EQ)
-    ts(R("T2", 0), A("J15"), pi, ALU.is_lt, -1.0, MUL)
-    lin(R("T2", 1), IB, -2048.0)
-    tt(R("T2", 2), R("T2", 0), A("OG"), MUL)
-    tt(R("T2", 3), R("T2", 2), R("T2", 1), ADD)
-    lin(dCF0, dP0, 1.0 / 1024)
-    lin(dCF1, dP0, -1.0, 1.0)
+    ts(A("OG"), A("JG"), pg, EQ, 0.25, MUL)
+    ts(R("T2", 2), A("J15"), pi, ALU.is_lt)
+    lin(R("T2", 3), IB, 512.0)
+    tt(R("T2", 4), R("T2", 2), A("OG"), MUL)
+    tt(R("T2", 1), R("T2", 4), R("T2", 3), ADD)
+    tt(R("T2", 0), A("OG"), R("T2", 1), SUB)
+    ms(rows("CF", 0, 32), 1.0)
+    lin(dTC, pp, 1.0 / 16)
+    lin(A("F8"), C("J", 0, 64), 1.0 / 1024, dTC)
+    dma("a", rows("CF", 0, 1), rows("F8", 0, 16), "tr")
     for t in range(RO):
         lin(col("DF", KSC + t), dP0, 49152.0 - t, float(t))
         lin(rows("KS", 0, 32, t), rows("ONB", 0, 32, slice(0, 128)), low(KSC + t))
     ts(col("DF", KD), pp, 1.0, EQ, -5.0, MUL)
     ts(col("DF", KD + 1), pp, 1.0, EQ, -10.0, MUL)
-    for k, al in enumerate((0.5, 1.0, 2.0, 4.0)):
+    for k, al in enumerate(STRIDE):
+        lin(R("AL", k), IB, al / 1024)
         ts(col("DF", KD + 2 + k), pp, 1.0, ALU.not_equal, al, MUL)
         lin(rows("KA", 0, 32, k), rows("SQ", 0, 32, 1), low(KD + k // 3), low(KD + 2 + k))
-    for h in range(2):
-        lin(rows("CF", 0, 32, slice(512 * h, 512 * h + 512)), rows("YI", 0, 32, slice(512 * h, 512 * h + 512)), low(12), low(13))
     lin(A("FC16"), C("FCI", 0, 64), None, pi)
     lin(A("FD"), C("FCI", 128, 256), None, p8)
     ts(C("FCI", 64, 128), C("FCI", 64, 128), 1023, AND)
@@ -329,16 +337,22 @@ def rank_program(g, core, T, topo):
     ts(col("DF", 48), pv64, 1.0 / 16, MUL, pc4, ADD)
     lin(dW4, pi4, 2.0, 1.0)
     lin(dTWL, col("DF", 48), 4.0, 3.0)
-    ts(R("WL", 0, 0, 36), C("J", 0, 36), dTWL, EQ, dW4, MUL)
+    ts(R("WL", 0), C("J", 0, 36), dTWL, EQ, dW4, MUL)
+    lin(R("WL", 1), R("WL", 0), -256.0)
+    lin(A("WF"), R("WL", 0))
+    ms(rows("KX", 0, 32), 256.0 * HB)
+    ms(rows("KY", 0, 32), 65536.0 * HB)
+    for q in (2, 3):
+        ms(rows("KY", 0, 32, slice(q, 32, 4)), -256.0 * HB)
     OWN = {1: 0, 2: 2, 4: 3}
-    unit = lambda j: (BIG + SEG * POS[j]) / 32
+    unit = lambda j: BIG + SEG * POS[j]
+    lin(R("PS", 2), IB, -6144.0)
+    lin(R("PS", 3), IB, 1024.0)
     for j in range(N):
-        if any(j and not j & OWN[r] for r in HELD):
-            ts(R("PX", j), R("JX", j), 0.0, EQ)
         if any(r > 1 and j & OWN[r] == j for r in HELD):
             lin(R("IS", j), IB, unit(j))
         if 2 in HELD and j & 1:
-            ts(R("PS", j // 2), R("JX", 1), 0.0, EQ, unit(j & 2), MUL)
+            lin(R("PS", j // 2), turn(1), unit(j & 2))
     for k, s in enumerate([2048.0, -1024.0, -512.0, -256.0]):
         lin(R("DI", k), IB, s)
 
@@ -358,9 +372,13 @@ def rank_program(g, core, T, topo):
     for a in [me] + peers[::-1]:
         for c in range(4):
             mm(rows("pW1", 32 * a, 32 * a + 32, slice(16 * c, 16 * c + 16)), uu(c), lx(a, 256, 272), True, True)
-            mm(rows("pZ%d" % (c // 2), 32 * a, 32 * a + 32, slice(256 * (c % 2), 256 * (c % 2) + 256)), uu(c), lx(a, 0, 256), True, True)
+            if TUNE["rc"]:
+                lin(rows("RT", 32 * a, 32 * a + 32, 2, slice(256 * c, 256 * c + 256)),
+                    rows("SR" if a == me else "LR", 32 * c, 32 * c + 32, a, slice(0, 256)))
+            else:
+                mm(rows("pZ%d" % (c // 2), 32 * a, 32 * a + 32, slice(256 * (c % 2), 256 * (c % 2) + 256)), uu(c), lx(a, 0, 256), True, True)
         mm(rows("pW1", 32 * a, 32 * a + 32, slice(128, 256)), lx(a, 256, 288), IH, True, True)
-    for k in range(2):
+    for k in range(2 * (not TUNE["rc"])):
         lin(R("RT", 2, 512 * k, 512 * k + 512), A("pZ%d" % k))
     cp(A("CUR"), C("pW1", 0, 64))
     lin(A("XT"), C("pW1", 128, 256))
@@ -381,25 +399,27 @@ def rank_program(g, core, T, topo):
         elif o == me:
             dma("s", rows("TAB", 32 * me, 32 * me + 32, slice(ORA, ORA + 4096)), rows("btab", 32 * me, 32 * me + 32), "ta", True, hold)
         else:
-            bank = ("pX0", "pW0", "pX1")[j]
+            bank = "p" + BANKS.split()[j]
             dma("s", R("SB", j), rows("btab", 32 * o, 32 * o + 32), "lb%d" % j, True, hold)
             mm(A(bank), IB, R("SB", j, 0, 512), True, False)
             mm(A(bank), I256, R("SB", j, 512, 1024), False, True)
             done[step[:2]] = whole(R("PK", j), A(bank))
             send(j, R("PK", j), lambda r: R("LP", r), "ap")
 
-    def split(lo, hi, x, hx, xx, ps):
+    def split(lo, hi, x, hx, xx, ps, plain=False):
         lin(hx, x, 1.0 / 256, HB - 0.498)
-        lin(xx, x, None, 256.0 * HB)
-        mm(ps, IM, hx, True, True)
+        lin(xx, x, None, None if plain else 256.0 * HB)
+        if plain:
+            mm(ps, rows("KX", 0, 1), rows("ONB", 0, 1, slice(0, ps[2])), True, False)
+        mm(ps, IM, hx, not plain, True)
         tt(lo, xx, ps, ADD)
         lin(hi, hx, None, -HB)
 
     def unstack():
         for j, q in enumerate(peers[::-1]):
             split(R("SB", j, 0, 512), R("SB", j, 512, 1024), R("LP", q), C("G4", 512 * j, 512 * j + 512),
-                  R("RT", 1, 512 * j, 512 * j + 512) if j < 2 else C("IC", 0, 512), A(UNP[j]))
-        inner = ["pY0", "pY1", "pZ0", "pZ1", "pX0", "pX1"]
+                  R("RT", 1, 512 * j, 512 * j + 512) if j < 2 else C("IC", 0, 512), A("p" + BANKS.split()[3 + j]))
+        inner, last = ["p" + x for x in BANKS.split()[6:]], [None, None]
         for a in [me if x[1] == "3" else peers[2 - int(x[1])] for x in ARRIVE.split()]:
             for c in range(4):
                 x = 768 * c
@@ -408,67 +428,70 @@ def rank_program(g, core, T, topo):
                     o = 768 * (a - c)
                     mm(rows(inner[x // 512], 32 * a, 32 * a + 32, slice(x % 512, (y - 1) % 512 + 1)), uu(c),
                        C("SH" if a == me else "LH", x + o, y + o), True, True)
+                    k = inner[x // 512][1] == "X"
+                    ops[-1]["after"], last[k] = last[k], len(ops) - 1
                     x = y
         for k in range(6):
             lin(C("IT", 512 * k, 512 * k + 512), A(inner[k]))
         for j, q in enumerate(peers[::-1]):
             dma("s", rows("TAB", 32 * q, 32 * q + 32, slice(ORA, ORA + 4096)), R("SB", j), "ta", True, [done[SET]])
+        if HELD[0] == 2 and TUNE["twice"]:
+            second = lambda q: rows("TAB", 32 * (q ^ 2), 32 * (q ^ 2) + 32, slice(ORG[2], ORG[2] + 4096))
+            if TUNE["twice"] > 1:
+                for x in range(0, 4096, 1024):
+                    for y in (0, 64):
+                        lin(rows("TAB", y, y + 64, slice(ORG[2] + x, ORG[2] + x + 1024)),
+                            rows("TAB", 64 - y, 128 - y, slice(ORA + x, ORA + x + 1024)))
+                return
+            for j, q in enumerate(peers[::-1]):
+                dma("s", second(q), R("SB", j), "tb2", True)
+            dma("s", second(me), rows("btab", 32 * me, 32 * me + 32), "tb2", True)
 
     def widen(src, j, a, b, sem):
-        n = 128 if j == 0 else 64 if j == 2 else 32
-        for x in range(0, 128, n):
-            y = x ^ (32 * j)
-            dma("s", rows("TAB", x, x + n, slice(a, b)), src(y, y + n), sem)
+        k = 32 * j
+        dma("s", rows("TAB", 0, 128 - k, slice(a, b)), src(k, 128), sem)
+        if j:
+            dma("s", rows("TAB", 128 - k, 128, slice(a, b)), src(0, k), sem)
 
     def held(t):
         return {1: (0,), 2: (0, 2), 4: (0, 2, 1, 3)}[HELD[t]]
 
     KW = 64 // NS
-    CW = KW + NS - 1
+    CW = KW + 1
 
-    def plane(ps, s, lvl, k=None, times=1):
-        if k is None:
-            mm(A(ps), rows("KB", 0, 1), rows("ONH", 0, 1), True, False)
-        else:
-            mm(A(ps), rows("KA", 0, 3, k), rows("CF", 0, 3, slice(512 * s, 512 * s + 512)), True, False)
-        for rep in range(times):
+    def plane(ps, s, lvl, k):
+        mm(A(ps), rows("KA", 0, 3, k), rows("CF", 0, 3, slice(512 * s, 512 * s + 512)), True, False)
+        for rep in range(1 + k // 3):
             for i in range(8):
-                mm(C(ps, i, 512, 8), R("QA", i), R("FT", lvl, 64 * s, 64 * s + 64), False, i == 7 and rep == times - 1)
+                mm(C(ps, i, 512, 8), R("QA", i), R("FT", lvl, 64 * s, 64 * s + 64), False, i == 7 and rep == k // 3)
 
-    def to_list(o, big, data, start=True):
+    def to_list(o, big, data, start=True, stop=True):
         for i in range(16):
-            mm(o, C(big, 15 - i, 143 - i), data(i), start and i == 0, i == 15)
+            mm(o, big(15 - i, 143 - i), data(i), start and i == 0, stop and i == 15)
 
     def gather(dst, win, lst, z):
-        for k in range(KW * z, KW * z + KW, 16):
-            lin(dst(16 * k, 16 * k + 256), ind(win, C(lst, k, k + 16)))
+        k = KW * z
+        for a, b in ((k, k + TUNE["cut"]), (k + TUNE["cut"], k + KW)):
+            lin(dst(16 * a, 16 * b), ind(win, C(lst, a, b)))
 
     def level(t, lvl, z):
-        if lvl == 0:
-            got, win = lambda a, b: R("RT", t, a, b), R("RT", (t - 1) % RO)
-            app = got
-        else:
-            got, win = lambda a, b: C("IC", a, b) if t else C("IT", 3072 + a, 3072 + b), C("IT", 0, (3072, 4096, 6144)[t])
-            app = (got, lambda a, b: C("IT", 4096 + 2 * a, 4096 + 2 * b, 2), lambda a, b: C("E0", a, b))[t]
-        bank = lambda s: "p%s%d" % ("XY"[lvl], s)
-        k0, k1, hs = KW * z, KW * z + KW, range(2 * z // NS, (2 * z + 2) // NS)
+        k, c0, c1 = t + lvl, 512 * z, 512 * z + 512
         stream[0] = z
-        o = C("pW%d" % z, 64 + 64 * lvl, 64 + 64 * lvl + KW)
-        gather(got, win, ("CUR", "IL")[lvl], z)
-        for s in hs:
-            plane(bank(s), s, lvl)
-            tt(R("SEL", lvl, 512 * s, 512 * s + 512), got(512 * s, 512 * s + 512), A(bank(s)), ALU.min)
-        for h in range(2):
-            mm(o, C("CC", 8 - 8 * h, 136 - 8 * h), R("FT", lvl, 2 * k0 + h, 2 * k1, 2), h == 0, False)
-        to_list(o, "GB", lambda i: R("SEL", lvl, 16 * k0 + i, 16 * k1, 16), False)
-        whole(C(("IL", "OL")[lvl], k0, k1), o, 2048.0, 6741.0 * 2048)
-        n0 = len(ops)
-        for s in hs if lvl or t < RO - 1 else ():
-            plane(bank(s), s, lvl, t + lvl, 1 + (t == RO - 1))
-            tt(app(512 * s, 512 * s + 512), got(512 * s, 512 * s + 512), A(bank(s)), ALU.max)
-        if t == lvl == 0 and TUNE["late"]:
-            late.extend(ops[n0:])
-            del ops[n0:]
+        bank = "p%s%d" % ("XY"[lvl], z)
+        gather(lambda a, b: R("GOT", lvl, a, b), C("IT", 0, (3072, 4096, 6144)[t]) if lvl else R("RT", (t - 1) % RO), ("CUR", "IL")[lvl], z)
+        plane(bank, z, lvl, k)
+        tt(R("APP", lvl, c0, c1), R("GOT", lvl, c0, c1), A(bank), ALU.max)
+        joint = TUNE["joint"] >> (2 * t + lvl) & 1
+        if z or not joint:
+            k0, k1 = KW * z * (not joint), KW * z + KW
+            o = C("pW%d" % z, 64 + 64 * lvl, 64 + 64 * lvl + k1 - k0)
+            mm(o, R("AL", k), C("FC16", k0, k1), True, False)
+            to_list(o, lambda a, b: R("GB", 0, a, b), lambda i: R("GOT", lvl, 16 * k0 + i, c1, 16), False, False)
+            to_list(o, lambda a, b: R("GB", 1, a, b), lambda i: R("APP", lvl, 16 * k0 + i, c1, 16), False)
+            whole(C(("IL", "OL")[lvl], k0, k1), o, 2048.0, 2048.0 * (1 + STRIDE[k]))
+        if t < RO - 1:
+            lin(R("RT", t, c0, c1) if lvl == 0 else C("IT", 3072 + c0, 3072 + c1) if t == 0 else C("IT", 4096 + 2 * c0, 4096 + 2 * c1, 2),
+                R("APP", lvl, c0, c1))
 
     def root_number(z, num, m, d, prod, w, f):
         ts(z, w, 7, AND)
@@ -496,16 +519,19 @@ def rank_program(g, core, T, topo):
     def send_inner():
         le = lambda r: C("LE", 256 * r, 256 * r + 256)
         for j, r in enumerate(peers + [me]):
-            dma("s", le(me) if r == me else C("LH", 256 * r, 256 * r + 256), rows("E0", 32 * r, 32 * r + 32), "le%d" % r)
+            dma("s", le(me) if r == me else C("LH", 256 * r, 256 * r + 256), rows("APP", 32 * r, 32 * r + 32, 1), "le%d" % r)
             if r != me:
                 send(j, C("LH", 256 * r, 256 * r + 256), le, "ae")
+
+    def decode_inner(hold):
         for s in range(2):
             e = lambda k: C("LH" if k else "LE", 1024 * k + 512 * s, 1024 * k + 512 * s + 512)
             for k, x in ((1, 1.0), (2, 2.0), (3, 4.0)):
-                relu(e(k), e(0), x)
+                ops[relu(e(k), e(0), x)]["hold"] = hold
             for k in range(4):
-                mm(A("pY%d" % s), R("DI", k), e(k), k == 0, k == 3)
-            lin(C("YI", 512 * s, 512 * s + 512), A("pY%d" % s), None, 2048.0)
+                mm(A("pZ%d" % s), R("DI", k), e(k), k == 0, k == 3)
+                ops[-1]["hold"] = hold
+            lin(C("YI", 512 * s, 512 * s + 512), A("pZ%d" % s), None, 2048.0)
         for r in range(N):
             dma("s", rows("yi", 32 * r, 32 * r + 32), C("YI", 256 * r, 256 * r + 256), "out")
 
@@ -516,41 +542,42 @@ def rank_program(g, core, T, topo):
         k0, k1, c0, c1 = KW * z, KW * z + KW, 16 * KW * z, 16 * KW * (z + 1)
         stream[0] = z
         sm = lambda name, j=0: C(name, 64 * j + k0, 64 * j + k1)
-        cl = lambda name, j: C(name, 4 * CW * z + CW * j + NS - 1, 4 * CW * z + CW * j + CW)
+        cl = lambda name, j: C(name, 4 * CW * z + CW * j + 1, 4 * CW * z + CW * j + CW)
         cz = lambda name: C(name, 4 * CW * z, 4 * CW * z + 4 * CW)
         gather(lambda a, b: C("OLD", a, b), C("TAB", ORA, ORA + (4096, 6144, 10240)[t]), "OL", z)
-        to_list(C(W, 192, 192 + KW), "WB", lambda i: C("OLD", c0 + i, c1, 16))
+        to_list(C(W, 192, 192 + KW), lambda a, b: C("WB", a, b), lambda i: C("OLD", c0 + i, c1, 16))
+        rr = lambda j: R("RR", j, k0, k1)
+        for j in range(N + 1):
+            ts(rr(j), C(W, 192, 192 + KW), col("DF", CQ + j), SUB, 1.5 * 2 ** 25, ADD)
         whole(sm("HI"), C(W, 192, 192 + KW))
-        ts(sm("Q0"), sm("HI"), 3, AND)
+        sc = lambda a, b, st=None: C("SC", 1 + 4 * CW * z + a, 1 + 4 * CW * z + b, st)
         if z:
-            lin(C("O", 4 * CW, 8 * CW, CW), C("SC", KW, 4 * CW, CW))
+            lin(sc(0, 4 * CW, CW), C("SC", 1 + KW, 1 + 4 * CW, CW))
         for j in range(N):
-            ts(cl("O", j), sm("Q0"), col("DF", CQ + j), EQ)
-        mask = C("SM", 0, 4 * CW)
-        add("v", lambda q: g.vector.tensor_tensor_scan(cz("SC")[0], mask[0], cz("O")[0], 0.0, MUL, ADD), regs(mask, cz("O")), cz("SC")[1],
-            {"v": tv(cz("SC"), cz("SC"))})
-        cnt = C(W, 256, 256 + 4 * CW)
-        mm(cnt, R("T2", 3), cz("O"), True, False)
-        mm(cnt, A("OG"), cz("SC"), False, True)
+            o, first = sc(CW * j + 1, CW * j + CW), sc(CW * j, CW * j + 1)
+            add("v", lambda q, o=o, j=j, first=first: g.vector.tensor_tensor_scan(o[0], rr(j)[0], rr(j + 1)[0], first[0], ADD, SUB),
+                regs(rr(j), rr(j + 1), first), o[1], {"v": tv(rr(j), o)})
+        cnt = C("pZ%d" % z, 256, 256 + 4 * CW)
+        mm(cnt, R("T2", 0), sc(0, 4 * CW), True, False)
+        mm(cnt, R("T2", 1), sc(-1, 4 * CW - 1), False, True)
         hi = C("VI", 2 * k0 + KW, 2 * k1)
         ts(C("VI", 2 * k0, 2 * k0 + KW), sm("HI"), 255, AND)
         ts(hi, sm("HI"), (4096 if t == 0 else 8192) - 256, AND)
         lin(C("VF", 2 * k0, 2 * k1), C("VI", 2 * k0, 2 * k1))
         mm(C(FAR, 0, KW * nb), rows("KZ", 0, 1, t), rows("ONH", 0, 1, slice(0, KW * nb)), True, False)
-        feats = [C("VF", 2 * k0, 2 * k0 + KW), C("VF", 2 * k0 + KW, 2 * k1)]
-        for k, (x, y) in enumerate([(4096.0, -6144.0), (5120.0, 1024.0)][:(0, 2, 1)[t]]):
-            feats.append(sm("C12", k))
-            ts(feats[-1], hi, x, ALU.is_ge, y, MUL)
-        ts(cz("GD"), cnt, CAP + 1 - 2048.0, ALU.is_lt, 32.0 if own else 32.0 * unit(0), MUL)
-        for x in feats:
+        for x in (C("VF", 2 * k0, 2 * k0 + KW), C("VF", 2 * k0 + KW, 2 * k1)):
             for b in range(nb):
-                mm(C(FAR, KW * b, KW * b + KW), R("PX", b), x, False, False)
+                mm(C(FAR, KW * b, KW * b + KW), turn(b), x, False, False)
+        for k, x in enumerate((4096.0, 5120.0)[:(0, 2, 1)[t]]):
+            edge(sm("C12", k), hi, x, True)
+            mm(C(FAR, 0, KW), R("PS", 2 + k), sm("C12", k), False, False)
+        edge(cz("GD"), cnt, CAP + 1 - 2048.0, False)
         for j in range(N):
             b = j & ~own
-            mm(C(FAR, KW * b, KW * b + KW), R("PX", j) if not own else R("PS", j // 2) if b else R("IS", j), cl("GD", j), False, j == N - 1)
+            mm(C(FAR, KW * b, KW * b + KW), R("PS", j // 2) if b else R("IS", j), cl("GD", j), False, j == N - 1)
         f0 = 4 * k0
         for x in range(0, KW * nb, 128):
-            cp(C("FL", f0 + x, f0 + min(x + 128, KW * nb)), C(FAR, x, min(x + 128, KW * nb)))
+            relu(C("FL", f0 + x, f0 + min(x + 128, KW * nb)), C(FAR, x, min(x + 128, KW * nb)), 0.0)
 
         def far(b, c):
             k = f0 + KW * b + 16 * c - k0
@@ -567,7 +594,7 @@ def rank_program(g, core, T, topo):
             mm(o, IB, C("OLD", x, x + 256), False, False)
             for b in range(nb):
                 far(b, c)
-                mm(o, R("PX", b), C("G4", 1024 * b + x, 1024 * b + x + 256), False, b == nb - 1)
+                mm(o, turn(-b), C("G4", 1024 * b + x, 1024 * b + x + 256), False, b == nb - 1)
             lin(C("Y", x, x + 256), o, -1.0, 127.5)
             tt(C("NEW", x, x + 256), o, C("Y", x, x + 256), ADD)
         if t == RO - 1:
@@ -598,8 +625,8 @@ def rank_program(g, core, T, topo):
 
     def finish(t):
         stream[0] = None
-        W, nb, banks = "pW0", N // HELD[t], ("pZ0", "pZ1", "pX0", "pX1")
-        homes = peers + [me]
+        W, nb, banks = "pX1", N // HELD[t], ("pY0", "pW0", "pY1", "pW1")
+        homes, gone = peers + [me], []
         for a, bank in zip(homes, banks):
             mm(C(bank, 0, 256), rows("KS", 0, 2, t), rows("ONB", 0, 2, slice(0, 256)), True, False)
             for c in range(4):
@@ -609,39 +636,50 @@ def rank_program(g, core, T, topo):
             o, x = C(bank, 0, 256), 256 * a
             for c in range(4):
                 for b in range(nb):
-                    mm(o, R("LO", a ^ b, 3 - c, 131 - c), C("G4", 1024 * b + 256 * c, 1024 * b + 256 * c + 256), False, c == 3 and b == nb - 1)
+                    mm(o, R("LO", (a + b) % N, 3 - c, 131 - c), C("G4", 1024 * b + 256 * c, 1024 * b + 256 * c + 256), False, c == 3 and b == nb - 1)
             lin(C("Y", x, x + 256), o, None, -127.5)
             if a == me:
                 tt(C("NH", x, x + 256), o, C("Y", x, x + 256), SUB)
                 continue
             tt(C("NEW", x, x + 256), o, C("Y", x, x + 256), SUB)
-            mm(C(bank, 256, 384), IB, C("NEW", x, x + 256, 2), True, False)
-            mm(C(bank, 256, 384), I256, C("NEW", x + 1, x + 256, 2), False, True)
-            whole(C("PY", 128 * a, 128 * a + 128), C(bank, 256, 384))
+            mm(C(bank, 256, 384), IB, C("NEW", x, x + 128), True, False)
+            mm(C(bank, 256, 384), I256, C("NEW", x + 128, x + 256), False, True)
+            gone.append(whole(C("PY", 128 * a, 128 * a + 128), C(bank, 256, 384)))
             send(j, C("PY", 128 * a, 128 * a + 128), ly, "ay")
+        decode_inner(gone[TUNE["dec"]:][:1])
         for r, bank in zip([me] + peers[::-1], (None,) + banks):
             x = 256 * r
             if r != me:
-                split(C("NH", x, x + 256, 2), C("NH", x + 1, x + 256, 2), ly(r), C("HY", 128 * r, 128 * r + 128),
-                      C("XY", 128 * r, 128 * r + 128), C(bank, 0, 128))
+                split(C("NH", x, x + 128), C("NH", x + 128, x + 256), ly(r), C("HY", 128 * r, 128 * r + 128),
+                      C("XY", 128 * r, 128 * r + 128), C(bank, 0, 128), True)
             dma("s", rows("yb", 32 * r, 32 * r + 32), C("NH", x, x + 256), "out")
+            o = rows(W, 32 * r, 32 * r + 32, slice(0, 64))
+            if r == me:
+                for q in range(4):
+                    mm(o, R("WL", 0, 3 - q, 35 - q), C("NH", x + 64 * q, x + 64 * q + 64), q == 0, q == 3)
+                continue
+            mm(o, rows("KY", 0, 1), rows("ONB", 0, 1, slice(0, 64)), True, False)
             for q in range(4):
-                mm(rows(W, 32 * r, 32 * r + 32, slice(0, 64)), R("WL", 0, 3 - q, 35 - q), C("NH", x + 64 * q, x + 64 * q + 64), q == 0, q == 3)
+                y = 128 * r + 64 * (q % 2)
+                mm(o, R("WL", int(q < 2), 3 - q, 35 - q), C("HY", y, y + 64), False, False)
+            for q in range(2):
+                y = 128 * r + 64 * q
+                mm(o, C("WF", 3 - q, 35 - q), C("XY", y, y + 64), False, q == 1)
         cp(R("WI2", 0), C(W, 0, 64))
         root_number(R("WI2", 1), R("WI2", 2), R("DF2", 0), R("DF2", 1), R("DF2", 2), R("WI2", 0), R("FL2", 0))
         tt(A("YNS"), R("DF2", 2), R("FL2", 1), ADD)
         dma("a", A("yn"), A("YNS"), "out")
 
     for t in range(RO):
+        stream[1] = t
         for z in range(NS):
             keys(t, z)
             level(t, 0, z)
         stream[0] = None
         if t == 0:
             unstack()
-            ops.extend(late)
         for j in held(t):
-            if j and (t == 0 or j not in held(t - 1)):
+            if j and (t == 0 and not TUNE["twice"] or t and j not in held(t - 1)):
                 widen(lambda x, y: rows("TAB", x, y, slice(ORA, ORA + 4096)), j, ORG[j], ORG[j] + 4096, "tb%d" % j)
         for z in range(NS):
             level(t, 1, z)
@@ -662,35 +700,40 @@ def rank_program(g, core, T, topo):
         if o["n"]:
             group.setdefault(o["sem"], []).append(n)
     for n, o in enumerate(ops):
-        pre = set(o["hold"])
+        pre, turn = set(o["hold"]), set()
         for mine, w in [(r, False) for r in o["rd"]] + [(r, True) for r in o["wr"]]:
             ps = mine[0] in PSUM
             keep = []
             for item in hist.get(mine[0], []):
                 m, reg, mw = item
                 if (w or mw or ps) and m != n and meet(mine, reg) and ops[m]["sem"] != "remote":
-                    pre.update(group[ops[m]["sem"]] if ops[m]["n"] else [m])
-                if not ((w or ps) and mine[1] <= reg[1] and reg[2] <= mine[2] and mine[3] <= reg[3] and reg[4] <= mine[4]):
+                    (pre if w or mw else turn).update(group[ops[m]["sem"]] if ops[m]["n"] else [m])
+                if not (w and mine[1] <= reg[1] and reg[2] <= mine[2] and mine[3] <= reg[3] and reg[4] <= mine[4]):
                     keep.append(item)
             keep.append((n, mine, w))
             hist[mine[0]] = keep
-        o["pre"] = pre
+        o["turn"] = turn - pre
+        o["pre"] = pre = pre | turn
         o["dep"] = pre | ({o["after"]} if o["after"] is not None else set())
         o["post"] = []
         o["due"] = TUNE["yi"] if o["wr"] and o["wr"][0][0] == "yi" else 0.0
+        if o["sem"] in ("rn0", "rn1"):
+            o["lat"] += 0.0
+            o["soon"] = TUNE["soon"]
     for n, o in enumerate(ops):
         for m in o["dep"]:
             ops[m]["post"].append(n)
     for n in range(n_ops - 1, -1, -1):
         o = ops[n]
-        own = min(o["cost"].values()) + (o["lat"] + RLAT if o["sem"] and o["e"] != "x" else 0.0)
-        o["rank"] = own + max([ops[m]["rank"] + HOP * (o["e"] != "t" or ops[m]["e"] != "t") for m in o["post"]] + [o["due"]])
+        own = min(o["cost"].values()) + (o["lat"] + RLAT if o["sem"] and o["e"] != "x" else 0.0) + o.get("soon", 0.0)
+        o["rank"] = own + max([ops[m]["rank"] + HOP * ((o["e"] != "t" or ops[m]["e"] != "t") and n not in ops[m]["turn"])
+                               - RLAT * (ops[m]["after"] == n and ops[m]["n"] == 16 != ops[m]["e"] != "x" and n not in ops[m]["pre"]) for m in o["post"]] + [o["due"]])
     can = [list(o["cost"]) if o["e"] == "*" else [o["e"]] for o in ops]
     tight = [{m: (ops[m]["after"] == n and ops[m]["e"] != "x" and n not in ops[m]["pre"]) or o["e"] == ops[m]["e"] == "t"
-              for m in o["post"]} for n, o in enumerate(ops)]
+              or n in ops[m]["turn"] for m in o["post"]} for n, o in enumerate(ops)]
     hop = [0.0 if o["e"] == "x" else HOP for o in ops]
 
-    def play(eng, queues):
+    def play(eng, queues, slow):
         eng = list(eng)
         free = {e: 0.0 for e in "vatgsx"}
         lanes = [0.0, TUNE["first"]]
@@ -698,16 +741,21 @@ def rank_program(g, core, T, topo):
         at, tail, seq = [0.0] * n_ops, [0.0] * n_ops, []
         ready = {n for n in range(n_ops) if not left[n]}
         head = {e: 0 for e in "vatgsx"}
+        other = [{} for _ in ops]
+
+        def start(n, e):
+            return max([free[e], at[n]] + [t for x, t in other[n].items() if x != e])
+
         while ready:
             if queues:
-                cand = [(max(free[e], at[q[head[e]]]), e, q[head[e]]) for e, q in queues.items() if head[e] < len(q) and q[head[e]] in ready]
+                cand = [(start(q[head[e]], e), e, q[head[e]]) for e, q in queues.items() if head[e] < len(q) and q[head[e]] in ready]
                 t1, e, n = min(cand)
                 head[e] += 1
             else:
                 cand = []
                 for n in ready:
-                    e = min(can[n], key=lambda x: max(free[x], at[n]) + ops[n]["cost"][x] * (1.0 + TUNE["pen"] * (x == "v")))
-                    cand.append((max(free[e], at[n]), e, n))
+                    e = min(can[n], key=lambda x: start(n, x) + ops[n]["cost"][x] * (1.0 + TUNE["pen"] * (x == "v")))
+                    cand.append((start(n, e), e, n))
                 t0, e0, _ = min(cand)
                 t1, e, n = max([c for c in cand if c[1] == e0 and c[0] <= t0 + TUNE["win"]], key=lambda c: (ops[c[2]]["rank"] + ops[c[2]]["lead"], -c[2]))
             o = ops[n]
@@ -717,7 +765,7 @@ def rank_program(g, core, T, topo):
             free[e] = issue if e != "x" else 0.0
             if o["sem"] and e != "x":
                 far = o["sem"] == "remote"
-                lanes[0] = max(end + (TUNE["rs"] + lanes[1] if far else TUNE["rs"]), lanes[0]) + o["lat"]
+                lanes[0] = max(end + (TUNE["rs"] + lanes[1] if far else TUNE["rs"]), lanes[0]) + o["lat"] * slow
                 lanes[1] *= not far
                 end = lanes[0] + 0.5 + (TUNE["ext"] if far else 0.0)
             elif e == "t":
@@ -726,6 +774,8 @@ def rank_program(g, core, T, topo):
             ready.remove(n)
             seq.append(n)
             for m in o["post"]:
+                if n in ops[m]["turn"]:
+                    other[m][e] = end + HOP
                 at[m] = max(at[m], issue if tight[n][m] else end + hop[m])
                 left[m] -= 1
                 if not left[m]:
@@ -738,12 +788,15 @@ def rank_program(g, core, T, topo):
         for n in order:
             o = ops[n]
             if back:
-                t = max([at[m] + ops[m]["cost"][eng[m]] + (0.0 if tight[n][m] else tail[n] + hop[m]) for m in o["post"]] + [tail[n] + o["due"]])
+                t = max([at[m] + ops[m]["cost"][eng[m]] + (0.0 if tight[n][m] else tail[n] + hop[m] + o.get("soon", 0.0)) for m in o["post"]]
+                        + [tail[n] + o["due"]])
             else:
                 t = max([at[m] + ops[m]["cost"][eng[m]] + (0.0 if tight[m][n] else tail[m] + hop[n]) for m in o["dep"]] + [0.0])
             best = None
+            turns = [m for m in o["post"] if n in ops[m]["turn"]] if back else o["turn"]
             for e in can[n]:
-                c, t1, k = o["cost"][e], t, 0
+                c, k = o["cost"][e], 0
+                t1 = max([t] + [at[m] + ops[m]["cost"][eng[m]] + HOP for m in turns if eng[m] != e])
                 if e != "x":
                     lo, hi = busy[e]
                     a, b = 0, len(hi)
@@ -763,15 +816,38 @@ def rank_program(g, core, T, topo):
                 busy[eng[n]][1].insert(k, at[n] + o["cost"][eng[n]])
         return at, eng
 
-    best = now = play([None] * n_ops, None)
-    for _ in range(TUNE["passes"]):
-        _, seq, eng, at, tail = now
-        pos = {n: k for k, n in enumerate(seq)}
-        at, eng = pack(sorted(seq, key=lambda n: (-at[n], -pos[n])), tail, True)
-        at, eng = pack(sorted(seq, key=lambda n: (-at[n] - ops[n]["cost"][eng[n]], pos[n])), tail, False)
-        seq = sorted(seq, key=lambda n: (at[n], pos[n]))
-        now = play(eng, {e: [n for n in seq if eng[n] == e] for e in "vatgsx"})
-        best = min(best, now, key=lambda x: x[0])
+    def ordered(key, back):
+        nxt, cnt = ("dep", "post") if back else ("post", "dep")
+        left = [len(o[cnt]) for o in ops]
+        ready = sorted((key[n], n) for n in range(n_ops) if not left[n])
+        out = []
+        while ready:
+            n = ready.pop(0)[1]
+            out.append(n)
+            for m in ops[n][nxt]:
+                left[m] -= 1
+                if not left[m]:
+                    a, b = 0, len(ready)
+                    while a < b:
+                        mid = (a + b) // 2
+                        a, b = (mid + 1, b) if ready[mid] < (key[m], m) else (a, mid)
+                    ready.insert(a, (key[m], m))
+        return out
+
+    best = None
+    for slow in SLOWS:
+        now = play([None] * n_ops, None, slow)
+        for k in range(TUNE["passes"] + 1):
+            _, seq, eng, at, tail = now
+            queues = {e: [n for n in seq if eng[n] == e] for e in "vatgsx"}
+            score = play(eng, queues, 1.0)[0] + TUNE["mix"] * play(eng, queues, TUNE["slow"])[0]
+            if best is None or score < best[0]:
+                best = (score, seq, eng)
+            pos = {n: x for x, n in enumerate(seq)}
+            at, eng = pack(ordered([-at[n] for n in range(n_ops)], True), tail, True)
+            at, eng = pack(ordered([-at[n] - ops[n]["cost"][eng[n]] for n in range(n_ops)], False), tail, False)
+            seq = sorted(seq, key=lambda n: (at[n], pos[n]))
+            now = play(eng, {e: [n for n in seq if eng[n] == e] for e in "vatgsx"}, slow)
     seq = best[1]
     for n, o in enumerate(ops):
         o["e"] = best[2][n]
@@ -787,7 +863,7 @@ def rank_program(g, core, T, topo):
         need = {}
         for m in o["pre"]:
             pm = ops[m]
-            if pm["e"] == "t" and o["e"] == "t":
+            if pm["e"] == o["e"] and (o["e"] == "t" or m in o["turn"]):
                 continue
             key = pm["sem"] or pm["e"]
             if key not in need or pos[m] > pos[need[key]]:

from concourse.bass import DstId, RemoteDMATransfer
from concourse.mybir import AluOpType as ALU, ActivationFunctionType as ACT

F, CAP, RO, N = 1024, 272, 3, 4
HELD = (2, 4, 4)
NS = 2
SEG = 6176
POS = {3: 0, 1: 1, 2: 2, 0: 3}
ORG = {j: SEG * k + 2080 for j, k in POS.items()}
ORA = ORG[0]
TW = 4 * SEG
BIG = 32768.0
HB = 1280.0
i32, u16, f32, f16, b16 = "int32", "uint16", "float32", "float16", "bfloat16"


def _s(d, *shape):
    return ("sbuf", [128] + list(shape), d)


SCRATCH = {
    "rx": _s(i32, 128), "RX": _s(f16, 128), "XT": _s(f16, 128), "SR": _s(f16, 4, 288), "LR": _s(f16, 4, 288),
    "SI": _s(i32, 4096), "SH": _s(f16, 3072), "LH": _s(f16, 4096), "SB": _s(b16, 3, 1024), "PK": _s(u16, 3, 512),
    "LP": _s(u16, 4, 512),
    "IT": _s(f32, 6144), "RT": _s(f32, 3, 1024), "IC": _s(f32, 512), "GOT": _s(f16, 2, 1024), "APP": _s(f16, 2, 1024),
    "AL": _s(f16, 4, 128), "F8": _s(f16, 64), "LE": _s(f16, 1024), "YI": _s(f32, 1024),
    "TAB": _s(b16, TW + 6144), "OLD": _s(b16, 1024), "IS": _s(f16, 4, 128), "PW": _s(f16, 256), "PS": _s(f16, 4, 128),
    "G4": _s(f16, 4096), "Y": _s(b16, 1024), "NEW": _s(b16, 1024), "PY": _s(u16, 512), "LY": _s(u16, 512),
    "HY": _s(f16, 512), "XY": _s(f32, 512), "NH": _s(b16, 1024),
    "CUR": _s(u16, 64), "IL": _s(u16, 64), "OL": _s(u16, 64), "FL": _s(u16, 256),
    "YNS": _s(f32, 64), "WI2": _s(i32, 3, 64), "DF2": _s(f32, 3, 64), "FL2": _s(f32, 2, 64),
    "WI": _s(i32, 128), "W3": _s(i32, 2, 128), "DM": _s(f16, 3, 128), "FD": _s(f32, 128), "D": _s(i32, 2, 128), "FT": _s(f16, 2, 128),
    "HI": _s(i32, 64), "RR": _s(f32, 5, 64), "SC": _s(b16, 272), "VI": _s(i32, 128), "VF": _s(b16, 128),
    "C12": _s(b16, 128), "GD": _s(f16, 264),
    "PI": _s(i32, 16), "PF": _s(f32, 16), "DF": _s(f32, 64), "J": _s(b16, 160), "J8": _s(b16, 144), "J15": _s(b16, 128),
    "JG": _s(b16, 128), "JU": _s(b16, 128), "CF": _s(f16, 1024), "ONH": _s(f16, 512),
    "ONB": _s(b16, 512), "FCI": _s(i32, 264), "FC16": _s(f16, 64),
    "WB": _s(b16, 144), "WD": _s(b16, 4, 144), "K256": _s(b16, 128), "GB": _s(f16, 2, 144), "XP": _s(f16, 2, 144), "UU": _s(f16, 128),
    "QT": _s(f16, 2, 128), "QB": _s(f16, 128), "QA": _s(f16, 8, 128), "SQ": _s(f32, 2, 128),
    "KZ": _s(f16, 3, 128), "KA": _s(f16, 4, 128), "OG": _s(f16, 128), "T2": _s(f16, 5, 128),
    "IB": _s(b16, 2, 128), "IH": _s(f16, 3, 128),
    "KS": _s(b16, 3, 128), "DI": _s(f16, 4, 128), "LO": _s(b16, 5, 144), "WL": _s(b16, 2, 36),
    "WF": _s(f32, 36), "KX": _s(b16, 128), "KY": _s(b16, 32),
}
for _k in "XYZW":
    for _h in "01":
        SCRATCH["p" + _k + _h] = ("psum", [128, 512], f32)
SHAPES = {k: v[1] for k, v in SCRATCH.items()}
SHAPES.update({"rtab": [128, 1024], "itab": [128, 3072], "btab": [128, 4096], "rn0": [128, 64], "x0": [8, 1024],
               "yb": [128, 1024], "yi": [128, 1024], "yn": [8, 1024]})
SIZE = {k: (4 if v[2] in (i32, f32) else 2) for k, v in SCRATCH.items()}
SIZE.update({"rtab": 4, "itab": 4, "btab": 2, "rn0": 4, "x0": 4, "yb": 2, "yi": 4, "yn": 4})
PSUM = [k for k, v in SCRATCH.items() if v[0] == "psum"]
SEMAPHORES = (["ev", "ea", "et", "eg", "sent", "out", "lrx", "tr", "ta", "tb1", "tb2", "tb3", "rn0", "rn1"]
              + [x + "%d" % q for x in ("lb", "li", "lr", "le", "ap", "ah", "ar", "ae", "ay") for q in range(N)])
CYC, GAT, PEC, HOP, FIX, BW, ROW, RIS, RLAT = 0.83e-3, 1.56, 0.42e-3, 0.19, 0.005, 400e3, 0.02, 0.4, 1.4
LOADS, ARRIVE, SET, BANKS = "i0 i1 b0 b1 b2i1 i2b0 i3b1 b3i2", "i0 i1 i3 i2", "i3", "X0 X1 W0 W1 W0 W1 Y0 Y1 Z0 Z1 X0 X1"
STRIDE = (0.5, 1.0, 2.0, 4.0)
SLOWS = (0.9, 1.0, 1.15, 1.3)
TUNE = {"pen": 0.3, "win": 0.06, "ext": 0.0, "cut": 16, "dec": 0, "soon": 4.0, "mix": 0.4, "slow": 1.8, "joint": 1, "rc": 1, "sig": 0, "shake": 0.0, "twice": 1, "ai": 1, "wy": 1, "rs": 0.8, "first": 1.8,
        "yi": 1.0, "pen2": 0.6, "passes": 2, "own": 1, "bias0": 0.0, "bias1": 0.0, "bias2": 0.0, "pe": 0.0, "nat": 1}


def rank_program(g, core, T, topo):
    me = T.rank_of(core)
    if me is None:
        return
    Q = {"v": g.vector, "a": g.scalar, "t": g.tensor, "g": g, "s": g.sync}
    ops = []
    stream = [None, 0]
    ALL = slice(None)

    def A(name, *idx):
        shp = SHAPES[name]
        idx = list(idx) + [ALL] * (len(shp) - len(idx))
        p = range(shp[0])[idx[0]]
        lo = hi = 0
        st = n = 1
        for d in range(len(shp) - 1, 0, -1):
            r = range(shp[d])[idx[d]]
            a, b = (r, r) if isinstance(r, int) else (r[0], r[-1])
            n *= 1 if isinstance(r, int) else len(r)
            lo += a * st
            hi += b * st
            st *= shp[d]
        reg = (name, 0, 128, 0, 512) if name in PSUM else (name, p[0], p[-1] + 1, lo, hi + 1)
        return (T[name][tuple(idx)], [reg], n, SIZE[name], len(p))

    def C(name, a, b, step=None):
        return A(name, ALL, slice(a, b, step))

    def R(name, k, a=None, b=None, step=None):
        return A(name, ALL, k, slice(a, b, step))

    def col(name, k):
        return C(name, k, k + 1)

    def rows(name, a, b, *idx):
        return A(name, slice(a, b), *idx)

    def ind(win, off):
        return (win[0].indirect(off[0]), win[1] + off[1], -16 * off[2], 4)

    def regs(*xs):
        out = []
        for x in xs:
            if isinstance(x, tuple):
                out += x[1]
        return out

    def val(x):
        return x[0] if isinstance(x, tuple) else x

    def add(e, fn, rd, wr, cost, sem=None, n=0, after=None, lat=0.0, hold=()):
        ops.append({"e": e, "fn": fn, "rd": rd, "wr": wr, "sem": sem, "n": n, "cost": cost, "after": after, "lat": lat, "hold": list(hold),
                    "lead": TUNE["bias%d" % stream[1]] * (stream[0] == 0)})
        return len(ops) - 1

    def tv(i, o, f=None):
        if i[2] < 0:
            return 0.05 - i[2] * GAT * CYC
        return max(64, i[2] * (f or (0.5 if i[3] == 2 and o[3] == 2 else 1.0))) * CYC + FIX

    def ta(i):
        return (0.065 - i[2] * GAT * CYC) if i[2] < 0 else max(64, i[2]) * CYC + 2 * FIX

    def lin(o, i, scale=None, bias=None, e="*"):
        def fn(q):
            if q == "a":
                if bias is None:
                    return g.scalar.activation(o[0], i[0], ACT.Copy, scale=1.0 if scale is None else val(scale))
                return g.scalar.activation(o[0], i[0], ACT.Identity, bias=val(bias), scale=1.0 if scale is None else val(scale))
            if scale is None and bias is None:
                return g.vector.tensor_copy(o[0], i[0])
            if bias is None:
                return g.vector.tensor_scalar(o[0], i[0], val(scale), None, ALU.mult)
            if scale is None:
                return g.vector.tensor_scalar(o[0], i[0], val(bias), None, ALU.add)
            return g.vector.tensor_scalar(o[0], i[0], val(scale), val(bias), ALU.mult, ALU.add)
        return add(e, fn, regs(i, scale, bias), o[1], {"v": tv(i, o), "a": ta(i)})

    def cp(o, i):
        return lin(o, i, e="v")

    def whole(o, i, scale=None, bias=None):
        return lin(o, i, scale, bias, "*" if TUNE["ai"] else "v")

    def act(o, i, func, scale, bias):
        return add("a", lambda q: g.scalar.activation(o[0], i[0], func, bias=val(bias), scale=val(scale)), regs(i, scale, bias), o[1],
                   {"a": ta(i)})

    def relu(o, i, x):
        def fn(q):
            if q == "a":
                return g.scalar.activation(o[0], i[0], ACT.Relu, bias=-x, scale=1.0)
            return g.vector.tensor_scalar(o[0], i[0], x, 0.0, ALU.subtract, ALU.max)
        return add("*", fn, i[1], o[1], {"v": tv(i, o), "a": ta(i)})

    def is_zero(o, i):
        def fn(q):
            if q == "a":
                return g.scalar.activation(o[0], i[0], ACT.Relu, bias=1.0, scale=-1.0)
            return g.vector.tensor_scalar(o[0], i[0], 0.0, None, ALU.is_equal)
        return add("*", fn, i[1], o[1], {"v": tv(i, o), "a": ta(i)})

    def edge(o, i, x, up):
        def fn(q):
            if q == "a":
                k = 64.0 if up else -64.0
                return g.scalar.activation(o[0], i[0], ACT.Sigmoid, bias=-k * (x - 0.5), scale=k)
            return g.vector.tensor_scalar(o[0], i[0], x, None, ALU.is_ge if up else ALU.is_lt)
        return add("*" if TUNE["sig"] else "v", fn, i[1], o[1], {"v": tv(i, o), "a": ta(i)})

    def ts(o, i, s1, op0, s2=None, op1=None):
        if op1 is None:
            add("v", lambda q: g.vector.tensor_scalar(o[0], i[0], val(s1), None, op0), regs(i, s1), o[1], {"v": tv(i, o)})
        else:
            add("v", lambda q: g.vector.tensor_scalar(o[0], i[0], val(s1), val(s2), op0, op1), regs(i, s1, s2), o[1], {"v": tv(i, o)})

    def tt(o, a, b, op):
        f = 1.0 if a[1][0][0] in PSUM or b[1][0][0] in PSUM else 2.0
        add("v", lambda q: g.vector.tensor_tensor(o[0], a[0], b[0], op), a[1] + b[1], o[1], {"v": tv(a, o, f)})

    def ms(o, c):
        add("v", lambda q: g.vector.memset(o[0], c), [], o[1], {"v": tv(o, o)})

    def mm(o, l, r, start, stop):
        add("t", lambda q: g.tensor.matmul(o[0], l[0], r[0], start, stop), l[1] + r[1], o[1],
            {"t": max(min(64, l[2]), r[2]) * PEC * (4 if l[3] == 4 else 1)})

    def iota(o, pat, base, cm, fl=False):
        c = {"g": 0.13 + 2 * o[2] * CYC}
        if fl:
            add("g", lambda q: g.iota(o[0], pat, base, cm, allow_small_or_imprecise_dtypes=True), [], o[1], c)
        else:
            add("g", lambda q: g.iota(o[0], pat, base, cm), [], o[1], c)

    chain = [None]

    def dma(e, o, i, sem, first=False, hold=()):
        run = min(o[2] if o[1][0][0] in SCRATCH else 1 << 20, i[2] if i[1][0][0] in SCRATCH else 1 << 20)
        size = o[2] * o[3] * o[4]
        k = add(e, lambda q: Q[q].dma_start(o[0], i[0]), i[1], o[1], {e: 0.06}, sem, 16, chain[0] if first else None,
                size / BW + max(16, o[2] * o[4] / run) / 16 * ROW, hold)
        if first:
            chain[0] = k
        return k

    peers = [(me + k) % N for k in (1, 2, 3)]
    engs = [x for x in topo.engines(core, T.cores[peers[0]]) if all(x in topo.engines(core, T.cores[r]) for r in peers)]
    NE = len(engs)
    sent = [0]

    def send(j, src, land, sem):
        r, q = peers[j], peers[N - 2 - j]
        rid, pnc = topo.addr(T.cores[r])[:2]
        tr = RemoteDMATransfer(dst_ids=[DstId(rid=rid, pnc=pnc)], dma_engine_mask=sum(1 << x for x in engs),
                               remote_sem=T.sem[sem + str(me)], srcs=[src[0]], dsts=[land(me)[0]])
        sent[0] += NE
        k = add("g", lambda _: g.remote_dma_fused([tr], local_sem=T.sem.sent), src[1], [], {"g": RIS}, "remote",
                lat=src[2] * src[3] * 128 / BW + 128 * ROW / NE)
        add("x", None, [], land(q)[1], {"x": 0.0}, sem + str(q), NE, k)

    EQ, MUL, ADD, SUB, AND, SHR = ALU.is_equal, ALU.mult, ALU.add, ALU.subtract, ALU.bitwise_and, ALU.logical_shift_right

    dma("s", C("rx", 0, 64), A("rn0"), "lrx", True)
    dma("s", C("rx", 64, 128), A("x0"), "lrx", True)
    for o in peers + [me]:
        if not TUNE["rc"]:
            dma("s", C("SI", 256 * o, 256 * o + 256), rows("rtab", 32 * o, 32 * o + 32), "lr%d" % o, True)
        for c in range(4 * (TUNE["rc"] > 0)):
            dma("sa"[c % 2], rows("SI", 32 * c, 32 * c + 32, slice(256 * o, 256 * o + 256)),
                rows("rtab", 32 * o, 32 * o + 32, slice(256 * c, 256 * c + 256)), "lr%d" % o, True)

    iota(col("PI", 9), [[0, 1]], 0, 1)
    iota(A("J"), [[1, 160]], 0, 0, True)
    iota(A("J8"), [[16, 9], [0, 2], [1, 8]], 0, 0, True)
    iota(A("J15"), [[0, 8], [1, 16]], 0, 0, True)
    iota(A("JG"), [[16, 8], [0, 16]], 0, 0, True)
    iota(A("JU"), [[1, 4], [4, 32]], 0, -1, True)
    iota(C("FCI", 0, 64), [[16, 64]], 0, 0)
    iota(C("FCI", 64, 128), [[1, 64]], 0, 64)
    iota(C("FCI", 128, 256), [[8, 128]], 0, 0)
    ms(rows("ONH", 0, 32), 1.0)
    ms(rows("ONB", 0, 32), 1.0)
    START = [ORA - 32 if t == 0 and r == 1 else TW - SEG * r for t, r in enumerate(HELD)]
    for t in range(RO):
        if START[t] not in START[:t]:
            ms(C("TAB", START[t], START[t] + 32), 0.0)
        ms(rows("KZ", 0, 32, t), 2080.0 - START[t] - BIG)
    ms(A("SC"), 0.0)
    p = col("PI", 9)
    for k, (sh, m) in enumerate([(0, 15), (0, 0x70), (0, 31), (5, 3), (3, 1), (0, 7), (2, 15), (0, 3), (0, 64)]):
        ts(col("PI", k), p, sh, SHR, m, AND)
    ts(col("PI", 10), p, 16, AND)
    cp(C("PF", 0, 11), C("PI", 0, 11))
    pi, pg, pr, pa, pb, p8, pi4, pc4, pv64, pp, pv16 = [col("PF", k) for k in range(11)]
    dTW, dC10, dC5, dTC, dCC, dNB, dWT, dTD, dP0, dTL, dTWL, dW4, dCF0, dCF1, dTX, dTY = [col("DF", k) for k in range(16)]
    M8, AM, MF, KSC, CQ, KD = 20, 28, 32, 36, 40, 56

    def low(k):
        return rows("DF", 0, 32, slice(k, k + 1))

    IB, I256, IH, IM = R("IB", 0), R("IB", 1), C("PW", 0, 128), R("IH", 2)
    turn = lambda b: C("PW", -32 * b % 128, -32 * b % 128 + 128)
    ts(IB, C("J", 0, 128), pp, EQ)
    ts(I256, C("J", 0, 128), pp, EQ, 256.0, MUL)
    ts(IM, C("J", 0, 128), pp, EQ, -256.0, MUL)
    ts(C("DF", AM, AM + 4), C("J", 0, 4), pa, EQ)
    lin(dTL, pr, 4.0, 3.0)
    ts(R("LO", 4), C("J", 0, 144), dTL, EQ)
    for a in range(N):
        lin(R("LO", a), R("LO", 4), col("DF", AM + a))
    ts(A("UU"), A("JU"), 0.0, EQ)
    lin(IH, IB)
    lin(C("PW", 128, 256), IB)
    lin(dNB, pb, -1.0, 1.0)
    lin(R("IH", 0), IB, dNB)
    lin(R("IH", 1), IB, pb)
    lin(dTW, pg, None, 15.0)
    lin(dTD, pg, None, 7.0)
    lin(dC10, pb, 10.0, -5.0)
    lin(dC5, pb, 5.0, -5.0)
    ts(C("DF", M8, M8 + 8), C("J", 0, 8), p8, EQ)
    lin(R("QT", 0), A("J15"), dC10, dC5)
    ts(R("QT", 1), A("JG"), pg, EQ)
    lin(R("SQ", 0), A("J15"), None, 1.0)
    tt(R("SQ", 1), R("SQ", 0), A("J15"), MUL)
    tt(A("QB"), R("QT", 0), R("QT", 1), MUL)
    ts(R("GB", 0), C("J", 0, 144), dTW, EQ)
    ts(R("GB", 1), C("J", 0, 144), dTW, EQ, -1.0, MUL)
    for a8 in range(8):
        lin(R("QA", a8), A("QB"), col("DF", M8 + a8))
    lin(dWT, pi, 2.0, 1.0)
    ts(dP0, pp, 0.0, EQ)
    ts(col("PI", 12), pa, pp, SUB, 128.0, ADD)
    ts(col("PI", 13), col("PI", 12), 3, AND)
    cp(col("DF", 47), col("PI", 13))
    ts(C("DF", CQ, CQ + 5), C("J", 0, 5), col("DF", 47), ADD, 1.5, ADD)
    ts(A("WB"), C("J", 0, 144), dTW, EQ, dWT, MUL)
    ts(R("WD", 0), A("J8"), dTD, EQ, dWT, MUL)
    ms(rows("K256", 0, 32), 256.0)
    for b in range(1, N // min(HELD[:-1])):
        ts(col("PI", 11), pp, 128.0 - 32 * b, ADD)
        ts(col("PI", 14), col("PI", 11), 0x70, AND)
        lin(col("DF", 46), col("PI", 14), None, 7.0)
        ts(R("WD", b), A("J8"), col("DF", 46), EQ, dWT, MUL)
    ts(dTX, pg, p8, ADD)
    lin(dTY, pv16, 1.0 / 16)
    ts(C("DF", MF, MF + 2), C("J", 0, 2), pb, EQ, dTY, MUL)
    for h in range(2):
        ts(R("XP", h), A("J8"), dTX, EQ, col("DF", MF + h), MUL)
    ts(A("OG"), A("JG"), pg, EQ, 0.25, MUL)
    ts(R("T2", 2), A("J15"), pi, ALU.is_lt)
    lin(R("T2", 3), IB, 512.0)
    tt(R("T2", 4), R("T2", 2), A("OG"), MUL)
    tt(R("T2", 1), R("T2", 4), R("T2", 3), ADD)
    tt(R("T2", 0), A("OG"), R("T2", 1), SUB)
    ms(rows("CF", 0, 32), 1.0)
    lin(dTC, pp, 1.0 / 16)
    lin(A("F8"), C("J", 0, 64), 1.0 / 1024, dTC)
    dma("a", rows("CF", 0, 1), rows("F8", 0, 16), "tr")
    for t in range(RO):
        lin(col("DF", KSC + t), dP0, 49152.0 - t, float(t))
        lin(rows("KS", 0, 32, t), rows("ONB", 0, 32, slice(0, 128)), low(KSC + t))
    ts(col("DF", KD), pp, 1.0, EQ, -5.0, MUL)
    ts(col("DF", KD + 1), pp, 1.0, EQ, -10.0, MUL)
    for k, al in enumerate(STRIDE):
        lin(R("AL", k), IB, al / 1024)
        ts(col("DF", KD + 2 + k), pp, 1.0, ALU.not_equal, al, MUL)
        lin(rows("KA", 0, 32, k), rows("SQ", 0, 32, 1), low(KD + k // 3), low(KD + 2 + k))
    lin(A("FC16"), C("FCI", 0, 64), None, pi)
    lin(A("FD"), C("FCI", 128, 256), None, p8)
    ts(C("FCI", 64, 128), C("FCI", 64, 128), 1023, AND)
    lin(R("FL2", 0), C("FCI", 64, 128))
    lin(R("FL2", 1), C("FCI", 64, 128), None, 3072.0)
    ts(col("DF", 48), pv64, 1.0 / 16, MUL, pc4, ADD)
    lin(dW4, pi4, 2.0, 1.0)
    lin(dTWL, col("DF", 48), 4.0, 3.0)
    ts(R("WL", 0), C("J", 0, 36), dTWL, EQ, dW4, MUL)
    lin(R("WL", 1), R("WL", 0), -256.0)
    lin(A("WF"), R("WL", 0))
    ms(rows("KX", 0, 32), 256.0 * HB)
    ms(rows("KY", 0, 32), 65536.0 * HB)
    for q in (2, 3):
        ms(rows("KY", 0, 32, slice(q, 32, 4)), -256.0 * HB)
    OWN = {1: 0, 2: 2, 4: 3}
    unit = lambda j: BIG + SEG * POS[j]
    lin(R("PS", 2), IB, -6144.0)
    lin(R("PS", 3), IB, 1024.0)
    for j in range(N):
        if any(r > 1 and j & OWN[r] == j for r in HELD):
            lin(R("IS", j), IB, unit(j))
        if 2 in HELD and j & 1:
            lin(R("PS", j // 2), turn(1), unit(j & 2))
    for k, s in enumerate([2048.0, -1024.0, -512.0, -256.0]):
        lin(R("DI", k), IB, s)

    lin(A("RX"), A("rx"))
    for o in range(N):
        for w in range(2):
            for c in range(4):
                mm(C("pW0", 32 * o + 16 * w, 32 * o + 16 * w + 16), R("LO", o, 3 - c, 131 - c),
                   C("RX", 64 * w + 16 * c, 64 * w + 16 * c + 16), c == 0, c == 3)
    for j, o in enumerate(peers + [me]):
        lin(R("SR", o, 0, 256), C("SI", 256 * o, 256 * o + 256), 1.0 / 2048, -1.0)
        lin(R("SR", o, 256, 288), C("pW0", 32 * o, 32 * o + 32))
        if o != me:
            send(j, R("SR", o), lambda r: R("LR", r), "ar")
    lx = lambda a, x, y: R("SR" if a == me else "LR", a, x, y)
    uu = lambda c: C("UU", 32 * c, 32 * c + 32)
    for a in [me] + peers[::-1]:
        for c in range(4):
            mm(rows("pW1", 32 * a, 32 * a + 32, slice(16 * c, 16 * c + 16)), uu(c), lx(a, 256, 272), True, True)
            if TUNE["rc"]:
                lin(rows("RT", 32 * a, 32 * a + 32, 2, slice(256 * c, 256 * c + 256)),
                    rows("SR" if a == me else "LR", 32 * c, 32 * c + 32, a, slice(0, 256)))
            else:
                mm(rows("pZ%d" % (c // 2), 32 * a, 32 * a + 32, slice(256 * (c % 2), 256 * (c % 2) + 256)), uu(c), lx(a, 0, 256), True, True)
        mm(rows("pW1", 32 * a, 32 * a + 32, slice(128, 256)), lx(a, 256, 288), IH, True, True)
    for k in range(2 * (not TUNE["rc"])):
        lin(R("RT", 2, 512 * k, 512 * k + 512), A("pZ%d" % k))
    cp(A("CUR"), C("pW1", 0, 64))
    lin(A("XT"), C("pW1", 128, 256))
    for h in range(2):
        for v in range(2):
            mm(C("pW1", 256 + h, 384, 2), R("XP", h, 16 - 16 * v, 144 - 16 * v), C("XT", 64 * v, 64 * v + 64), v == 0, v == 1)
    cp(A("WI"), C("pW1", 256, 384))
    done = {}
    for step in LOADS.split():
        j, hold = int(step[1]), [done[step[2:]]] if step[2:] else []
        o = (peers + [me])[j]
        if step[0] == "i":
            dma("s", C("SI", 1024 + 768 * o, 1792 + 768 * o), rows("itab", 32 * o, 32 * o + 32), "li%d" % o, True, hold)
            for x in range(768 * o, 768 * o + 768, 384):
                done[step[:2]] = lin(C("SH", x, x + 384), C("SI", 1024 + x, 1408 + x), 1.0 / 2048, -1.0)
            if o != me:
                send(j, C("SH", 768 * o, 768 * o + 768), lambda r: C("LH", 768 * r, 768 * r + 768), "ah")
        elif o == me:
            dma("s", rows("TAB", 32 * me, 32 * me + 32, slice(ORA, ORA + 4096)), rows("btab", 32 * me, 32 * me + 32), "ta", True, hold)
        else:
            bank = "p" + BANKS.split()[j]
            dma("s", R("SB", j), rows("btab", 32 * o, 32 * o + 32), "lb%d" % j, True, hold)
            mm(A(bank), IB, R("SB", j, 0, 512), True, False)
            mm(A(bank), I256, R("SB", j, 512, 1024), False, True)
            done[step[:2]] = whole(R("PK", j), A(bank))
            send(j, R("PK", j), lambda r: R("LP", r), "ap")

    def split(lo, hi, x, hx, xx, ps, plain=False):
        lin(hx, x, 1.0 / 256, HB - 0.498)
        lin(xx, x, None, None if plain else 256.0 * HB)
        if plain:
            mm(ps, rows("KX", 0, 1), rows("ONB", 0, 1, slice(0, ps[2])), True, False)
        mm(ps, IM, hx, not plain, True)
        tt(lo, xx, ps, ADD)
        lin(hi, hx, None, -HB)

    def unstack():
        for j, q in enumerate(peers[::-1]):
            split(R("SB", j, 0, 512), R("SB", j, 512, 1024), R("LP", q), C("G4", 512 * j, 512 * j + 512),
                  R("RT", 1, 512 * j, 512 * j + 512) if j < 2 else C("IC", 0, 512), A("p" + BANKS.split()[3 + j]))
        inner, last = ["p" + x for x in BANKS.split()[6:]], [None, None]
        for a in [me if x[1] == "3" else peers[2 - int(x[1])] for x in ARRIVE.split()]:
            for c in range(4):
                x = 768 * c
                while x < 768 * c + 768:
                    y = min(768 * c + 768, x // 512 * 512 + 512)
                    o = 768 * (a - c)
                    mm(rows(inner[x // 512], 32 * a, 32 * a + 32, slice(x % 512, (y - 1) % 512 + 1)), uu(c),
                       C("SH" if a == me else "LH", x + o, y + o), True, True)
                    k = inner[x // 512][1] == "X"
                    ops[-1]["after"], last[k] = last[k], len(ops) - 1
                    x = y
        for k in range(6):
            lin(C("IT", 512 * k, 512 * k + 512), A(inner[k]))
        for j, q in enumerate(peers[::-1]):
            dma("s", rows("TAB", 32 * q, 32 * q + 32, slice(ORA, ORA + 4096)), R("SB", j), "ta", True, [done[SET]])
        if HELD[0] == 2 and TUNE["twice"]:
            second = lambda q: rows("TAB", 32 * (q ^ 2), 32 * (q ^ 2) + 32, slice(ORG[2], ORG[2] + 4096))
            if TUNE["twice"] > 1:
                for x in range(0, 4096, 1024):
                    for y in (0, 64):
                        lin(rows("TAB", y, y + 64, slice(ORG[2] + x, ORG[2] + x + 1024)),
                            rows("TAB", 64 - y, 128 - y, slice(ORA + x, ORA + x + 1024)))
                return
            for j, q in enumerate(peers[::-1]):
                dma("s", second(q), R("SB", j), "tb2", True)
            dma("s", second(me), rows("btab", 32 * me, 32 * me + 32), "tb2", True)

    def widen(src, j, a, b, sem):
        k = 32 * j
        dma("s", rows("TAB", 0, 128 - k, slice(a, b)), src(k, 128), sem)
        if j:
            dma("s", rows("TAB", 128 - k, 128, slice(a, b)), src(0, k), sem)

    def held(t):
        return {1: (0,), 2: (0, 2), 4: (0, 2, 1, 3)}[HELD[t]]

    KW = 64 // NS
    CW = KW + 1

    def plane(ps, s, lvl, k):
        mm(A(ps), rows("KA", 0, 3, k), rows("CF", 0, 3, slice(512 * s, 512 * s + 512)), True, False)
        for rep in range(1 + k // 3):
            for i in range(8):
                mm(C(ps, i, 512, 8), R("QA", i), R("FT", lvl, 64 * s, 64 * s + 64), False, i == 7 and rep == k // 3)

    def to_list(o, big, data, start=True, stop=True):
        for i in range(16):
            mm(o, big(15 - i, 143 - i), data(i), start and i == 0, stop and i == 15)

    def gather(dst, win, lst, z):
        k = KW * z
        for a, b in ((k, k + TUNE["cut"]), (k + TUNE["cut"], k + KW)):
            lin(dst(16 * a, 16 * b), ind(win, C(lst, a, b)))

    def level(t, lvl, z):
        k, c0, c1 = t + lvl, 512 * z, 512 * z + 512
        stream[0] = z
        bank = "p%s%d" % ("XY"[lvl], z)
        gather(lambda a, b: R("GOT", lvl, a, b), C("IT", 0, (3072, 4096, 6144)[t]) if lvl else R("RT", (t - 1) % RO), ("CUR", "IL")[lvl], z)
        plane(bank, z, lvl, k)
        tt(R("APP", lvl, c0, c1), R("GOT", lvl, c0, c1), A(bank), ALU.max)
        joint = TUNE["joint"] >> (2 * t + lvl) & 1
        if z or not joint:
            k0, k1 = KW * z * (not joint), KW * z + KW
            o = C("pW%d" % z, 64 + 64 * lvl, 64 + 64 * lvl + k1 - k0)
            mm(o, R("AL", k), C("FC16", k0, k1), True, False)
            to_list(o, lambda a, b: R("GB", 0, a, b), lambda i: R("GOT", lvl, 16 * k0 + i, c1, 16), False, False)
            to_list(o, lambda a, b: R("GB", 1, a, b), lambda i: R("APP", lvl, 16 * k0 + i, c1, 16), False)
            whole(C(("IL", "OL")[lvl], k0, k1), o, 2048.0, 2048.0 * (1 + STRIDE[k]))
        if t < RO - 1:
            lin(R("RT", t, c0, c1) if lvl == 0 else C("IT", 3072 + c0, 3072 + c1) if t == 0 else C("IT", 4096 + 2 * c0, 4096 + 2 * c1, 2),
                R("APP", lvl, c0, c1))

    def root_number(z, num, m, d, prod, w, f):
        ts(z, w, 7, AND)
        ts(num, w, 3, SHR, 1023, AND)
        is_zero(m, z)
        tt(d, num, f, SUB)
        tt(prod, d, m, MUL)

    def keys(t, z):
        W, k0, k1 = "pW%d" % z, KW * z, KW * z + KW
        stream[0] = z
        d = lambda name, j: R(name, j, 2 * k0, 2 * k1)
        wi = C("WI", 2 * k0, 2 * k1)
        if t:
            whole(wi, C(W, 256, 256 + 2 * KW))
            root_number(d("W3", 0), d("W3", 1), d("DM", 0), d("DM", 1), d("DM", 2), wi, C("FD", 2 * k0, 2 * k1))
            mm(C(W, 0, KW), IH, C("FC16", k0, k1), True, False)
            for h in range(2):
                mm(C(W, 0, KW), R("IH", h), R("DM", 2, 2 * k0 + h, 2 * k1, 2), False, h == 1)
            whole(C("CUR", k0, k1), C(W, 0, KW))
        for lvl in range(2):
            ts(d("D", lvl), wi, 4 * lvl, SHR, 15, AND)
            act(d("FT", lvl), d("D", lvl), ACT.Square, 1.0, pb)

    def send_inner():
        le = lambda r: C("LE", 256 * r, 256 * r + 256)
        for j, r in enumerate(peers + [me]):
            dma("s", le(me) if r == me else C("LH", 256 * r, 256 * r + 256), rows("APP", 32 * r, 32 * r + 32, 1), "le%d" % r)
            if r != me:
                send(j, C("LH", 256 * r, 256 * r + 256), le, "ae")

    def decode_inner(hold):
        for s in range(2):
            e = lambda k: C("LH" if k else "LE", 1024 * k + 512 * s, 1024 * k + 512 * s + 512)
            for k, x in ((1, 1.0), (2, 2.0), (3, 4.0)):
                ops[relu(e(k), e(0), x)]["hold"] = hold
            for k in range(4):
                mm(A("pZ%d" % s), R("DI", k), e(k), k == 0, k == 3)
                ops[-1]["hold"] = hold
            lin(C("YI", 512 * s, 512 * s + 512), A("pZ%d" % s), None, 2048.0)
        for r in range(N):
            dma("s", rows("yi", 32 * r, 32 * r + 32), C("YI", 256 * r, 256 * r + 256), "out")

    def blocks(t, z):
        own = OWN[HELD[t]]
        nb = N // HELD[t]
        W, FAR = "pW%d" % z, "pW1" if NS == 1 else "pX%d" % z
        k0, k1, c0, c1 = KW * z, KW * z + KW, 16 * KW * z, 16 * KW * (z + 1)
        stream[0] = z
        sm = lambda name, j=0: C(name, 64 * j + k0, 64 * j + k1)
        cl = lambda name, j: C(name, 4 * CW * z + CW * j + 1, 4 * CW * z + CW * j + CW)
        cz = lambda name: C(name, 4 * CW * z, 4 * CW * z + 4 * CW)
        gather(lambda a, b: C("OLD", a, b), C("TAB", ORA, ORA + (4096, 6144, 10240)[t]), "OL", z)
        to_list(C(W, 192, 192 + KW), lambda a, b: C("WB", a, b), lambda i: C("OLD", c0 + i, c1, 16))
        rr = lambda j: R("RR", j, k0, k1)
        for j in range(N + 1):
            ts(rr(j), C(W, 192, 192 + KW), col("DF", CQ + j), SUB, 1.5 * 2 ** 25, ADD)
        whole(sm("HI"), C(W, 192, 192 + KW))
        sc = lambda a, b, st=None: C("SC", 1 + 4 * CW * z + a, 1 + 4 * CW * z + b, st)
        if z:
            lin(sc(0, 4 * CW, CW), C("SC", 1 + KW, 1 + 4 * CW, CW))
        for j in range(N):
            o, first = sc(CW * j + 1, CW * j + CW), sc(CW * j, CW * j + 1)
            add("v", lambda q, o=o, j=j, first=first: g.vector.tensor_tensor_scan(o[0], rr(j)[0], rr(j + 1)[0], first[0], ADD, SUB),
                regs(rr(j), rr(j + 1), first), o[1], {"v": tv(rr(j), o)})
        cnt = C("pZ%d" % z, 256, 256 + 4 * CW)
        mm(cnt, R("T2", 0), sc(0, 4 * CW), True, False)
        mm(cnt, R("T2", 1), sc(-1, 4 * CW - 1), False, True)
        hi = C("VI", 2 * k0 + KW, 2 * k1)
        ts(C("VI", 2 * k0, 2 * k0 + KW), sm("HI"), 255, AND)
        ts(hi, sm("HI"), (4096 if t == 0 else 8192) - 256, AND)
        lin(C("VF", 2 * k0, 2 * k1), C("VI", 2 * k0, 2 * k1))
        mm(C(FAR, 0, KW * nb), rows("KZ", 0, 1, t), rows("ONH", 0, 1, slice(0, KW * nb)), True, False)
        for x in (C("VF", 2 * k0, 2 * k0 + KW), C("VF", 2 * k0 + KW, 2 * k1)):
            for b in range(nb):
                mm(C(FAR, KW * b, KW * b + KW), turn(b), x, False, False)
        for k, x in enumerate((4096.0, 5120.0)[:(0, 2, 1)[t]]):
            edge(sm("C12", k), hi, x, True)
            mm(C(FAR, 0, KW), R("PS", 2 + k), sm("C12", k), False, False)
        edge(cz("GD"), cnt, CAP + 1 - 2048.0, False)
        for j in range(N):
            b = j & ~own
            mm(C(FAR, KW * b, KW * b + KW), R("PS", j // 2) if b else R("IS", j), cl("GD", j), False, j == N - 1)
        f0 = 4 * k0
        for x in range(0, KW * nb, 128):
            relu(C("FL", f0 + x, f0 + min(x + 128, KW * nb)), C(FAR, x, min(x + 128, KW * nb)), 0.0)

        def far(b, c):
            k = f0 + KW * b + 16 * c - k0
            lin(C("G4", 1024 * b + 256 * c, 1024 * b + 256 * c + 256), ind(C("TAB", START[t], TW), C("FL", k, k + 16)), 3.0)

        for c in range(c0 // 256, c1 // 256):
            if t == RO - 1:
                for b in range(nb):
                    far(b, c)
                continue
            bank = ("pZ0", "pZ1", "pX0", "pX1")[c] if NS == 1 else "p%s%d" % ("ZY"[c % 2], z)
            o, x = C(bank, 0, 256), 256 * c
            mm(o, rows("KS", 0, 2, t), rows("ONB", 0, 2, slice(0, 256)), True, False)
            mm(o, IB, C("OLD", x, x + 256), False, False)
            for b in range(nb):
                far(b, c)
                mm(o, turn(-b), C("G4", 1024 * b + x, 1024 * b + x + 256), False, b == nb - 1)
            lin(C("Y", x, x + 256), o, -1.0, 127.5)
            tt(C("NEW", x, x + 256), o, C("Y", x, x + 256), ADD)
        if t == RO - 1:
            return
        o = C(W, 256, 256 + 2 * KW)
        terms = [(0, "OLD", 0)] + [(b, "G4", 1024 * b) for b in range(nb)] + [(0, "Y", 0)] if TUNE["wy"] else [(0, "NEW", 0)]
        if TUNE["wy"]:
            mm(o, rows("KS", 0, 2, t), rows("K256", 0, 2, slice(0, 2 * KW)), True, False)
        for b, name, x in terms:
            for i in range(8):
                mm(o, R("WD", b, 7 - i, 135 - i), C(name, x + c0 + i, x + c1, 8), i == 0 and name == "NEW", i == 7 and name in ("Y", "NEW"))
        st = (2, 4)[t]
        for x in range(c0, c1, 512):
            o = ORA + (4096, 6144)[t] + st * x
            lin(C("TAB", o, o + 512 * st, st), C("NEW", x, x + 512))

    def spread(t):
        stream[0] = None
        o = 1024 * t - 2048
        n = 1024 // TUNE["nat"]
        for x in range(0, 1024, n):
            for j in held(RO - 1):
                if j == 0 and TUNE["own"]:
                    for y in range(x, x + n, 512):
                        lin(C("TAB", ORA + o + y, ORA + o + y + 512), C("NEW", y, y + 512))
                else:
                    widen(lambda a, b: rows("NEW", a, b, slice(x, x + n)), j, ORG[j] + o + x, ORG[j] + o + x + n, "rn%d" % t)

    def finish(t):
        stream[0] = None
        W, nb, banks = "pX1", N // HELD[t], ("pY0", "pW0", "pY1", "pW1")
        homes, gone = peers + [me], []
        for a, bank in zip(homes, banks):
            mm(C(bank, 0, 256), rows("KS", 0, 2, t), rows("ONB", 0, 2, slice(0, 256)), True, False)
            for c in range(4):
                mm(C(bank, 0, 256), R("LO", a, 3 - c, 131 - c), C("OLD", 256 * c, 256 * c + 256), False, False)
        ly = lambda r: C("LY", 128 * r, 128 * r + 128)
        for j, (a, bank) in enumerate(zip(homes, banks)):
            o, x = C(bank, 0, 256), 256 * a
            for c in range(4):
                for b in range(nb):
                    mm(o, R("LO", (a + b) % N, 3 - c, 131 - c), C("G4", 1024 * b + 256 * c, 1024 * b + 256 * c + 256), False, c == 3 and b == nb - 1)
            lin(C("Y", x, x + 256), o, None, -127.5)
            if a == me:
                tt(C("NH", x, x + 256), o, C("Y", x, x + 256), SUB)
                continue
            tt(C("NEW", x, x + 256), o, C("Y", x, x + 256), SUB)
            mm(C(bank, 256, 384), IB, C("NEW", x, x + 128), True, False)
            mm(C(bank, 256, 384), I256, C("NEW", x + 128, x + 256), False, True)
            gone.append(whole(C("PY", 128 * a, 128 * a + 128), C(bank, 256, 384)))
            send(j, C("PY", 128 * a, 128 * a + 128), ly, "ay")
        decode_inner(gone[TUNE["dec"]:][:1])
        for r, bank in zip([me] + peers[::-1], (None,) + banks):
            x = 256 * r
            if r != me:
                split(C("NH", x, x + 128), C("NH", x + 128, x + 256), ly(r), C("HY", 128 * r, 128 * r + 128),
                      C("XY", 128 * r, 128 * r + 128), C(bank, 0, 128), True)
            dma("s", rows("yb", 32 * r, 32 * r + 32), C("NH", x, x + 256), "out")
            o = rows(W, 32 * r, 32 * r + 32, slice(0, 64))
            if r == me:
                for q in range(4):
                    mm(o, R("WL", 0, 3 - q, 35 - q), C("NH", x + 64 * q, x + 64 * q + 64), q == 0, q == 3)
                continue
            mm(o, rows("KY", 0, 1), rows("ONB", 0, 1, slice(0, 64)), True, False)
            for q in range(4):
                y = 128 * r + 64 * (q % 2)
                mm(o, R("WL", int(q < 2), 3 - q, 35 - q), C("HY", y, y + 64), False, False)
            for q in range(2):
                y = 128 * r + 64 * q
                mm(o, C("WF", 3 - q, 35 - q), C("XY", y, y + 64), False, q == 1)
        cp(R("WI2", 0), C(W, 0, 64))
        root_number(R("WI2", 1), R("WI2", 2), R("DF2", 0), R("DF2", 1), R("DF2", 2), R("WI2", 0), R("FL2", 0))
        tt(A("YNS"), R("DF2", 2), R("FL2", 1), ADD)
        dma("a", A("yn"), A("YNS"), "out")

    for t in range(RO):
        stream[1] = t
        for z in range(NS):
            keys(t, z)
            level(t, 0, z)
        stream[0] = None
        if t == 0:
            unstack()
        for j in held(t):
            if j and (t == 0 and not TUNE["twice"] or t and j not in held(t - 1)):
                widen(lambda x, y: rows("TAB", x, y, slice(ORA, ORA + 4096)), j, ORG[j], ORG[j] + 4096, "tb%d" % j)
        for z in range(NS):
            level(t, 1, z)
        stream[0] = None
        if t == RO - 1:
            send_inner()
        for z in range(NS):
            blocks(t, z)
        (spread if t < RO - 1 else finish)(t)

    def meet(x, y):
        return x[1] < y[2] and y[1] < x[2] and x[3] < y[4] and y[3] < x[4]

    n_ops = len(ops)
    hist = {}
    group = {}
    for n, o in enumerate(ops):
        if o["n"]:
            group.setdefault(o["sem"], []).append(n)
    for n, o in enumerate(ops):
        pre, turn = set(o["hold"]), set()
        for mine, w in [(r, False) for r in o["rd"]] + [(r, True) for r in o["wr"]]:
            ps = mine[0] in PSUM
            keep = []
            for item in hist.get(mine[0], []):
                m, reg, mw = item
                if (w or mw or ps) and m != n and meet(mine, reg) and ops[m]["sem"] != "remote":
                    (pre if w or mw else turn).update(group[ops[m]["sem"]] if ops[m]["n"] else [m])
                if not (w and mine[1] <= reg[1] and reg[2] <= mine[2] and mine[3] <= reg[3] and reg[4] <= mine[4]):
                    keep.append(item)
            keep.append((n, mine, w))
            hist[mine[0]] = keep
        o["turn"] = turn - pre
        o["pre"] = pre = pre | turn
        o["dep"] = pre | ({o["after"]} if o["after"] is not None else set())
        o["post"] = []
        o["due"] = TUNE["yi"] if o["wr"] and o["wr"][0][0] == "yi" else 0.0
        if o["sem"] in ("rn0", "rn1"):
            o["lat"] += 0.0
            o["soon"] = TUNE["soon"]
    for n, o in enumerate(ops):
        for m in o["dep"]:
            ops[m]["post"].append(n)
    for n in range(n_ops - 1, -1, -1):
        o = ops[n]
        own = min(o["cost"].values()) + (o["lat"] + RLAT if o["sem"] and o["e"] != "x" else 0.0) + o.get("soon", 0.0)
        o["rank"] = own + max([ops[m]["rank"] + HOP * ((o["e"] != "t" or ops[m]["e"] != "t") and n not in ops[m]["turn"])
                               - RLAT * (ops[m]["after"] == n and ops[m]["n"] == 16 != ops[m]["e"] != "x" and n not in ops[m]["pre"]) for m in o["post"]] + [o["due"]])
    can = [list(o["cost"]) if o["e"] == "*" else [o["e"]] for o in ops]
    tight = [{m: (ops[m]["after"] == n and ops[m]["e"] != "x" and n not in ops[m]["pre"]) or o["e"] == ops[m]["e"] == "t"
              or n in ops[m]["turn"] for m in o["post"]} for n, o in enumerate(ops)]
    hop = [0.0 if o["e"] == "x" else HOP for o in ops]

    def play(eng, queues, slow):
        eng = list(eng)
        free = {e: 0.0 for e in "vatgsx"}
        lanes = [0.0, TUNE["first"]]
        left = [len(o["dep"]) for o in ops]
        at, tail, seq = [0.0] * n_ops, [0.0] * n_ops, []
        ready = {n for n in range(n_ops) if not left[n]}
        head = {e: 0 for e in "vatgsx"}
        other = [{} for _ in ops]

        def start(n, e):
            return max([free[e], at[n]] + [t for x, t in other[n].items() if x != e])

        while ready:
            if queues:
                cand = [(start(q[head[e]], e), e, q[head[e]]) for e, q in queues.items() if head[e] < len(q) and q[head[e]] in ready]
                t1, e, n = min(cand)
                head[e] += 1
            else:
                cand = []
                for n in ready:
                    e = min(can[n], key=lambda x: start(n, x) + ops[n]["cost"][x] * (1.0 + TUNE["pen"] * (x == "v")))
                    cand.append((start(n, e), e, n))
                t0, e0, _ = min(cand)
                t1, e, n = max([c for c in cand if c[1] == e0 and c[0] <= t0 + TUNE["win"]], key=lambda c: (ops[c[2]]["rank"] + ops[c[2]]["lead"], -c[2]))
            o = ops[n]
            eng[n] = e
            at[n] = t1
            issue = end = t1 + o["cost"][e]
            free[e] = issue if e != "x" else 0.0
            if o["sem"] and e != "x":
                far = o["sem"] == "remote"
                lanes[0] = max(end + (TUNE["rs"] + lanes[1] if far else TUNE["rs"]), lanes[0]) + o["lat"] * slow
                lanes[1] *= not far
                end = lanes[0] + 0.5 + (TUNE["ext"] if far else 0.0)
            elif e == "t":
                end += TUNE["pe"]
            tail[n] = end - issue
            ready.remove(n)
            seq.append(n)
            for m in o["post"]:
                if n in ops[m]["turn"]:
                    other[m][e] = end + HOP
                at[m] = max(at[m], issue if tight[n][m] else end + hop[m])
                left[m] -= 1
                if not left[m]:
                    ready.add(m)
        return max(at[n] + ops[n]["cost"][eng[n]] + tail[n] for n in seq), seq, eng, at, tail

    def pack(order, tail, back):
        busy = {e: ([], []) for e in "vatgs"}
        at, eng = [0.0] * n_ops, [None] * n_ops
        for n in order:
            o = ops[n]
            if back:
                t = max([at[m] + ops[m]["cost"][eng[m]] + (0.0 if tight[n][m] else tail[n] + hop[m] + o.get("soon", 0.0)) for m in o["post"]]
                        + [tail[n] + o["due"]])
            else:
                t = max([at[m] + ops[m]["cost"][eng[m]] + (0.0 if tight[m][n] else tail[m] + hop[n]) for m in o["dep"]] + [0.0])
            best = None
            turns = [m for m in o["post"] if n in ops[m]["turn"]] if back else o["turn"]
            for e in can[n]:
                c, k = o["cost"][e], 0
                t1 = max([t] + [at[m] + ops[m]["cost"][eng[m]] + HOP for m in turns if eng[m] != e])
                if e != "x":
                    lo, hi = busy[e]
                    a, b = 0, len(hi)
                    while a < b:
                        mid = (a + b) // 2
                        a, b = (mid + 1, b) if hi[mid] <= t1 else (a, mid)
                    k = a
                    while k < len(lo) and lo[k] < t1 + c:
                        t1 = hi[k]
                        k += 1
                key = t1 + c * (1.0 + TUNE["pen2"] * (e == "v"))
                if best is None or key < best[0]:
                    best = (key, t1, e, k)
            _, at[n], eng[n], k = best
            if eng[n] != "x":
                busy[eng[n]][0].insert(k, at[n])
                busy[eng[n]][1].insert(k, at[n] + o["cost"][eng[n]])
        return at, eng

    def ordered(key, back):
        nxt, cnt = ("dep", "post") if back else ("post", "dep")
        left = [len(o[cnt]) for o in ops]
        ready = sorted((key[n], n) for n in range(n_ops) if not left[n])
        out = []
        while ready:
            n = ready.pop(0)[1]
            out.append(n)
            for m in ops[n][nxt]:
                left[m] -= 1
                if not left[m]:
                    a, b = 0, len(ready)
                    while a < b:
                        mid = (a + b) // 2
                        a, b = (mid + 1, b) if ready[mid] < (key[m], m) else (a, mid)
                    ready.insert(a, (key[m], m))
        return out

    best = None
    for slow in SLOWS:
        now = play([None] * n_ops, None, slow)
        for k in range(TUNE["passes"] + 1):
            _, seq, eng, at, tail = now
            queues = {e: [n for n in seq if eng[n] == e] for e in "vatgsx"}
            score = play(eng, queues, 1.0)[0] + TUNE["mix"] * play(eng, queues, TUNE["slow"])[0]
            if best is None or score < best[0]:
                best = (score, seq, eng)
            pos = {n: x for x, n in enumerate(seq)}
            at, eng = pack(ordered([-at[n] for n in range(n_ops)], True), tail, True)
            at, eng = pack(ordered([-at[n] - ops[n]["cost"][eng[n]] for n in range(n_ops)], False), tail, False)
            seq = sorted(seq, key=lambda n: (at[n], pos[n]))
            now = play(eng, {e: [n for n in seq if eng[n] == e] for e in "vatgsx"}, slow)
    seq = best[1]
    for n, o in enumerate(ops):
        o["e"] = best[2][n]
    esem = {"v": "ev", "a": "ea", "t": "et", "g": "eg"}
    total = {k: sum(ops[m]["n"] for m in v) for k, v in group.items()}
    pos = {n: k for k, n in enumerate(seq)}
    seen = {e: {} for e in Q}
    for n in seq:
        o = ops[n]
        o["wait"] = []
        if o["e"] == "x":
            continue
        need = {}
        for m in o["pre"]:
            pm = ops[m]
            if pm["e"] == o["e"] and (o["e"] == "t" or m in o["turn"]):
                continue
            key = pm["sem"] or pm["e"]
            if key not in need or pos[m] > pos[need[key]]:
                need[key] = m
        for key, m in need.items():
            if seen[o["e"]].get(key, -1) < pos[m]:
                seen[o["e"]][key] = n_ops if ops[m]["sem"] else pos[m]
                o["wait"].append(m)
                ops[m]["sig"] = True
    count = {e: 0 for e in esem}
    for n in seq:
        o = ops[n]
        e = o["e"]
        if e == "x":
            continue
        for m in o["wait"]:
            pm = ops[m]
            if pm["sem"]:
                Q[e].wait_ge(T.sem[pm["sem"]], total[pm["sem"]])
            else:
                Q[e].wait_ge(T.sem[esem[pm["e"]]], pm["cnt"])
        ins = o["fn"](e)
        if o["sem"] == "remote":
            continue
        if o["sem"]:
            ins.then_inc(T.sem[o["sem"]], 16)
        elif o.get("sig"):
            count[e] += 1
            o["cnt"] = count[e]
            ins.then_inc(T.sem[esem[e]], 1)
    for e in esem:
        if count[e]:
            g.wait_ge(T.sem[esem[e]], count[e])
    g.wait_ge(T.sem.sent, sent[0])
    g.wait_ge(T.sem.out, total["out"])
